import numpy as np, ml_dtypes
CORES = [1,5,17,21,33,37,49,53]
N = 8
BF = ml_dtypes.bfloat16
A, W, B, BL, RO = 768, 4096, 64, 3, 3
def parts(rng):
    share = rng.choice(np.array([0.5, 0.75, 0.95]), (N, 8, 1, 1)) * rng.random((N, 8, 1, A))
    s = np.where(rng.random((N, 8, 16, A)) < share, 4096, rng.integers(0, 4096, (N, 8, 16, A)))
    l = np.minimum(np.maximum(rng.integers(90, 201, (N, 8, 1, A)) + rng.integers(-60, 61, (N, 8, 16, A)), 0), 255)
    return s, l, rng.integers(0, 4096, (N, 8, A)), rng.integers(0, 256, (N, 8, 16, W))
def pack(s, l, k, f):
    return {"sr": np.ascontiguousarray(s.reshape(N, 128, A)).astype(np.int32), "lim": np.ascontiguousarray(l.reshape(N, 128, A)).astype(np.int32),
            "u": np.ascontiguousarray(k).astype(np.int32), "fit": np.ascontiguousarray(f.reshape(N, 128, W)).astype(np.float32).astype(BF)}
def setup_inputs(rng):
    return pack(*parts(rng))
def setup_inputs_ties(rng):
    s, l, k, f = parts(rng); g = rng.permutation(8); cnt = rng.integers(0, 17, (N, 8, A))
    cnt[:, g[0]] = rng.integers(15, 17, (N, A)); cnt[:, g[1]] = rng.choice(np.array([0, 15, 16]), (N, A)); cnt[:, g[2]] = 8
    cnt[:, g[3]] = 0; cnt[:, g[4]] = 16; cnt[:, g[4], 0] = 0; cnt[:, g[4], A - 1] = 0
    cnt[:, g[5]] = 0
    for q in rng.permutation(N)[1:]: cnt[q, g[5], rng.permutation(A // 2)[:A // 32]] = 1
    l[:, g[[0, 1, 2, 5]]] = 255
    whole = rng.integers(0, 4096, s.shape)
    s = np.where(np.argsort(rng.random(s.shape), axis=2) < cnt[:, :, None, :], 4096, whole)
    return pack(s, l, k, f)
def setup_inputs_level(rng):
    s, l, k, f = parts(rng); base = rng.integers(1, 255, (1, 8, 16, 1))
    n = rng.choice(np.array([0, 3, 5, 7, 7, 8, 8, 11, 11, 12]), (N, 8, 1, W))
    over = np.argsort(rng.random(f.shape, dtype=np.float32), axis=2) < n
    f = base + np.where(over, 1, -rng.integers(0, 2, f.shape))
    return pack(s, l * 0 + base, k, f)
def setup_inputs_ends(rng):
    s, l, k, f = parts(rng); g = rng.permutation(8)
    e = rng.choice(np.array([0, 1, 31, 32, 2048, 4094, 4095]), s.shape)
    s = np.where((s < 4096) & (rng.random((N, 8, 1, A)) < 0.7), e, s)
    k = np.where(rng.random(k.shape) < 0.7, rng.choice(np.array([0, 1, 31, 32, 2048, 4094, 4095, 3099, 2102, 1105]), k.shape), k)
    m = rng.integers(0, 6, (N, 8, 1, A))
    l = np.where(m == 0, 0, np.where(m == 1, 255, np.where(m == 2, 255 * rng.integers(0, 2, l.shape), l)))
    f[:, g[:4]] = 255 * rng.integers(0, 2, (N, 4, 16, W))
    f[:, :, :, 0] = 255 * rng.integers(0, 2, (N, 8, 16)); f[:, :, :, W - 1] = 255 * rng.integers(0, 2, (N, 8, 16))
    q = int(rng.integers(0, N)); hole = (np.argsort(rng.random((8, 16, 1)), axis=1) < 8) == (np.arange(A) < A // 2)
    s[q] = np.where(hole, 4096, np.where(rng.random(hole.shape) < 0.7, e[q], rng.integers(0, 4096, hole.shape))); l[q] = 255
    return pack(s, l, k, f)
def setup_inputs_alike(rng):
    s, l, k, f = parts(rng); o = rng.permutation(8); g = o[:4]; d = int(o[4]); q = rng.permutation(N)
    s[q[0]] = rng.integers(0, 4096, (8, 16, A)); s[q[1]] = np.where(rng.random((8, 16, A)) < 0.9, 4096, rng.integers(0, 4096, (8, 16, A)))
    for h in g:
        few = rng.integers(0, 4096, 5); s[:, h] = np.where(s[:, h] < 4096, few[rng.integers(0, 5, (N, 16, A))], 4096)
        k[:, h] = int(rng.integers(0, 4096))
    f[:, d] = f[:, d] % 101; f[q[0], d] = rng.integers(200, 256, (16, W)); l[q[0], d] = rng.integers(100, 200, (16, A))
    return pack(s, l, k, f)
def setup_inputs_spread(rng):
    s, l, k, f = parts(rng)
    s = np.where(s < 4096, np.minimum(np.exp2(12 * rng.random(s.shape)).astype(np.int64), 4095), 4096)
    k = np.minimum(np.exp2(12 * rng.random(k.shape)).astype(np.int64), 4095)
    l = np.minimum((np.exp2(4 + 4 * rng.random((N, 8, 1, A))) * (0.5 + 0.5 * rng.random(l.shape))).astype(np.int64), 255)
    f = np.minimum((np.exp2(8 * rng.random((N, 8, 1, W))) * rng.random(f.shape)).astype(np.int64), 255)
    return pack(s, l, k, f)
def check_inputs(d):
    bad = []
    for n, hi in (("sr", 4096), ("lim", 255), ("u", 4095), ("fit", 255)):
        a = np.asarray(d[n]).astype(np.float64)
        if not (np.min(a) >= 0 and np.max(a) <= hi): bad.append("range of " + n)
    a = np.asarray(d["fit"]).astype(np.float32)
    if not np.all(a == np.floor(a)): bad.append("whole numbers in fit")
    return bad
def records(f, s, v):
    c = ((s * v[:, :, None, :]) >> 5) & (W - 1)
    return np.take_along_axis(f, c.reshape(N, 8, 1, -1), 3).reshape(N, 8, 16, 16, -1)
def reference(sr, lim, u, fit):
    s = sr.astype(np.int64).reshape(N, 8, 16, A); l = lim.astype(np.int16).reshape(N, 8, 16, A); k = u.astype(np.int64)
    f = fit.astype(np.float32).astype(np.int16).reshape(N, 8, 16, W); h = A // 2
    for t in range(RO):
        over = np.sum(records(f, s, (k + 997 * t) & 4095) > l[:, :, :, None, :], axis=2)
        s = np.where(over >= 12, 4096, s)
        holes = np.minimum(np.sum(s == 4096, axis=2), 15)
        o = np.argsort(holes, axis=2, kind="stable")
        s = np.take_along_axis(s, o[:, :, None, :], 3); l = np.take_along_axis(l, o[:, :, None, :], 3); k = np.take_along_axis(k, o, 2)
        have = s[..., :h]; give = s[..., h:][..., ::-1]
        good = np.sum(records(f, give, (k[..., :h] + 997 * t) & 4095) <= l[:, :, :, None, :h], axis=2)
        move = (have == 4096) & (give < 4096) & (good >= 9)
        s = np.concatenate([np.where(move, give, have), np.where(move, 4096, give)[..., ::-1]], axis=3)
        for b in range(BL):
            c = slice(A - BL * B + b * B, A - BL * B + (b + 1) * B)
            s[..., c] = np.roll(s[..., c], b + 1, axis=0); l[..., c] = np.roll(l[..., c], b + 1, axis=0); k[..., c] = np.roll(k[..., c], b + 1, axis=0)
    return {"ysr": s.reshape(N, 128, A).astype(np.float32), "ylim": l.reshape(N, 128, A).astype(np.float32), "yu": k.astype(np.float32)}

@@ -1,0 +1,676 @@
+import numpy as np
+from concourse.bass import DstId, RemoteDMATransfer
+from concourse.mybir import dt, AluOpType, AxisListType, ActivationFunctionType
+
+AL = AluOpType
+AF = ActivationFunctionType
+s_ = np.s_
+N = 8
+RO = 3
+W1, XV = 192, 384
+ST1 = 6
+NCS = (0, 1, 1)
+NRS = ((2, 16), (2, 16), (5, 9))
+ROWS = sorted(set(NCS + tuple(a for p in NRS for a in p)) - {0, 16})
+LC = 16 * W1 + 3072 + max(NCS) * XV
+B, H, F, I, U = "bfloat16", "float16", "float32", "int32", "uint16"
+SB = {
+    "si": ([128, 768], I), "li": ([128, 768], I), "ui": ([8, 768], I), "fb": ([128, 4096], B),
+    "u16": ([8, 768], H), "hi8": ([8, 768], B), "one": ([128, 512], B), "cb": ([1, 768], B),
+    "wid": ([128, 160], B), "w0": ([128, 160], B), "w1": ([128, 160], B), "nid": ([128, 128], B), "bigi": ([128, 128], B),
+    "blk0": ([128, 128], B), "blk": ([128, 128], B), "tri": ([128, 128], B), "zz": ([128, 7, 144], B), "zc": ([128, 144], H),
+    "z8": ([8, 144], B), "z8d": ([8, 128], B), "zr": ([1, 144], B), "zd": ([1, len(ROWS), 128], B), "ir": ([1, 1536], B),
+    "pi": ([128, 8], I), "pg": ([128, 8], I), "ph": ([128, 8], I), "pb": ([128, 8], I), "cols": ([128, 8], F), "b8": ([128, 8], F),
+    "ai1": ([128, 768], B), "ai2": ([128, 768], B), "meta0": ([128, 768], B),
+    "t0": ([128, 24, 2, 16], H), "pr": ([128, 16, 48], I), "pe": ([128, 16, 24], I),
+    "vi": ([128, 48], I), "vc": ([128, 48], I), "ve": ([128, 24], I), "vj": ([128, 24], I), "vr": ([128, 24], I),
+    "offv": ([128, 16, 24], U), "offc": ([128, 192], U), "offd": ([128, 2, 192], U),
+    "cmpv": ([128, 16, 384], B), "fc": ([128, LC], B), "cmpc": ([128, LC], B),
+    "sw": ([128, 768], F), "hol": ([128, 768], B), "oh": ([128, 768], B), "cum": ([128, 768], H), "cm": ([128, 768], H),
+    "ini": ([128, 4], F), "plc": ([128, 48], U), "orv": ([128, 24], U), "onat": ([128, 48], U),
+    "give": ([128, 384], H), "have": ([128, 384], H), "val": ([128, 384], F), "nrf": ([128, 384], F),
+    "ys": ([128, 768], F), "yin": ([128, 192], F), "yub": ([128, 48], F), "lim3": ([128, 768], B),
+}
+for _t in range(RO):
+    SB.update({"sn%d" % _t: ([128, 768], H), "lim%d" % _t: ([128, 768], B), "ms%d" % _t: ([128, 768], B),
+               "mi%d" % _t: ([128, 192], B), "lo%d" % _t: ([128, 192], B), "offl%d" % _t: ([128, 192], U)})
+    if _t:
+        SB.update({"sin%d" % _t: ([128, 192], H), "offi%d" % _t: ([128, 192], U)})
+SCRATCH = {_k: ("sbuf", _v[0], _v[1]) for _k, _v in SB.items()}
+SCRATCH.update({"pc": ("psum", [128, 1536], F), "pg2": ("psum", [128, 1024], F),
+                "p4": ("psum", [128, 32, 2, 16], F), "pm": ("psum", [128, 512], F)})
+BANK0 = {"pc": 0, "pg2": 3, "p4": 5, "pm": 7}
+SEMAPHORES = ["qV", "qA", "qP", "qG"] + ["d%d" % _k for _k in range(60)]
+
+CY, GA, SCT, PECY, HOP = 0.83, 1.56, 3.8, 0.42, 100.0
+
+
+def _cells(ap):
+    shape = SCRATCH[ap[0]][1]
+    idx = ap[1] if isinstance(ap[1], tuple) else (ap[1],)
+    return np.arange(int(np.prod(shape[1:]))).reshape(shape[1:])[idx[1:]].reshape(-1)
+
+
+def build():
+    ops = []
+    lw, rd, bank, grp = {}, {}, {}, {}
+
+    def add(q, fn, reads, writes, cost, kind="c", acc=None, after=None, lat=0.0):
+        me = len(ops)
+        deps = set()
+        banks = set()
+        for ap, wr in [(a, False) for a in reads] + [(a, True) for a in writes]:
+            nm = ap[0]
+            if nm not in SCRATCH:
+                continue
+            cells = _cells(ap)
+            size = int(np.prod(SCRATCH[nm][1][1:]))
+            if nm not in lw:
+                lw[nm] = np.full(size, -1)
+                rd[nm] = []
+            if nm in BANK0:
+                banks.update(int(b) + BANK0[nm] for b in np.unique(cells // 512))
+            if acc is not None and wr and not acc[0]:
+                continue
+            deps.update(int(w) for w in np.unique(lw[nm][cells]) if w >= 0)
+            m = np.zeros(size, bool)
+            m[cells] = True
+            if wr:
+                keep = []
+                for o, om in rd[nm]:
+                    if (om & m).any():
+                        deps.add(o)
+                        om = om & ~m
+                    if om.any():
+                        keep.append((o, om))
+                rd[nm] = keep
+                lw[nm][cells] = me
+            else:
+                rd[nm].append((me, m))
+        for b in banks:
+            e = bank.setdefault(b, [q, [], []])
+            if e[0] != q:
+                bank[b] = e = [q, [], e[1]]
+            deps.update(e[2])
+            e[1].append(me)
+        if acc is not None:
+            b = min(banks)
+            if acc[0]:
+                if b in grp:
+                    deps.add(grp[b][-1])
+                grp[b] = [me]
+                grp[(b, "c")] = [writes[0]]
+            else:
+                deps.add(grp[b][0])
+                if acc[1]:
+                    deps.update(grp[b])
+                grp[b].append(me)
+                grp[(b, "c")].append(writes[0])
+            if acc[1]:
+                for ap in grp[(b, "c")]:
+                    lw[ap[0]][_cells(ap)] = me
+        deps.discard(me)
+        ops.append({"q": q, "fn": fn, "deps": deps, "cost": cost, "kind": kind, "after": after, "lat": lat})
+        return me
+
+    def n_of(ap):
+        return len(_cells(ap))
+
+    def A_(T, ap):
+        if not isinstance(ap, tuple):
+            return ap
+        if len(ap) == 3:
+            return T[ap[0]][ap[1]].indirect(T[ap[2][0]][ap[2][1]])
+        return T[ap[0]][ap[1]]
+
+    def parts(ap):
+        return [ap[:2], ap[2]] if len(ap) == 3 else [ap]
+
+    def vec(call, out, ins, mul=None, extra=()):
+        reads = [p for a in ins for p in parts(a)] + [e for e in extra if isinstance(e, tuple)] + parts(out)[1:]
+        if len(out) == 3:
+            c = 50 + SCT * CY * n_of(ins[0])
+        elif len(ins[0]) == 3:
+            c = 50 + GA * CY * n_of(out)
+        else:
+            if mul is None:
+                mul = 0.5 if all(SCRATCH[a[0]][2] in (B, H, U) for a in [out] + ins) else 1
+            c = max(64, mul * n_of(out)) * CY
+        return add("V", call, reads, [out[:2]], c)
+
+    def v_copy(out, a):
+        return vec(lambda g, T: g.vector.tensor_copy(A_(T, out), A_(T, a)), out, [a])
+
+    def v_tt(out, a, b, op):
+        return vec(lambda g, T: g.vector.tensor_tensor(A_(T, out), A_(T, a), A_(T, b), op), out, [a, b],
+                   1 if a[0] in BANK0 or b[0] in BANK0 else 2)
+
+    def v_ts(out, a, s1, op0, s2=None, op1=None):
+        def call(g, T):
+            if op1 is None:
+                return g.vector.tensor_scalar(A_(T, out), A_(T, a), A_(T, s1), None, op0)
+            return g.vector.tensor_scalar(A_(T, out), A_(T, a), A_(T, s1), A_(T, s2), op0, op1)
+        return vec(call, out, [a], None, (s1, s2))
+
+    def v_set(out, c):
+        return add("V", lambda g, T: g.vector.memset(A_(T, out), c), [], [out], max(64, n_of(out) / 2) * CY)
+
+    def v_tr(out, a):
+        return vec(lambda g, T: g.vector.transpose(A_(T, out), A_(T, a)), out, [a])
+
+    def v_scan(out, a, ini):
+        return vec(lambda g, T: g.vector.tensor_tensor_scan(A_(T, out), A_(T, a), A_(T, a), A_(T, ini), AL.add, AL.max), out, [a], None, (ini,))
+
+    def act(out, a, func, bias=0.0, scale=1.0):
+        c = 65 + GA * CY * n_of(out) if len(a) == 3 else max(64, n_of(out)) * CY + 30
+
+        def call(g, T):
+            if func == AF.Copy:
+                return g.scalar.activation(A_(T, out), A_(T, a), func, scale=A_(T, scale))
+            return g.scalar.activation(A_(T, out), A_(T, a), func, bias=bias, scale=A_(T, scale))
+        return add("A", call, parts(a) + ([scale] if isinstance(scale, tuple) else []), [out], c)
+
+    def mm(out, l, r, start, stop, after=None):
+        return add("P", lambda g, T: g.tensor.matmul(A_(T, out), A_(T, l), A_(T, r), start, stop), [l, r], [out],
+                   max(64, n_of(r)) * PECY, acc=(start, stop), after=after)
+
+    def group(items, after=None):
+        for k, (o, l, r) in enumerate(items):
+            mm(o, l, r, k == 0, k == len(items) - 1, after)
+
+    def g_iota(out, pat, base, cm):
+        def call(g, T):
+            if SCRATCH[out[0]][2] != I:
+                return g.iota(A_(T, out), pat, base, cm, allow_small_or_imprecise_dtypes=True)
+            return g.iota(A_(T, out), pat, base, cm)
+        return add("G", call, [], [out], 130 + 2 * CY * n_of(out))
+
+    def g_sel(out, a, pat, cmp, base, cm):
+        return add("G", lambda g, T: g.affine_select(A_(T, out), A_(T, a), pat, cmp, 0.0, base, cm), [a], [out], 170 + 2 * CY * n_of(out))
+
+    def dma(q, out, a, lat):
+        return add(q, lambda g, T: {"S": g.sync, "A": g.scalar, "G": g}[q].dma_start(A_(T, out), A_(T, a)), [a], [out], 60.0, kind="dma", lat=lat)
+
+    def send(src, c0, dst, d0):
+        srcs = [(src, s_[:, c0 + 64 * b:c0 + 64 * b + 64]) for b in range(3)]
+        dsts = [(dst, s_[:, d0 + 64 * b:d0 + 64 * b + 64]) for b in range(3)]
+        me = add("G", (srcs, dsts), srcs, [], 700.0, kind="send", lat=4500.0)
+        ops[me]["arr"] = [add("R", b, [], [dsts[b]], 0.0, kind="arr", after=me) for b in range(3)]
+
+    ID = ("wid", s_[:, 16:144])
+    Z4096, Z2048, Z1, ZU, ZO = range(5)
+    B_CV, B_CC, B_2K, B_RV, B_BIG, B_D = range(6)
+
+    def zq(k, q):
+        return ("zz", s_[:, k, 15 - q:143 - q])
+
+    def bias(k):
+        return ("cb", s_[0:1, 128 * k:128 * k + 128])
+
+    def ones(n):
+        return ("one", s_[0:1, 0:n])
+
+    def rows(a):
+        return ("zd", s_[:, ROWS.index(a), :])
+
+    dma("S", ("si", s_[:]), ("sr", s_[:]), 3000.0)
+    dma("A", ("ui", s_[:]), ("u", s_[:]), 2200.0)
+    dma("S", ("li", s_[:]), ("lim", s_[:]), 4000.0)
+    dma("S", ("fb", s_[:]), ("fit", s_[:]), 8000.0)
+    v_set(("one", s_[:]), 1.0)
+    g_iota(("pi", s_[:]), [[-16, 8]], 0, 1)
+    v_set(("zz", s_[:]), 0.0)
+    v_set(("zc", s_[:]), 0.0)
+    v_set(("zr", s_[:]), 0.0)
+    for k, c in enumerate((-47104.0, -14336.0, 2048.0, -30720.0, 67108864.0, 32768.0)):
+        v_set(bias(k), c)
+    g_sel(("z8", s_[:]), ("one", s_[0:8, 0:144]), [[1, 144]], AL.is_equal, -15, -16)
+    g_sel(("wid", s_[:]), ("one", s_[:, 0:160]), [[1, 160]], AL.is_equal, -16, -1)
+    for a in ROWS:
+        g_sel(rows(a), bias(B_D), [[0, 8], [-1, 16]], AL.is_ge, a - 1, 0)
+    g_iota(("ir", s_[:, 0:768]), [[32, 24], [0, 32]], 0, 0)
+    g_iota(("ir", s_[:, 768:1536]), [[0, 24], [1, 32]], 0, 0)
+    g_sel(("blk0", s_[:]), ("one", s_[:, 0:128]), [[-16, 8], [0, 16]], AL.is_ge, 0, 1)
+    g_sel(("blk", s_[:]), ("blk0", s_[:]), [[16, 8], [0, 16]], AL.is_ge, 15, -1)
+    g_sel(("tri", s_[:]), ("blk", s_[:]), [[1, 128]], AL.is_gt, 0, -1)
+    v_set(("zr", s_[:, 15:144:16]), 1.0)
+    v_ts(("pg", s_[:]), ("pi", s_[:]), 4, AL.arith_shift_right)
+    v_ts(("ph", s_[:]), ("pi", s_[:]), 1, AL.arith_shift_right)
+    v_ts(("pb", s_[:, 0:1]), ("pi", s_[:, 0:1]), 4, AL.arith_shift_right, 1, AL.bitwise_and)
+    v_ts(("pb", s_[:, 1:2]), ("pi", s_[:, 0:1]), 15, AL.bitwise_and)
+    v_ts(("zz", s_[:, Z4096, 15:128:16]), ("pg", s_[:]), 0.0, AL.is_equal, 4096.0, AL.mult)
+    v_ts(("zz", s_[:, Z2048, 15:128:16]), ("pg", s_[:]), 0.0, AL.is_equal, 2048.0, AL.mult)
+    v_copy(("cols", s_[:, 0:2]), ("pb", s_[:, 0:2]))
+    v_ts(("cols", s_[:, 2:3]), ("pb", s_[:, 0:1]), 0.0, AL.is_equal)
+    v_ts(("zz", s_[:, Z1, 15:128:16]), ("pg", s_[:]), 0.0, AL.is_equal)
+    v_ts(("b8", s_[:]), ("pg", s_[:]), 0.0, AL.is_equal)
+    for k in range(4):
+        v_ts(("zz", s_[:, ZU + k, 15:128:16]), ("ph", s_[:]), float(k), AL.is_equal)
+    v_tt(("z8d", s_[:]), ("z8", s_[:, 15:143]), ("z8", s_[:, 14:142]), AL.subtract)
+    v_ts(("u16", s_[:]), ("ui", s_[:]), -2048.0, AL.add)
+    act(("w0", s_[:]), ("wid", s_[:]), AF.Copy, scale=("cols", s_[:, 2:3]))
+    act(("w1", s_[:]), ("wid", s_[:]), AF.Copy, scale=("cols", s_[:, 0:1]))
+    act(("nid", s_[:]), ID, AF.Copy, scale=-1.0)
+    act(("bigi", s_[:]), ID, AF.Copy, scale=-32768.0)
+    group([(("pm", s_[:, 0:48]), ("z8", s_[:, 15 - q:143 - q]), ("u16", s_[:, q:768:16])) for q in range(16)])
+    for lo, hi in ((0, 512), (512, 768)):
+        mm(("pg2", s_[0:8, lo:hi]), ("wid", s_[0:8, 16:24]), ("u16", s_[:, lo:hi]), True, True)
+    act(("hi8", s_[:]), ("pg2", s_[0:8, 0:768]), AF.Copy)
+    v_ts(("sn0", s_[:]), ("si", s_[:]), -2048.0, AL.add)
+    v_tr(("t0", s_[:]), ("sn0", s_[:]))
+
+    def keys(out, tmp, n, t, src):
+        v_ts((tmp, s_[:, 0:n]), src, 2048.0 + 997 * t, AL.add)
+        v_ts((out, s_[:, 0:n]), (tmp, s_[:, 0:n]), 4095, AL.bitwise_and)
+    keys("vc", "vi", 48, 0, ("pm", s_[:, 0:48]))
+    v_copy(("lim0", s_[:]), ("li", s_[:]))
+
+    def own_number(t, lo, hi):
+        o = ("pg2", s_[:, lo:hi])
+        return [(o, ("zr", s_[:, 13 - 2 * t:141 - 2 * t]), ("ir", s_[:, lo:hi])),
+                (o, ("zr", s_[:, 12 - 2 * t:140 - 2 * t]), ("ir", s_[:, 768 + lo:768 + hi]))]
+    hold = [None]
+
+    def offsets(runs, p0, v, pr, first, staged):
+        nb = sum(hi - lo for lo, hi in runs)
+        for k0 in range(p0 // 16, (p0 + nb + 15) // 16):
+            a0, a1 = max(p0, 16 * k0), min(p0 + nb, 16 * k0 + 16)
+            items = [(("p4", s_[:, a0:a1]), bias(B_2K), ones(32 * (a1 - a0)))]
+            at = p0
+            for lo, hi in runs:
+                x0, x1 = max(at, a0), min(at + hi - lo, a1)
+                for b in range(2):
+                    for x in range(2):
+                        c0 = 16 + 16 * (b - x)
+                        if x1 > x0:
+                            items.append((("p4", s_[:, x0:x1, b, :]), ("w%d" % b, s_[:, c0:c0 + 128]),
+                                          ("t0", s_[:, lo + x0 - at:lo + x1 - at, x, :])))
+                at += hi - lo
+            group(items, len(ops) - 1 if k0 > p0 // 16 else None)
+        nm = 2 * nb
+        hold[0] = len(ops) - 1
+        for i0, i1 in ((0, ST1), (ST1, 16)) if staged else ((0, 16),):
+            for i in range(i0, i1):
+                v_tt((pr, s_[:, i, 0:nm]), ("p4", s_[:, p0:p0 + nb, :, i]), v, AL.mult)
+            v_ts((pr, s_[:, i0:i1, 0:nm]), (pr, s_[:, i0:i1, 0:nm]), 5, AL.arith_shift_right, 4095, AL.bitwise_and)
+            for buf, r, m0 in first:
+                dst = (buf, s_[:, 12 * i0:12 * i1]) if r is None else (buf, s_[:, r, 12 * i0:12 * i1])
+                v_copy(dst, (pr, s_[:, i0:i1, m0:m0 + 12]))
+
+    def leaving(offl, pr, m0):
+        for b in range(3):
+            v_copy((offl, s_[:, 64 * b:64 * b + 64]), (pr, s_[:, :, m0 + 4 * b:m0 + 4 * b + 4]))
+
+    FIT = ("fb", s_[:, 0:4096])
+
+    def stream(parts_):
+        gath, segl, at = [], [], 0
+        for buf, c0, cuts, ss in parts_:
+            for a, b in zip(cuts[:-1], cuts[1:]):
+                lo, hi = c0 + a // 16, c0 + b // 16
+                gath.append((at + a, at + b, (buf, s_[:, lo:hi]) if isinstance(buf, str) else (buf[0], s_[:, buf[1], lo:hi])))
+            for w, i, c in ss:
+                segl.append((at, at + w, i, c))
+                at += w
+        cuts = list(range(0, at, 512)) + [at]
+        return gath, segl, list(zip(cuts[:-1], cuts[1:]))
+
+    def cut(segl, a, b):
+        return [(max(a, p), min(b, q), i, c + max(a, p) - p) for p, q, i, c in segl if p < b and q > a]
+
+    def scalar_path(st, lim, count):
+        gath, segl, units = st
+        gi = [0]
+
+        def upto(x):
+            while gi[0] < len(gath) and gath[gi[0]][0] < x:
+                a, b, off = gath[gi[0]]
+                act(("fc", s_[:, a:b]), FIT + (off,), AF.Copy)
+                gi[0] += 1
+
+        def sub(u):
+            a, b = units[u]
+            base = 512 * (u % 2) - a
+            group([(("pg2", s_[:, base + a:base + b]), ID, ("fc", s_[:, a:b]))] +
+                  [(("pg2", s_[:, base + p:base + q]), ("nid", s_[:]), (lim, s_[:, c:c + q - p])) for p, q, i, c in cut(segl, a, b)])
+        upto(units[0][1])
+        sub(0)
+        for u, (a, b) in enumerate(units):
+            if u + 1 < len(units):
+                upto(units[min(u + 2, len(units) - 1)][1])
+                sub(u + 1)
+            act(("cmpc", s_[:, a:b]), ("pg2", s_[:, 512 * (u % 2):512 * (u % 2) + b - a]), AF.Sign, bias=-0.5)
+            for p, q, i, c in cut(segl, a, b):
+                count(p, q, i, c)
+
+    def head(buf, c, n1):
+        out = []
+        for a, b in ((0, min(n1, ST1)), (ST1, n1)):
+            if b > a:
+                n = (b - a) * 192
+                out.append((buf, a * 12, list(range(0, max(n - 399, 1), 1024 if a else 576)) + [n], [(192, i, c) for i in range(a, b)]))
+        return out
+
+    def grouped(todo):
+        def go(o, l, r, b):
+            todo[b] -= 1
+            mm(o, l, r, False, todo[b] == 0)
+        return go
+
+    offsets([(0, 24)], 0, ("vc", s_[:]), "pr", [("offc", None, 0)], True)
+    v_copy(("offv", s_[:]), ("pr", s_[:, :, 12:36]))
+    leaving("offl0", "pr", 36)
+    for lo, hi in ((0, 512), (512, 768)):
+        o = ("pg2", s_[:, lo:hi])
+        group([(o, ("z8", s_[:, 14:142]), ("u16", s_[:, lo:hi])), (o, ("z8d", s_[:]), ("hi8", s_[:, lo:hi]))] + own_number(0, lo, hi), hold[0])
+    act(("meta0", s_[:]), ("pg2", s_[:, 0:768]), AF.Copy)
+
+    for t in range(RO):
+        last = t == RO - 1
+        lim, sn, ms, limn = "lim%d" % t, "sn%d" % t, "ms%d" % t, "lim%d" % (t + 1)
+        offi = "offi%d" % t if t else "offl0"
+        NC = NCS[t]
+        st = stream(head("offc", 0, 16) + [(("offv", i), 0, [0, XV], [(XV, i, W1)]) for i in range(NC)] +
+                    [(offi, 64 * b, [0, 1024], [(64, i, 576 + 64 * b) for i in range(16)]) for b in range(3)])
+
+        def split(p, q, c):
+            out = []
+            if c < 512:
+                e = min(q, p + 512 - c)
+                out.append((p, e, c, 0))
+                p, c = e, c + e - p
+            if p < q:
+                out.append((p, q, c, 1) if c < 576 else (p, q, c + 448, 2))
+            return out
+        todo = {0: 17 - NC + (NC > 0), 1: 16 - NC + (NC > 0), 2: 0}
+        for a, b in st[2]:
+            for p, q, i, c in cut(st[1], a, b):
+                for x in split(p, q, c):
+                    todo[x[3]] += 1
+        go = grouped(todo)
+        mm(("pc", s_[:, 0:512]), bias(B_CV), ones(512), True, False)
+        go(("pc", s_[:, 0:W1]), bias(B_D), ones(W1), 0)
+        mm(("pc", s_[:, 512:576]), bias(B_CV), ones(64), True, False)
+        if NC:
+            go(("pc", s_[:, W1:512]), rows(NC), ones(512 - W1), 0)
+            go(("pc", s_[:, 512:576]), rows(NC), ones(64), 1)
+        mm(("pc", s_[:, 1024:1216]), bias(B_CC), ones(192), True, False)
+
+        def count_c(p, q, i, c):
+            for a, b, col, bk in split(p, q, c):
+                go(("pc", s_[:, col:col + b - a]), zq(Z2048, i), ("cmpc", s_[:, a:b]), bk)
+        for i in range(NC, 16):
+            v_tt(("cmpv", s_[:, i, :]), FIT + (("offv", s_[:, i, :]),), (lim, s_[:, W1:576]), AL.is_gt)
+        scalar_path(st, lim, count_c)
+        for i in range(NC, 16):
+            go(("pc", s_[:, W1:512]), zq(Z4096, i), ("cmpv", s_[:, i, 0:512 - W1]), 0)
+            go(("pc", s_[:, 512:576]), zq(Z4096, i), ("cmpv", s_[:, i, 512 - W1:XV]), 1)
+        halves = ((0, 288, 0), (288, 576, 16))
+        for lo, hi, n0 in halves:
+            v_tt(("sw", s_[:, lo:hi]), ("pc", s_[:, lo:hi]), (sn, s_[:, lo:hi]), AL.max)
+        for lo, hi, n0 in halves:
+            v_ts(("hol", s_[:, lo:hi]), ("sw", s_[:, lo:hi]), 2048.0, AL.is_ge)
+            mm(("p4", s_[:, n0:n0 + 9]), ("blk", s_[:]), ("hol", s_[:, lo:hi]), True, True)
+        for lo, hi, n0 in halves:
+            v_ts(("oh", s_[:, lo:hi]), ("p4", s_[:, n0:n0 + 9]), 15.0, AL.min, ("cols", s_[:, 1:2]), AL.is_equal)
+        c = s_[:, 0:576]
+        v_scan(("cum", c), ("oh", c), 0.0)
+        v_tt(("cm", c), ("cum", c), ("oh", c), AL.mult)
+        v_copy(("ini", s_[:, 0:1]), ("cum", s_[:, 575:576]))
+        c = s_[:, 576:768]
+        v_tt(("sw", c), ("pc", s_[:, 1024:1216]), ("sin%d" % t, s_[:]) if t else (sn, c), AL.max)
+        v_ts(("hol", c), ("sw", c), 2048.0, AL.is_ge)
+        mm(("p4", s_[:, 0:6]), ("blk", s_[:]), ("hol", c), True, True)
+        v_ts(("oh", c), ("p4", s_[:, 0:6]), 15.0, AL.min, ("cols", s_[:, 1:2]), AL.is_equal)
+        v_scan(("cum", c), ("oh", c), ("ini", s_[:, 0:1]))
+        mm(("pg2", s_[:, 0:1]), ("tri", s_[:]), ("cum", s_[:, 767:768]), True, True)
+        v_tt(("cm", c), ("cum", c), ("oh", c), AL.mult)
+        v_ts(("zc", s_[:, 15:128:16]), ("b8", s_[:]), ("pg2", s_[:, 0:1]), AL.mult)
+        group([(("pm", s_[:, 0:48]), zq(Z1, q), ("cm", s_[:, q:768:16])) for q in range(16)] +
+              [(("pm", s_[:, 0:48]), ("zc", s_[:, 15 - q:143 - q]), ("oh", s_[:, q:768:16])) for q in range(16)])
+        v_ts(("plc", s_[:]), ("pm", s_[:, 0:48]), -1.0, AL.add)
+        if t == 0:
+            v_copy((ms, s_[:, 0:768], ("plc", s_[:])), ("meta0", s_[:]))
+            for k in (1, 2):
+                for lo, hi in ((0, 512), (512, 768)):
+                    group(own_number(k, lo, hi))
+                act(("ai%d" % k, s_[:]), ("pg2", s_[:, 0:768]), AF.Copy)
+        else:
+            ai = "ai%d" % t
+            v_tt((ms, s_[:, 0:768], ("plc", s_[:, 0:36])), ("ms%d" % (t - 1), s_[:, 0:576]), (ai, s_[:, 0:576]), AL.add)
+            v_tt((ms, s_[:, 0:768], ("plc", s_[:, 36:48])), ("mi%d" % (t - 1), s_[:]), (ai, s_[:, 576:768]), AL.add)
+        group([(("pm", s_[:, 0:24]), zq(ZO + t, q), (ms, s_[:, 767 - q:383 - q:-16])) for q in range(16)])
+        group([(("pg2", s_[:, 0:48]), zq(ZO + t, q), (ms, s_[:, q:768:16])) for q in range(16)])
+        nu = 24 if last else 48
+        group([(("pg2", s_[:, 512:512 + nu]), zq(ZU, q), (ms, s_[:, q:16 * nu:16])) for q in range(16)])
+        send(ms, 576, "mi%d" % t, 0)
+        SW = ("sw", s_[:, 0:768])
+        LW = (lim, s_[:, 0:768])
+        v_copy(("orv", s_[:]), ("pm", s_[:, 0:24]))
+        v_ts(("give", s_[:]), SW + (("orv", s_[:]),), 2048.0, AL.min)
+        v_copy(("onat", s_[:]), ("pg2", s_[:, 0:48]))
+        v_tr(("t0", s_[:, 0:12]), ("give", s_[:]))
+        keys("vr", "vj", 24, t, ("pg2", s_[:, 512:536]))
+        act((limn, s_[:, 0:384]), LW + (("onat", s_[:, 0:24]),), AF.Copy)
+        act(("lo%d" % t, s_[:]), LW + (("onat", s_[:, 36:48]),), AF.Copy)
+        send("lo%d" % t, 0, limn, 576)
+        act((limn, s_[:, 384:576]), LW + (("onat", s_[:, 24:36]),), AF.Copy)
+        offsets([(0, 12)], 0, ("vr", s_[:]), "pr", [("offd", 0, 0), ("offd", 1, 12)], True)
+        if not last:
+            keys("vc", "vi", 48, t + 1, ("pg2", s_[:, 512:560]))
+            v_ts(("ve", s_[:, 0:12]), ("vi", s_[:, 0:12]), 4095, AL.bitwise_and)
+            v_ts(("ve", s_[:, 12:24]), ("vi", s_[:, 36:48]), 4095, AL.bitwise_and)
+        v_ts(("have", s_[:]), SW + (("onat", s_[:, 0:24]),), 2048.0, AL.min)
+        TP = ("pm", s_[:, 0:384])
+        group([(TP, ID, ("give", s_[:])), (TP, ID, ("have", s_[:]))] + ([(TP, bias(B_2K), ones(384))] if last else []))
+        mm(("pc", s_[:, 1024:1408]), ID, ("have", s_[:]), True, True)
+        a1, a2 = NRS[t]
+        st = stream(head(("offd", 0), 0, a1) + head(("offd", 1), 192, a2))
+        todo = {0: 18 - a1 + (a1 < 16), 1: 18 - a2 + (a2 < 16)}
+        for a, b in st[2]:
+            for p, q, i, c in cut(st[1], a, b):
+                todo[c // 192] += 1
+        go = grouped(todo)
+        for r, a in enumerate((a1, a2)):
+            o = ("pc", s_[:, 512 * r:512 * r + 192])
+            mm(o, bias(B_RV if a < 16 else B_2K), ones(192), True, False)
+            if a < 16:
+                go(o, rows(a), ones(192), r)
+            go(o, ("bigi", s_[:]), ("have", s_[:, 192 * r:192 * r + 192]), r)
+            go(o, bias(B_BIG), ones(192), r)
+
+        def count_r(p, q, i, c):
+            col = c + 320 * (c // 192)
+            go(("pc", s_[:, col:col + q - p]), zq(Z2048, i), ("cmpc", s_[:, p:q]), c // 192)
+        scalar_path(st, limn, count_r)
+        new = "ys" if last else "sn%d" % (t + 1)
+        rec = "nrf" if last else new
+        for r in range(2):
+            lo, hi = 192 * r, 192 * r + 192
+            c = s_[:, lo:hi]
+            for i in range(NRS[t][r], 16):
+                v_tt(("cmpv", s_[:, i, lo:hi]), FIT + (("offd", s_[:, r, 12 * i:12 * i + 12]),), (limn, c), AL.is_gt)
+                go(("pc", s_[:, 512 * r:512 * r + 192]), zq(Z4096, i), ("cmpv", s_[:, i, lo:hi]), r)
+            v_tt(("val", c), ("pc", s_[:, 512 * r:512 * r + 192]), ("give", c), AL.max)
+            v_tt((rec, c), ("pc", s_[:, 1024 + lo:1024 + hi]), ("val", c), AL.min)
+            v_tt((new, s_[:, 767 - lo:767 - hi:-1]), ("pm", c), (rec, c), AL.subtract)
+            if r == 0:
+                send(new, 576, "yin" if last else "sin%d" % (t + 1), 0)
+            if last:
+                act(("ys", c), ("nrf", c), AF.Identity, bias=2048.0)
+                if r == 0:
+                    dma("S", ("ysr", c), ("ys", c), 2000.0)
+                    yp = ("p4", s_[:, 16:19, 0, :])
+                    group([(yp, zq(ZU, k), ("ms2", s_[:, 48 * k:48 * k + 48]) if k < 12 else ("mi2", s_[:, 48 * k - 576:48 * k - 528]))
+                           for k in range(16)])
+                    act(("yub", s_[:]), yp, AF.Identity, bias=2048.0)
+                    dma("S", ("yu", s_[:]), ("yub", s_[:]), 2000.0)
+            elif r == 0:
+                v_tr(("t0", s_[:, 0:6]), (new, s_[:, 0:192]))
+                v_tr(("t0", s_[:, 18:24]), (new, s_[:, 576:768]))
+                offsets([(0, 6), (18, 24)], 0, ("ve", s_[:]), "pe", [("offc", None, 0)], False)
+                leaving("offl%d" % (t + 1), "pe", 12)
+                send("offl%d" % (t + 1), 0, "offi%d" % (t + 1), 0)
+            else:
+                v_tr(("t0", s_[:, 6:18]), (new, s_[:, 192:576]))
+                offsets([(6, 18)], 16, ("vc", s_[:, 12:36]), "pr", [], False)
+                v_copy(("offv", s_[:]), ("pr", s_[:, :, 0:24]))
+    dma("S", ("ysr", s_[:, 192:576]), ("ys", s_[:, 192:576]), 2000.0)
+    dma("A", ("ysr", s_[:, 576:768]), ("yin", s_[:]), 2000.0)
+    dma("G", ("ylim", s_[:]), ("lim3", s_[:]), 2500.0)
+    return ops
+
+
+def lay_out(ops):
+    n = len(ops)
+    pre = [set(o["deps"]) | ({o["after"]} if o["after"] is not None else set()) for o in ops]
+    users = [[] for _ in ops]
+    for k, p in enumerate(pre):
+        for d in p:
+            users[d].append(k)
+    left = [len(p) for p in pre]
+    ready = [0.0] * n
+    queues = {}
+    for k, o in enumerate(ops):
+        queues.setdefault(o["q"], []).append(k)
+    head = {q: 0 for q in queues}
+    free = {q: 0.0 for q in queues}
+    level = [0.0] * n
+    nxt = {}
+    for k in range(n - 1, -1, -1):
+        o = ops[k]
+        m = max([level[u] + o["lat"] + HOP for u in users[k]] + [0.0])
+        if o["q"] not in "PR":
+            m = max(m, nxt.get(o["q"], 0.0))
+        level[k] = m + o["cost"]
+        nxt[o["q"]] = level[k]
+    loose = set(k for k in range(n) if ops[k]["q"] in "PR" and left[k] == 0)
+    order = []
+    while len(order) < n:
+        cand = list(loose)
+        for q in queues:
+            if q not in "PR" and head[q] < len(queues[q]) and left[queues[q][head[q]]] == 0:
+                cand.append(queues[q][head[q]])
+        k = min(cand, key=lambda c: (max(ready[c], free[ops[c]["q"]]), -level[c], c))
+        o = ops[k]
+        st = max(ready[k], free[o["q"]])
+        free[o["q"]] = st + o["cost"]
+        if o["q"] in "PR":
+            loose.discard(k)
+        else:
+            head[o["q"]] += 1
+        order.append(k)
+        for u in users[k]:
+            hop = 0.0 if o["q"] == ops[u]["q"] == "P" else HOP
+            ready[u] = max(ready[u], st + o["cost"] + o["lat"] + hop)
+            left[u] -= 1
+            if left[u] == 0 and ops[u]["q"] in "PR":
+                loose.add(u)
+    return order
+
+
+def plan():
+    ops = build()
+    order = lay_out(ops)
+    pos = {k: j for j, k in enumerate(order)}
+    known = {}
+    for k in order:
+        o = ops[k]
+        o["waits"] = []
+        if o["kind"] == "arr":
+            o["clock"] = {}
+            continue
+        kn = known.setdefault(o["q"], {})
+        for d in sorted(o["deps"], key=lambda x: -pos[x]):
+            e = ops[d]
+            key = e["q"] if e["kind"] == "c" else d
+            if o["q"] == e["q"] == "P" or kn.get(key, -1) >= pos[d]:
+                continue
+            o["waits"].append(d)
+            e["sig"] = True
+            kn[key] = pos[d]
+            for a, b in e["clock"].items():
+                if kn.get(a, -1) < b:
+                    kn[a] = b
+        o["clock"] = dict(kn)
+    cnt, nd = {}, 0
+    for k in order:
+        o = ops[k]
+        if o["kind"] == "c":
+            if o.get("sig"):
+                cnt[o["q"]] = cnt.get(o["q"], 0) + 1
+                o["sem"], o["n"] = "q" + o["q"], cnt[o["q"]]
+        else:
+            o["sem"] = "d%d" % nd
+            nd += 1
+    return ops, order
+
+
+PLAN = []
+
+
+def engine_sets(topo, src, dsts):
+    can = [topo.engines(src, d) for d in dsts]
+    pool = [e for e in can[0] if all(e in c for c in can)]
+    out = [None] * len(dsts)
+    for k, c in enumerate(can):
+        own = [e for e in c if e not in pool and not any(o and e in o for o in out)]
+        if own:
+            out[k] = own
+    rest = [k for k in range(len(dsts)) if out[k] is None]
+    for j, k in enumerate(rest):
+        left = len(rest) - j
+        n = 1
+        while (left + 1) * n <= len(pool):
+            n *= 2
+        out[k], pool = pool[:n], pool[n:]
+    return out
+
+
+def rank_program(g, core, T, topo):
+    rank = T.rank_of(core)
+    if rank is None:
+        return
+    if not PLAN:
+        PLAN.append(plan())
+    ops, order = PLAN[0]
+    cores = T.cores
+
+    def sets(r):
+        return engine_sets(topo, cores[r], [cores[(r + 1 + b) % N] for b in range(3)])
+    mine = sets(rank)
+    Q = {"V": g.vector, "A": g.scalar, "P": g.tensor, "G": g, "S": g.sync}
+
+    def full(o):
+        if o["kind"] == "c":
+            return o["n"]
+        if o["kind"] == "dma":
+            return 16
+        if o["kind"] == "send":
+            return sum(len(e) for e in mine)
+        return len(sets((rank - 1 - o["fn"]) % N)[o["fn"]])
+    for k in order:
+        o = ops[k]
+        if o["kind"] == "arr":
+            continue
+        for d in o["waits"]:
+            Q[o["q"]].wait_ge(T.sem[ops[d]["sem"]], full(ops[d]))
+        if o["kind"] == "send":
+            srcs, dsts = o["fn"]
+            trs = []
+            for b in range(3):
+                rid, pid, _se = topo.addr(cores[(rank + 1 + b) % N])
+                trs.append(RemoteDMATransfer(dst_ids=[DstId(rid=rid, pnc=pid)], dma_engine_mask=sum(1 << e for e in mine[b]),
+                                             remote_sem=T.sem[ops[o["arr"][b]]["sem"]],
+                                             src=T[srcs[b][0]][srcs[b][1]], dst=T[dsts[b][0]][dsts[b][1]]))
+            g.remote_dma_fused(trs, local_sem=T.sem[o["sem"]])
+            continue
+        ins = o["fn"](g, T)
+        if o["kind"] == "dma":
+            ins.then_inc(T.sem[o["sem"]], 16)
+        elif o.get("sig"):
+            ins.then_inc(T.sem[o["sem"]], 1)
+    for k in order:
+        o = ops[k]
+        if o["kind"] != "c" and not o.get("sig"):
+            g.wait_ge(T.sem[o["sem"]], full(o))

@@ -7,42 +7,46 @@ AF = ActivationFunctionType
 s_ = np.s_
 N = 8
 RO = 3
-W1, XV = 192, 384
-ST1 = 6
-NCS = (0, 1, 1)
-NRS = ((2, 16), (2, 16), (5, 9))
-ROWS = sorted(set(NCS + tuple(a for p in NRS for a in p)) - {0, 16})
-LC = 16 * W1 + 3072 + max(NCS) * XV
+VS = 288
+CHK0 = (((160, 288), (64, 160)), ((0, 64),))
+CHK = (((320, 384), (256, 320), (192, 256), (64, 192)), ((0, 64),))
+ROBV = (((0, 192),), ((0, 192),), ((0, 128), (192, 288)))
+ROBS = (((320, 384), (256, 320), (192, 256)),) * 2 + (((128, 192), (288, 384)),)
+ONV0 = ((0, 0), (1, 1), (1, 1), (1, 1))
+ONV = ((1, 1), (1, 1), (1, 1), (1, 1))
+NV0 = (768 - VS) // 16
+LC = 9216
 B, H, F, I, U = "bfloat16", "float16", "float32", "int32", "uint16"
 SB = {
     "si": ([128, 768], I), "li": ([128, 768], I), "ui": ([8, 768], I), "fb": ([128, 4096], B),
-    "u16": ([8, 768], H), "hi8": ([8, 768], B), "one": ([128, 512], B), "cb": ([1, 768], B),
+    "u16": ([8, 784], H), "flag": ([64, 768], B), "hi": ([64, 768], B), "one": ([128, 512], B), "cb": ([1, 640], B), "ck": ([1, 128], H),
     "wid": ([128, 160], B), "w0": ([128, 160], B), "w1": ([128, 160], B), "nid": ([128, 128], B), "bigi": ([128, 128], B),
-    "blk0": ([128, 128], B), "blk": ([128, 128], B), "tri": ([128, 128], B), "zz": ([128, 7, 144], B), "zc": ([128, 144], H),
-    "z8": ([8, 144], B), "z8d": ([8, 128], B), "zr": ([1, 144], B), "zd": ([1, len(ROWS), 128], B), "ir": ([1, 1536], B),
-    "pi": ([128, 8], I), "pg": ([128, 8], I), "ph": ([128, 8], I), "pb": ([128, 8], I), "cols": ([128, 8], F), "b8": ([128, 8], F),
+    "blk0": ([128, 128], B), "blk": ([128, 128], B), "up": ([128, 128], B), "dn": ([128, 128], B), "dia": ([128, 128], B),
+    "d1": ([128, 128], B), "d2": ([128, 128], B), "bk": ([128, 3, 128], B),
+    "zz": ([128, 8, 144], B), "zc": ([128, 144], H), "z8": ([8, 144], B), "b8w": ([8, 128], B), "zr": ([1, 144], B), "ir": ([1, 2, 784], B),
+    "r3": ([8, 64], B), "pu": ([8, 128], B), "ev": ([64, 144], B), "phi": ([64, 128], B), "pfl": ([64, 128], B),
+    "n4k": ([64, 64], B),
+    "pi": ([128, 8], I), "pg": ([128, 8], I), "ph": ([128, 8], I), "pb": ([128, 8], I), "cols": ([128, 20], F), "b8": ([128, 8], F),
     "ai1": ([128, 768], B), "ai2": ([128, 768], B), "meta0": ([128, 768], B),
-    "t0": ([128, 24, 2, 16], H), "pr": ([128, 16, 48], I), "pe": ([128, 16, 24], I),
-    "vi": ([128, 48], I), "vc": ([128, 48], I), "ve": ([128, 24], I), "vj": ([128, 24], I), "vr": ([128, 24], I),
-    "offv": ([128, 16, 24], U), "offc": ([128, 192], U), "offd": ([128, 2, 192], U),
-    "cmpv": ([128, 16, 384], B), "fc": ([128, LC], B), "cmpc": ([128, LC], B),
-    "sw": ([128, 768], F), "hol": ([128, 768], B), "oh": ([128, 768], B), "cum": ([128, 768], H), "cm": ([128, 768], H),
-    "ini": ([128, 4], F), "plc": ([128, 48], U), "orv": ([128, 24], U), "onat": ([128, 48], U),
-    "give": ([128, 384], H), "have": ([128, 384], H), "val": ([128, 384], F), "nrf": ([128, 384], F),
+    "sn0": ([128, 768 - VS], H), "t0": ([128, 16, 2, 16], H), "pq": ([128, 16, 48], I), "vt": ([128, 48], F), "pw": ([128, 384], I),
+    "off0": ([128, 16, NV0], U), "offr": ([128, 16, 16], U), "offd": ([128, 16, 24], U), "onr": ([128, 384], U), "onc": ([128, 384], U),
+    "cv": ([128, 16, 768 - VS], B), "cr": ([128, 16, 256], B), "fc": ([128, LC], B), "cc": ([128, LC], B),
+    "sw": ([128, 768], F), "hol": ([128, 784], B), "th": ([128, 768], B), "cum": ([128, 768], H), "cm": ([128, 768], H),
+    "ini": ([128, 8], F), "plc": ([128, 48], U), "ld": ([128, 24], U), "lr": ([128, 48], U),
+    "give": ([128, 384], H), "have": ([128, 384], H), "g32": ([128, 384], F), "val": ([128, 384], F), "rec": ([128, 384], F),
     "ys": ([128, 768], F), "yin": ([128, 192], F), "yub": ([128, 48], F), "lim3": ([128, 768], B),
 }
 for _t in range(RO):
-    SB.update({"sn%d" % _t: ([128, 768], H), "lim%d" % _t: ([128, 768], B), "ms%d" % _t: ([128, 768], B),
-               "mi%d" % _t: ([128, 192], B), "lo%d" % _t: ([128, 192], B), "offl%d" % _t: ([128, 192], U)})
-    if _t:
-        SB.update({"sin%d" % _t: ([128, 192], H), "offi%d" % _t: ([128, 192], U)})
+    SB.update({"lim%d" % _t: ([128, 768], B), "ms%d" % _t: ([128, 976], B), "lo%d" % _t: ([128, 192], B)})
+    if _t < RO - 1:
+        SB.update({"nd%d" % _t: ([128, 384], F), "sin%d" % _t: ([128, 192], F), "osd%d" % _t: ([128, 192], I), "oin%d" % _t: ([128, 192], I)})
 SCRATCH = {_k: ("sbuf", _v[0], _v[1]) for _k, _v in SB.items()}
-SCRATCH.update({"pc": ("psum", [128, 1536], F), "pg2": ("psum", [128, 1024], F),
+SCRATCH.update({"pd": ("psum", [128, 1024], F), "pr": ("psum", [128, 512], F), "pn": ("psum", [128, 512], F), "px": ("psum", [128, 512], F),
                 "p4": ("psum", [128, 32, 2, 16], F), "pm": ("psum", [128, 512], F)})
-BANK0 = {"pc": 0, "pg2": 3, "p4": 5, "pm": 7}
-SEMAPHORES = ["qV", "qA", "qP", "qG"] + ["d%d" % _k for _k in range(60)]
+BANK0 = {"pd": 0, "pr": 2, "pn": 3, "px": 4, "p4": 5, "pm": 7}
+SEMAPHORES = ["qV", "qA", "qP", "qG"] + ["d%d" % _k for _k in range(70)]
 
-CY, GA, SCT, PECY, HOP = 0.83, 1.56, 3.8, 0.42, 100.0
+CY, GA, SCT, PECY, HOP, PASSES, SLACKS = 0.83, 1.56, 3.8, 0.42, 100.0, 3, (0.0, 120.0, 250.0)
 
 
 def _cells(ap):
@@ -51,11 +55,21 @@ def _cells(ap):
     return np.arange(int(np.prod(shape[1:]))).reshape(shape[1:])[idx[1:]].reshape(-1)
 
 
+def spans(runs):
+    out = []
+    for lo, hi in sorted(runs):
+        if out and out[-1][1] == lo:
+            out[-1] = (out[-1][0], hi)
+        else:
+            out.append((lo, hi))
+    return out
+
+
 def build():
     ops = []
     lw, rd, bank, grp = {}, {}, {}, {}
 
-    def add(q, fn, reads, writes, cost, kind="c", acc=None, after=None, lat=0.0):
+    def add(q, fn, reads, writes, cost, kind="c", acc=None, after=None, lat=0.0, ind=False):
         me = len(ops)
         deps = set()
         banks = set()
@@ -110,7 +124,8 @@ def build():
                 for ap in grp[(b, "c")]:
                     lw[ap[0]][_cells(ap)] = me
         deps.discard(me)
-        ops.append({"q": q, "fn": fn, "deps": deps, "cost": cost, "kind": kind, "after": after, "lat": lat})
+        ops.append({"q": q, "fn": fn, "deps": deps, "cost": cost, "kind": kind, "after": after, "lat": lat, "ind": ind,
+                    "nm": (writes + reads)[0][0]})
         return me
 
     def n_of(ap):
@@ -126,7 +141,7 @@ def build():
     def parts(ap):
         return [ap[:2], ap[2]] if len(ap) == 3 else [ap]
 
-    def vec(call, out, ins, mul=None, extra=()):
+    def vec(call, out, ins, mul=None, extra=(), after=None):
         reads = [p for a in ins for p in parts(a)] + [e for e in extra if isinstance(e, tuple)] + parts(out)[1:]
         if len(out) == 3:
             c = 50 + SCT * CY * n_of(ins[0])
@@ -136,14 +151,14 @@ def build():
             if mul is None:
                 mul = 0.5 if all(SCRATCH[a[0]][2] in (B, H, U) for a in [out] + ins) else 1
             c = max(64, mul * n_of(out)) * CY
-        return add("V", call, reads, [out[:2]], c)
+        return add("V", call, reads, [out[:2]], c, after=after, ind=len(out) == 3 or len(ins[0]) == 3)
 
     def v_copy(out, a):
         return vec(lambda g, T: g.vector.tensor_copy(A_(T, out), A_(T, a)), out, [a])
 
-    def v_tt(out, a, b, op):
+    def v_tt(out, a, b, op, after=None):
         return vec(lambda g, T: g.vector.tensor_tensor(A_(T, out), A_(T, a), A_(T, b), op), out, [a, b],
-                   1 if a[0] in BANK0 or b[0] in BANK0 else 2)
+                   1 if a[0] in BANK0 or b[0] in BANK0 else 2, after=after)
 
     def v_ts(out, a, s1, op0, s2=None, op1=None):
         def call(g, T):
@@ -167,8 +182,11 @@ def build():
         def call(g, T):
             if func == AF.Copy:
                 return g.scalar.activation(A_(T, out), A_(T, a), func, scale=A_(T, scale))
-            return g.scalar.activation(A_(T, out), A_(T, a), func, bias=bias, scale=A_(T, scale))
-        return add("A", call, parts(a) + ([scale] if isinstance(scale, tuple) else []), [out], c)
+            return g.scalar.activation(A_(T, out), A_(T, a), func, bias=A_(T, bias), scale=A_(T, scale))
+        return add("A", call, parts(a) + [x for x in (bias, scale) if isinstance(x, tuple)], [out], c, ind=len(a) == 3)
+
+    def step(out, a, bias):
+        return act(out, a, AF.Sigmoid, bias, 256.0)
 
     def mm(out, l, r, start, stop, after=None):
         return add("P", lambda g, T: g.tensor.matmul(A_(T, out), A_(T, l), A_(T, r), start, stop), [l, r], [out],
@@ -191,15 +209,18 @@ def build():
     def dma(q, out, a, lat):
         return add(q, lambda g, T: {"S": g.sync, "A": g.scalar, "G": g}[q].dma_start(A_(T, out), A_(T, a)), [a], [out], 60.0, kind="dma", lat=lat)
 
-    def send(src, c0, dst, d0):
-        srcs = [(src, s_[:, c0 + 64 * b:c0 + 64 * b + 64]) for b in range(3)]
-        dsts = [(dst, s_[:, d0 + 64 * b:d0 + 64 * b + 64]) for b in range(3)]
+    def send(src, c0, dst, d0, back):
+        at = [64 * (2 - b if back else b) for b in range(3)]
+        srcs = [(src, s_[:, c0 + a:c0 + a + 64]) for a in at]
+        dsts = [(dst, s_[:, d0 + a:d0 + a + 64]) for a in at]
         me = add("G", (srcs, dsts), srcs, [], 700.0, kind="send", lat=4500.0)
         ops[me]["arr"] = [add("R", b, [], [dsts[b]], 0.0, kind="arr", after=me) for b in range(3)]
 
     ID = ("wid", s_[:, 16:144])
-    Z4096, Z2048, Z1, ZU, ZO = range(5)
-    B_CV, B_CC, B_2K, B_RV, B_BIG, B_D = range(6)
+    Z4096, Z1, ZK, ZO = 0, 1, 2, 5
+    B_CHK, B_ROB, B_2K, B_4K, B_BIG = range(5)
+    C_W1, C_ROW, C_TH, C_W0, C_FL, C_HI, C_T3, C_DG, C_PAIR, C_BK = range(10)
+    FIT = ("fb", s_[:, 0:4096])
 
     def zq(k, q):
         return ("zz", s_[:, k, 15 - q:143 - q])
@@ -210,73 +231,84 @@ def build():
     def ones(n):
         return ("one", s_[0:1, 0:n])
 
-    def rows(a):
-        return ("zd", s_[:, ROWS.index(a), :])
+    def col(k, p=128):
+        return ("cols", s_[0:p, k:k + 1])
+
+    def blocks(lo, hi):
+        return ("p4", s_[:, lo // 32:hi // 32])
+
+    def back(buf, lo, hi):
+        return (buf, s_[:, 783 - lo:783 - hi:-1])
 
     dma("S", ("si", s_[:]), ("sr", s_[:]), 3000.0)
     dma("A", ("ui", s_[:]), ("u", s_[:]), 2200.0)
     dma("S", ("li", s_[:]), ("lim", s_[:]), 4000.0)
-    dma("S", ("fb", s_[:]), ("fit", s_[:]), 8000.0)
+    dma("S", ("fb", s_[:]), ("fit", s_[:]), 7500.0)
     v_set(("one", s_[:]), 1.0)
     g_iota(("pi", s_[:]), [[-16, 8]], 0, 1)
-    v_set(("zz", s_[:]), 0.0)
-    v_set(("zc", s_[:]), 0.0)
-    v_set(("zr", s_[:]), 0.0)
-    for k, c in enumerate((-47104.0, -14336.0, 2048.0, -30720.0, 67108864.0, 32768.0)):
+    g_iota(("ph", s_[:]), [[1, 8]], 0, 0)
+    v_set(("zz", s_[:, Z1, :]), 0.0)
+    for z in ("zc", "zr", "ck", "r3", "pu"):
+        v_set((z, s_[:]), 0.0)
+    for k, c in enumerate((-45056.0, -28672.0, 2048.0, 4096.0, 67108864.0)):
         v_set(bias(k), c)
-    g_sel(("z8", s_[:]), ("one", s_[0:8, 0:144]), [[1, 144]], AL.is_equal, -15, -16)
     g_sel(("wid", s_[:]), ("one", s_[:, 0:160]), [[1, 160]], AL.is_equal, -16, -1)
-    for a in ROWS:
-        g_sel(rows(a), bias(B_D), [[0, 8], [-1, 16]], AL.is_ge, a - 1, 0)
-    g_iota(("ir", s_[:, 0:768]), [[32, 24], [0, 32]], 0, 0)
-    g_iota(("ir", s_[:, 768:1536]), [[0, 24], [1, 32]], 0, 0)
+    g_sel(("z8", s_[:]), ("one", s_[0:8, 0:144]), [[1, 144]], AL.is_equal, -15, -16)
+    g_sel(("b8w", s_[:]), ("one", s_[0:8, 0:128]), [[1, 8], [0, 16]], AL.is_equal, 0, -1)
+    g_sel(("ev", s_[:]), ("one", s_[0:64, 0:144]), [[1, 144]], AL.is_equal, -16, -2)
+    g_iota(("ir", s_[:, 0, 16:784]), [[-32, 24], [0, 32]], 736, 0)
+    g_iota(("ir", s_[:, 1, 16:784]), [[0, 24], [-1, 32]], 31, 0)
     g_sel(("blk0", s_[:]), ("one", s_[:, 0:128]), [[-16, 8], [0, 16]], AL.is_ge, 0, 1)
     g_sel(("blk", s_[:]), ("blk0", s_[:]), [[16, 8], [0, 16]], AL.is_ge, 15, -1)
-    g_sel(("tri", s_[:]), ("blk", s_[:]), [[1, 128]], AL.is_gt, 0, -1)
+    g_sel(("up", s_[:]), ("blk", s_[:]), [[1, 128]], AL.is_equal, 1, -1)
+    g_sel(("dn", s_[:]), ("blk", s_[:]), [[1, 128]], AL.is_equal, -1, -1)
     v_set(("zr", s_[:, 15:144:16]), 1.0)
+    v_set(("ck", s_[:, 3:128:16]), 997.0)
+    v_set(("ck", s_[:, 5:128:16]), 1994.0)
     v_ts(("pg", s_[:]), ("pi", s_[:]), 4, AL.arith_shift_right)
-    v_ts(("ph", s_[:]), ("pi", s_[:]), 1, AL.arith_shift_right)
     v_ts(("pb", s_[:, 0:1]), ("pi", s_[:, 0:1]), 4, AL.arith_shift_right, 1, AL.bitwise_and)
     v_ts(("pb", s_[:, 1:2]), ("pi", s_[:, 0:1]), 15, AL.bitwise_and)
-    v_ts(("zz", s_[:, Z4096, 15:128:16]), ("pg", s_[:]), 0.0, AL.is_equal, 4096.0, AL.mult)
-    v_ts(("zz", s_[:, Z2048, 15:128:16]), ("pg", s_[:]), 0.0, AL.is_equal, 2048.0, AL.mult)
-    v_copy(("cols", s_[:, 0:2]), ("pb", s_[:, 0:2]))
-    v_ts(("cols", s_[:, 2:3]), ("pb", s_[:, 0:1]), 0.0, AL.is_equal)
+    v_ts(("pb", s_[:, 2:3]), ("pi", s_[:, 0:1]), 7, AL.bitwise_and)
+    v_ts(("pb", s_[:, 3:4]), ("pi", s_[:, 0:1]), 1, AL.arith_shift_right, 7, AL.bitwise_and)
+    v_copy(("cols", s_[:, C_W1:C_ROW + 1]), ("pb", s_[:, 0:2]))
+    v_ts(col(C_W0), ("pb", s_[:, 0:1]), 0.0, AL.is_equal)
+    v_ts(col(C_TH), ("pb", s_[:, 1:2]), -256.0, AL.mult, 128.0, AL.add)
+    v_ts(col(C_FL), ("pb", s_[:, 2:3]), 256.0 * 997, AL.mult, -256.0 * 2047.5, AL.add)
+    v_ts(col(C_HI), ("pb", s_[:, 2:3]), 997.0, AL.mult)
+    v_ts(col(C_T3), ("pb", s_[:, 2:3]), 3.0, AL.is_lt)
+    v_ts(col(C_DG), ("pb", s_[:, 1:2]), 0.0, AL.is_equal, -2.0, AL.add)
+    v_copy(col(C_PAIR), ("pb", s_[:, 3:4]))
+    v_ts(("cols", s_[:, C_BK:C_BK + 8]), ("ph", s_[:]), col(C_PAIR), AL.is_equal)
     v_ts(("zz", s_[:, Z1, 15:128:16]), ("pg", s_[:]), 0.0, AL.is_equal)
-    v_ts(("b8", s_[:]), ("pg", s_[:]), 0.0, AL.is_equal)
-    for k in range(4):
-        v_ts(("zz", s_[:, ZU + k, 15:128:16]), ("ph", s_[:]), float(k), AL.is_equal)
-    v_tt(("z8d", s_[:]), ("z8", s_[:, 15:143]), ("z8", s_[:, 14:142]), AL.subtract)
-    v_ts(("u16", s_[:]), ("ui", s_[:]), -2048.0, AL.add)
-    act(("w0", s_[:]), ("wid", s_[:]), AF.Copy, scale=("cols", s_[:, 2:3]))
-    act(("w1", s_[:]), ("wid", s_[:]), AF.Copy, scale=("cols", s_[:, 0:1]))
+    act(("zz", s_[:, Z4096, :]), ("zz", s_[:, Z1, :]), AF.Copy, scale=4096.0)
+    act(("b8", s_[:]), ("zz", s_[:, Z1, 15:128:16]), AF.Copy)
+    for k in range(6):
+        act(("zz", s_[:, ZK + k, :]), ("zz", s_[:, Z1, :]), AF.Copy, scale=col(C_BK + k))
+    U16 = ("u16", s_[:, 16:784])
+    v_ts(U16, ("ui", s_[:]), -2048.0, AL.add)
+    act(("w0", s_[:]), ("wid", s_[:]), AF.Copy, scale=col(C_W0))
+    act(("w1", s_[:]), ("wid", s_[:]), AF.Copy, scale=col(C_W1))
     act(("nid", s_[:]), ID, AF.Copy, scale=-1.0)
-    act(("bigi", s_[:]), ID, AF.Copy, scale=-32768.0)
-    group([(("pm", s_[:, 0:48]), ("z8", s_[:, 15 - q:143 - q]), ("u16", s_[:, q:768:16])) for q in range(16)])
-    for lo, hi in ((0, 512), (512, 768)):
-        mm(("pg2", s_[0:8, lo:hi]), ("wid", s_[0:8, 16:24]), ("u16", s_[:, lo:hi]), True, True)
-    act(("hi8", s_[:]), ("pg2", s_[0:8, 0:768]), AF.Copy)
-    v_ts(("sn0", s_[:]), ("si", s_[:]), -2048.0, AL.add)
-    v_tr(("t0", s_[:]), ("sn0", s_[:]))
+    for t in range(RO):
+        act(("r3", s_[:, t:64:8]), ("wid", s_[0:8, 16:24]), AF.Copy)
+        act(("pu", s_[:, 2 * t + 1:128:16]), ("wid", s_[0:8, 16:24]), AF.Copy)
+    act(("n4k", s_[:]), ("wid", s_[0:64, 16:80]), AF.Copy, scale=-4096.0)
 
-    def keys(out, tmp, n, t, src):
-        v_ts((tmp, s_[:, 0:n]), src, 2048.0 + 997 * t, AL.add)
-        v_ts((out, s_[:, 0:n]), (tmp, s_[:, 0:n]), 4095, AL.bitwise_and)
-    keys("vc", "vi", 48, 0, ("pm", s_[:, 0:48]))
-    v_copy(("lim0", s_[:]), ("li", s_[:]))
+    HALVES = ((0, 512), (512, 768))
+    for lo, hi in HALVES:
+        mm(("pd", s_[0:64, lo:hi]), ("r3", s_[:]), back("u16", lo, hi), True, True)
+    step(("flag", s_[:]), ("pd", s_[0:64, 0:768]), col(C_FL, 64))
+    for lo, hi in HALVES:
+        o = ("pd", s_[0:64, lo:hi])
+        group([(o, ("r3", s_[:]), back("u16", lo, hi)), (o, ("n4k", s_[:]), ("flag", s_[:, lo:hi]))])
+    act(("hi", s_[:]), ("pd", s_[0:64, 0:768]), AF.Identity, bias=col(C_HI, 64))
 
-    def own_number(t, lo, hi):
-        o = ("pg2", s_[:, lo:hi])
-        return [(o, ("zr", s_[:, 13 - 2 * t:141 - 2 * t]), ("ir", s_[:, lo:hi])),
-                (o, ("zr", s_[:, 12 - 2 * t:140 - 2 * t]), ("ir", s_[:, 768 + lo:768 + hi]))]
-    hold = [None]
-
-    def offsets(runs, p0, v, pr, first, staged):
+    def t_stage(runs, v):
         nb = sum(hi - lo for lo, hi in runs)
-        for k0 in range(p0 // 16, (p0 + nb + 15) // 16):
-            a0, a1 = max(p0, 16 * k0), min(p0 + nb, 16 * k0 + 16)
+        for k0 in range((nb + 15) // 16):
+            a0, a1 = 16 * k0, min(nb, 16 * k0 + 16)
             items = [(("p4", s_[:, a0:a1]), bias(B_2K), ones(32 * (a1 - a0)))]
-            at = p0
+            at = 0
             for lo, hi in runs:
                 x0, x1 = max(at, a0), min(at + hi - lo, a1)
                 for b in range(2):
@@ -286,287 +318,352 @@ def build():
                             items.append((("p4", s_[:, x0:x1, b, :]), ("w%d" % b, s_[:, c0:c0 + 128]),
                                           ("t0", s_[:, lo + x0 - at:lo + x1 - at, x, :])))
                 at += hi - lo
-            group(items, len(ops) - 1 if k0 > p0 // 16 else None)
-        nm = 2 * nb
-        hold[0] = len(ops) - 1
-        for i0, i1 in ((0, ST1), (ST1, 16)) if staged else ((0, 16),):
-            for i in range(i0, i1):
-                v_tt((pr, s_[:, i, 0:nm]), ("p4", s_[:, p0:p0 + nb, :, i]), v, AL.mult)
-            v_ts((pr, s_[:, i0:i1, 0:nm]), (pr, s_[:, i0:i1, 0:nm]), 5, AL.arith_shift_right, 4095, AL.bitwise_and)
-            for buf, r, m0 in first:
-                dst = (buf, s_[:, 12 * i0:12 * i1]) if r is None else (buf, s_[:, r, 12 * i0:12 * i1])
-                v_copy(dst, (pr, s_[:, i0:i1, m0:m0 + 12]))
+            group(items)
+        for i in range(16):
+            v_tt(("pq", s_[:, i, 0:2 * nb]), ("p4", s_[:, 0:nb, :, i]), (v, s_[:, 0:2 * nb]), AL.mult)
 
-    def leaving(offl, pr, m0):
-        for b in range(3):
-            v_copy((offl, s_[:, 64 * b:64 * b + 64]), (pr, s_[:, :, m0 + 4 * b:m0 + 4 * b + 4]))
+    def cut(out, a):
+        v_ts(out, a, 5, AL.arith_shift_right, 4095, AL.bitwise_and)
 
-    FIT = ("fb", s_[:, 0:4096])
+    def t_offsets(out, m0, m1):
+        a = ("pq", s_[:, :, m0:m1])
+        cut(a, a)
+        v_copy(out, a)
 
-    def stream(parts_):
-        gath, segl, at = [], [], 0
-        for buf, c0, cuts, ss in parts_:
-            for a, b in zip(cuts[:-1], cuts[1:]):
-                lo, hi = c0 + a // 16, c0 + b // 16
-                gath.append((at + a, at + b, (buf, s_[:, lo:hi]) if isinstance(buf, str) else (buf[0], s_[:, buf[1], lo:hi])))
-            for w, i, c in ss:
-                segl.append((at, at + w, i, c))
-                at += w
-        cuts = list(range(0, at, 512)) + [at]
-        return gath, segl, list(zip(cuts[:-1], cuts[1:]))
+    def n_offsets(out, s, v, lo, hi):
+        c = s_[:, lo:hi]
+        v_tt(("pw", c), (s, c), v, AL.mult)
+        cut(("pw", c), ("pw", c))
+        v_copy((out, c), ("pw", c))
 
-    def cut(segl, a, b):
-        return [(max(a, p), min(b, q), i, c + max(a, p) - p) for p, q, i, c in segl if p < b and q > a]
+    ring, unit, held, tail = [0], [0], [], [None]
 
-    def scalar_path(st, lim, count):
-        gath, segl, units = st
-        gi = [0]
+    def line(k):
+        ops[k]["after"] = tail[0]
+        tail[0] = k
 
-        def upto(x):
-            while gi[0] < len(gath) and gath[gi[0]][0] < x:
-                a, b, off = gath[gi[0]]
-                act(("fc", s_[:, a:b]), FIT + (off,), AF.Copy)
-                gi[0] += 1
+    def flush(most=99):
+        for _ in range(min(most, len(held))):
+            line(held.pop(0))
 
-        def sub(u):
-            a, b = units[u]
-            base = 512 * (u % 2) - a
-            group([(("pg2", s_[:, base + a:base + b]), ID, ("fc", s_[:, a:b]))] +
-                  [(("pg2", s_[:, base + p:base + q]), ("nid", s_[:]), (lim, s_[:, c:c + q - p])) for p, q, i, c in cut(segl, a, b)])
-        upto(units[0][1])
-        sub(0)
-        for u, (a, b) in enumerate(units):
-            if u + 1 < len(units):
-                upto(units[min(u + 2, len(units) - 1)][1])
-                sub(u + 1)
-            act(("cmpc", s_[:, a:b]), ("pg2", s_[:, 512 * (u % 2):512 * (u % 2) + b - a]), AF.Sign, bias=-0.5)
-            for p, q, i, c in cut(segl, a, b):
-                count(p, q, i, c)
+    def scalar_run(off, lo, hi, lim, out, first, ahead=True):
+        n = hi - lo
+        at = ring[0]
+        ring[0] += 16 * n
+        if not ahead:
+            flush()
+        for a in range(lo, hi, 64):
+            b = min(hi, a + 64)
+            line(act(("fc", s_[:, at + 16 * (a - lo):at + 16 * (b - lo)]), FIT + ((off, s_[:, a:b]),), AF.Copy))
+            flush(2 if b < hi else 99)
+        for k, (l, r) in enumerate(first):
+            mm(out, l, r, k == 0, False)
+        per = 8 if n <= 64 else 4
+        for i0 in range(0, 16, per):
+            base = 512 * (unit[0] % 2)
+            unit[0] += 1
+            for j in range(per):
+                o = ("pd", s_[:, base + n * j:base + n * j + n])
+                group([(o, ID, ("fc", s_[:, at + i0 + j:at + 16 * n:16])), (o, ("nid", s_[:]), (lim, s_[:, lo:hi]))])
+            held.append(step(("cc", s_[:, at + n * i0:at + n * (i0 + per)]), ("pd", s_[:, base:base + n * per]), -128.0))
+            for i in range(i0, i0 + per):
+                mm(out, zq(Z4096, i), ("cc", s_[:, at + n * i:at + n * i + n]), False, i == 15)
 
-    def head(buf, c, n1):
-        out = []
-        for a, b in ((0, min(n1, ST1)), (ST1, n1)):
-            if b > a:
-                n = (b - a) * 192
-                out.append((buf, a * 12, list(range(0, max(n - 399, 1), 1024 if a else 576)) + [n], [(192, i, c) for i in range(a, b)]))
-        return out
+    chain = [None]
 
-    def grouped(todo):
-        def go(o, l, r, b):
-            todo[b] -= 1
-            mm(o, l, r, False, todo[b] == 0)
-        return go
+    def vector_run(off, m0, cmp, c0, lim, out, first):
+        n = n_of(lim)
+        for k, (l, r) in enumerate(first):
+            mm(out, l, r, k == 0, False)
+        for i in range(16):
+            c = (cmp, s_[:, i, c0:c0 + n])
+            chain[0] = v_tt(c, FIT + ((off, s_[:, i, m0:m0 + n // 16]),), lim, AL.is_gt, chain[0])
+            mm(out, zq(Z4096, i), c, False, i == 15)
 
-    offsets([(0, 24)], 0, ("vc", s_[:]), "pr", [("offc", None, 0)], True)
-    v_copy(("offv", s_[:]), ("pr", s_[:, :, 12:36]))
-    leaving("offl0", "pr", 36)
-    for lo, hi in ((0, 512), (512, 768)):
-        o = ("pg2", s_[:, lo:hi])
-        group([(o, ("z8", s_[:, 14:142]), ("u16", s_[:, lo:hi])), (o, ("z8d", s_[:]), ("hi8", s_[:, lo:hi]))] + own_number(0, lo, hi), hold[0])
-    act(("meta0", s_[:]), ("pg2", s_[:, 0:768]), AF.Copy)
+    nini = [0]
 
+    def post(r0, r1, src, onv):
+        pieces = [(a, b) for a, b in ((r0, min(r1, 384)), (max(r0, 384), r1)) if a < b]
+        for a, b in pieces:
+            o = blocks(a + 128 * (a >= 384), b + 128 * (a >= 384))
+            mm(o, ("blk", s_[:]), src(a, b), True, True)
+            if onv:
+                v_ts(("th", s_[:, a:b]), o, col(C_ROW), AL.is_ge)
+            else:
+                step(("th", s_[:, a:b]), o, col(C_TH))
+        c = s_[:, r0:r1]
+        v_scan(("cum", c), ("th", c), ("ini", s_[:, nini[0] % 8:nini[0] % 8 + 1]) if r0 else 0.0)
+        if r1 < 768:
+            nini[0] += 1
+            v_copy(("ini", s_[:, nini[0] % 8:nini[0] % 8 + 1]), ("cum", s_[:, r1 - 1:r1]))
+        else:
+            mm(("pn", s_[:, 500:501]), ("d1", s_[:]), ("cum", s_[:, 767:768]), True, True)
+            v_ts(("zc", s_[:, 15:128:16]), ("b8", s_[:]), ("pn", s_[:, 500:501]), AL.mult)
+        for a, b in pieces:
+            o = blocks(a + 128 * (a >= 384), b + 128 * (a >= 384))
+            mm(o, ("d2", s_[:]), ("cum", s_[:, a:b]), True, True)
+            v_tt(("cm", s_[:, a:b]), o, ("th", s_[:, a:b]), AL.mult)
+
+    def mark(lo, hi, onv):
+        if onv:
+            v_ts(("hol", s_[:, 16 + lo:16 + hi]), ("sw", s_[:, lo:hi]), 4096.0, AL.is_ge)
+        else:
+            step(("hol", s_[:, 16 + lo:16 + hi]), ("sw", s_[:, lo:hi]), -256.0 * 4095.5)
+
+    def holes(lo, hi, p, s, onv):
+        v_tt(("sw", s_[:, lo:hi]), p, s, AL.max)
+        mark(lo, hi, onv)
+
+    def hol_back(a, b):
+        return back("hol", a, b)
+
+    def checks(plan_, lim, s, offsets, donors, onv):
+        for k, runs in enumerate(plan_):
+            pb = "pr" if (len(plan_) - k) % 2 else "px"
+            for lo, hi in runs:
+                offsets(lo, hi)
+                scalar_run("onc", lo, hi, lim, (pb, s_[:, lo:hi]), [(bias(B_CHK), ones(hi - lo))], (lo, hi) != plan_[0][0])
+            if k == 0:
+                donors()
+            lo, hi = min(r[0] for r in runs), max(r[1] for r in runs)
+            holes(lo, hi, (pb, s_[:, lo:hi]), (s, s_[:, lo:hi]), onv[k + 1][0])
+            post(768 - hi, 768 - lo, hol_back, onv[k + 1][1])
+        flush()
+
+    group([(("pn", s_[:, 0:NV0]), ("z8", s_[:, 15 - q:143 - q]), ("u16", s_[:, 16 + VS + q:784:16])) for q in range(16)])
+    act(("vt", s_[:, 0:NV0]), ("pn", s_[:, 0:NV0]), AF.Identity, bias=2048.0)
+    o = ("pm", s_[:, 128:128 + VS])
+    group([(o, bias(B_2K), ones(VS)), (o, ("b8w", s_[:]), ("u16", s_[:, 16:16 + VS]))])
+    v_ts(("sn0", s_[:]), ("si", s_[:, VS:768]), -2048.0, AL.add)
+    v_tr(("t0", s_[:, 0:NV0 // 2]), ("sn0", s_[:]))
+    v_copy(("lim0", s_[:, 0:VS]), ("li", s_[:, 0:VS]))
+    v_copy(("lim0", s_[:, VS:768]), ("li", s_[:, VS:768]))
+    t_stage([(0, NV0 // 2)], "vt")
+    t_offsets(("off0", s_[:]), 0, NV0)
+    act(("bigi", s_[:]), ID, AF.Copy, scale=-32768.0)
+    act(("dia", s_[:]), ID, AF.Copy, scale=col(C_DG))
+    for t in range(RO):
+        act(("bk", s_[:, t, :]), ("blk", s_[:]), AF.Copy, scale=col(C_BK + t))
+    o = ("px", s_[0:64, 0:128])
+    group([(o, ("wid", s_[0:64, 16:80]), ("ev", s_[:, 16:144])), (o, ("nid", s_[0:64, 0:64]), ("ev", s_[:, 15:143]))])
+    o = ("px", s_[0:64, 128:256])
+    mm(o, ("n4k", s_[:]), ("ev", s_[:, 15:143]), True, True)
+    o = ("px", s_[:, 256:384])
+    group([(o, ID, (z, s_[:])) for z in ("up", "dn", "dia")])
+    o = ("px", s_[:, 384:512])
+    group([(o, ID, ID), (o, ("nid", s_[:]), ("up", s_[:]))])
+    act(("phi", s_[:]), ("px", s_[0:64, 0:128]), AF.Copy, scale=col(C_T3, 64))
+    act(("pfl", s_[:]), ("px", s_[0:64, 128:256]), AF.Copy, scale=col(C_T3, 64))
+    act(("d2", s_[:]), ("px", s_[:, 256:384]), AF.Copy)
+    act(("d1", s_[:]), ("px", s_[:, 384:512]), AF.Copy)
+
+    def digits(t):
+        return [("zr", s_[:, 9 - 2 * t - k:137 - 2 * t - k]) for k in range(2)]
+    for (lo, hi), o in zip(HALVES, (blocks(512, 1024), ("px", s_[:, 0:256]))):
+        group([(o, ("pu", s_[:]), back("u16", lo, hi)), (o, ("pfl", s_[:]), ("flag", s_[:, lo:hi])), (o, ("phi", s_[:]), ("hi", s_[:, lo:hi])),
+               (o, ("ck", s_[:]), ones(hi - lo))] + [(o, z, ("ir", s_[:, k, 16 + lo:16 + hi])) for k, z in enumerate(digits(0))])
+        act(("meta0", s_[:, lo:hi]), o, AF.Copy)
+
+    def donors0():
+        vector_run("off0", 0, "cv", 0, ("lim0", s_[:, VS:768]), ("pn", s_[:, 0:768 - VS]), [(bias(B_CHK), ones(768 - VS))])
+        holes(VS, 768, ("pn", s_[:, 0:768 - VS]), ("si", s_[:, VS:768]), ONV0[0][0])
+        post(0, 768 - VS, hol_back, ONV0[0][1])
+    checks(CHK0, "lim0", "si", lambda lo, hi: n_offsets("onc", "si", ("pm", s_[:, 128 + lo:128 + hi]), lo, hi), donors0, ONV0)
+
+    SW = ("sw", s_[:, 0:768])
     for t in range(RO):
         last = t == RO - 1
-        lim, sn, ms, limn = "lim%d" % t, "sn%d" % t, "ms%d" % t, "lim%d" % (t + 1)
-        offi = "offi%d" % t if t else "offl0"
-        NC = NCS[t]
-        st = stream(head("offc", 0, 16) + [(("offv", i), 0, [0, XV], [(XV, i, W1)]) for i in range(NC)] +
-                    [(offi, 64 * b, [0, 1024], [(64, i, 576 + 64 * b) for i in range(16)]) for b in range(3)])
-
-        def split(p, q, c):
-            out = []
-            if c < 512:
-                e = min(q, p + 512 - c)
-                out.append((p, e, c, 0))
-                p, c = e, c + e - p
-            if p < q:
-                out.append((p, q, c, 1) if c < 576 else (p, q, c + 448, 2))
-            return out
-        todo = {0: 17 - NC + (NC > 0), 1: 16 - NC + (NC > 0), 2: 0}
-        for a, b in st[2]:
-            for p, q, i, c in cut(st[1], a, b):
-                for x in split(p, q, c):
-                    todo[x[3]] += 1
-        go = grouped(todo)
-        mm(("pc", s_[:, 0:512]), bias(B_CV), ones(512), True, False)
-        go(("pc", s_[:, 0:W1]), bias(B_D), ones(W1), 0)
-        mm(("pc", s_[:, 512:576]), bias(B_CV), ones(64), True, False)
-        if NC:
-            go(("pc", s_[:, W1:512]), rows(NC), ones(512 - W1), 0)
-            go(("pc", s_[:, 512:576]), rows(NC), ones(64), 1)
-        mm(("pc", s_[:, 1024:1216]), bias(B_CC), ones(192), True, False)
-
-        def count_c(p, q, i, c):
-            for a, b, col, bk in split(p, q, c):
-                go(("pc", s_[:, col:col + b - a]), zq(Z2048, i), ("cmpc", s_[:, a:b]), bk)
-        for i in range(NC, 16):
-            v_tt(("cmpv", s_[:, i, :]), FIT + (("offv", s_[:, i, :]),), (lim, s_[:, W1:576]), AL.is_gt)
-        scalar_path(st, lim, count_c)
-        for i in range(NC, 16):
-            go(("pc", s_[:, W1:512]), zq(Z4096, i), ("cmpv", s_[:, i, 0:512 - W1]), 0)
-            go(("pc", s_[:, 512:576]), zq(Z4096, i), ("cmpv", s_[:, i, 512 - W1:XV]), 1)
-        halves = ((0, 288, 0), (288, 576, 16))
-        for lo, hi, n0 in halves:
-            v_tt(("sw", s_[:, lo:hi]), ("pc", s_[:, lo:hi]), (sn, s_[:, lo:hi]), AL.max)
-        for lo, hi, n0 in halves:
-            v_ts(("hol", s_[:, lo:hi]), ("sw", s_[:, lo:hi]), 2048.0, AL.is_ge)
-            mm(("p4", s_[:, n0:n0 + 9]), ("blk", s_[:]), ("hol", s_[:, lo:hi]), True, True)
-        for lo, hi, n0 in halves:
-            v_ts(("oh", s_[:, lo:hi]), ("p4", s_[:, n0:n0 + 9]), 15.0, AL.min, ("cols", s_[:, 1:2]), AL.is_equal)
-        c = s_[:, 0:576]
-        v_scan(("cum", c), ("oh", c), 0.0)
-        v_tt(("cm", c), ("cum", c), ("oh", c), AL.mult)
-        v_copy(("ini", s_[:, 0:1]), ("cum", s_[:, 575:576]))
-        c = s_[:, 576:768]
-        v_tt(("sw", c), ("pc", s_[:, 1024:1216]), ("sin%d" % t, s_[:]) if t else (sn, c), AL.max)
-        v_ts(("hol", c), ("sw", c), 2048.0, AL.is_ge)
-        mm(("p4", s_[:, 0:6]), ("blk", s_[:]), ("hol", c), True, True)
-        v_ts(("oh", c), ("p4", s_[:, 0:6]), 15.0, AL.min, ("cols", s_[:, 1:2]), AL.is_equal)
-        v_scan(("cum", c), ("oh", c), ("ini", s_[:, 0:1]))
-        mm(("pg2", s_[:, 0:1]), ("tri", s_[:]), ("cum", s_[:, 767:768]), True, True)
-        v_tt(("cm", c), ("cum", c), ("oh", c), AL.mult)
-        v_ts(("zc", s_[:, 15:128:16]), ("b8", s_[:]), ("pg2", s_[:, 0:1]), AL.mult)
-        group([(("pm", s_[:, 0:48]), zq(Z1, q), ("cm", s_[:, q:768:16])) for q in range(16)] +
-              [(("pm", s_[:, 0:48]), ("zc", s_[:, 15 - q:143 - q]), ("oh", s_[:, q:768:16])) for q in range(16)])
-        v_ts(("plc", s_[:]), ("pm", s_[:, 0:48]), -1.0, AL.add)
+        ms, limn = "ms%d" % t, "lim%d" % (t + 1)
+        LW = ("lim%d" % t, s_[:, 0:768])
+        ring[0] = 0
+        X = ("pm", s_[:, 0:48])
+        group([(X, zq(Z1, q), ("cm", s_[:, q:768:16])) for q in range(16)] +
+              [(X, ("zc", s_[:, 15 - q:143 - q]), ("th", s_[:, q:768:16])) for q in range(16)])
+        WIN = (ms, s_[:, 16:784], ("plc", s_[:]))
         if t == 0:
-            v_copy((ms, s_[:, 0:768], ("plc", s_[:])), ("meta0", s_[:]))
-            for k in (1, 2):
-                for lo, hi in ((0, 512), (512, 768)):
-                    group(own_number(k, lo, hi))
-                act(("ai%d" % k, s_[:]), ("pg2", s_[:, 0:768]), AF.Copy)
+            v_ts(("plc", s_[:]), X, -1.0, AL.mult, 767.0, AL.add)
+            v_copy(WIN, ("meta0", s_[:]))
+            for o, src in ((blocks(0, 192), s_[207:15:-1]), (blocks(512, 896), s_[400:784]), (blocks(192, 384), s_[399:207:-1])):
+                group([(o, z, ("ir", s_[:, k, src])) for k, z in enumerate(digits(1))])
+            act(("ai1", s_[:, 0:192]), blocks(0, 192), AF.Copy)
+            act(("ai1", s_[:, 576:768]), blocks(192, 384), AF.Copy)
+            act(("ai1", s_[:, 192:576]), blocks(512, 896), AF.Copy)
+            dma("S", ("ai2", s_[2:128, :]), ("ai1", s_[0:126, :]), 2500.0)
+            dma("S", ("ai2", s_[0:2, :]), ("ai1", s_[0:2, :]), 2500.0)
         else:
-            ai = "ai%d" % t
-            v_tt((ms, s_[:, 0:768], ("plc", s_[:, 0:36])), ("ms%d" % (t - 1), s_[:, 0:576]), (ai, s_[:, 0:576]), AL.add)
-            v_tt((ms, s_[:, 0:768], ("plc", s_[:, 36:48])), ("mi%d" % (t - 1), s_[:]), (ai, s_[:, 576:768]), AL.add)
-        group([(("pm", s_[:, 0:24]), zq(ZO + t, q), (ms, s_[:, 767 - q:383 - q:-16])) for q in range(16)])
-        group([(("pg2", s_[:, 0:48]), zq(ZO + t, q), (ms, s_[:, q:768:16])) for q in range(16)])
-        nu = 24 if last else 48
-        group([(("pg2", s_[:, 512:512 + nu]), zq(ZU, q), (ms, s_[:, q:16 * nu:16])) for q in range(16)])
-        send(ms, 576, "mi%d" % t, 0)
-        SW = ("sw", s_[:, 0:768])
-        LW = (lim, s_[:, 0:768])
-        v_copy(("orv", s_[:]), ("pm", s_[:, 0:24]))
-        v_ts(("give", s_[:]), SW + (("orv", s_[:]),), 2048.0, AL.min)
-        v_copy(("onat", s_[:]), ("pg2", s_[:, 0:48]))
-        v_tr(("t0", s_[:, 0:12]), ("give", s_[:]))
-        keys("vr", "vj", 24, t, ("pg2", s_[:, 512:536]))
-        act((limn, s_[:, 0:384]), LW + (("onat", s_[:, 0:24]),), AF.Copy)
-        act(("lo%d" % t, s_[:]), LW + (("onat", s_[:, 36:48]),), AF.Copy)
-        send("lo%d" % t, 0, limn, 576)
-        act((limn, s_[:, 384:576]), LW + (("onat", s_[:, 24:36]),), AF.Copy)
-        offsets([(0, 12)], 0, ("vr", s_[:]), "pr", [("offd", 0, 0), ("offd", 1, 12)], True)
-        if not last:
-            keys("vc", "vi", 48, t + 1, ("pg2", s_[:, 512:560]))
-            v_ts(("ve", s_[:, 0:12]), ("vi", s_[:, 0:12]), 4095, AL.bitwise_and)
-            v_ts(("ve", s_[:, 12:24]), ("vi", s_[:, 36:48]), 4095, AL.bitwise_and)
-        v_ts(("have", s_[:]), SW + (("onat", s_[:, 0:24]),), 2048.0, AL.min)
-        TP = ("pm", s_[:, 0:384])
-        group([(TP, ID, ("give", s_[:])), (TP, ID, ("have", s_[:]))] + ([(TP, bias(B_2K), ones(384))] if last else []))
-        mm(("pc", s_[:, 1024:1408]), ID, ("have", s_[:]), True, True)
-        a1, a2 = NRS[t]
-        st = stream(head(("offd", 0), 0, a1) + head(("offd", 1), 192, a2))
-        todo = {0: 18 - a1 + (a1 < 16), 1: 18 - a2 + (a2 < 16)}
-        for a, b in st[2]:
-            for p, q, i, c in cut(st[1], a, b):
-                todo[c // 192] += 1
-        go = grouped(todo)
-        for r, a in enumerate((a1, a2)):
-            o = ("pc", s_[:, 512 * r:512 * r + 192])
-            mm(o, bias(B_RV if a < 16 else B_2K), ones(192), True, False)
-            if a < 16:
-                go(o, rows(a), ones(192), r)
-            go(o, ("bigi", s_[:]), ("have", s_[:, 192 * r:192 * r + 192]), r)
-            go(o, bias(B_BIG), ones(192), r)
+            v_ts(("plc", s_[:, 0:36]), ("pm", s_[:, 12:48]), -1.0, AL.mult, 767.0, AL.add)
+            v_ts(("plc", s_[:, 36:48]), ("pm", s_[:, 0:12]), -1.0, AL.mult, 767.0, AL.add)
+            v_tt(WIN, ("ms%d" % (t - 1), s_[:, 208:976]), ("ai%d" % t, s_[:]), AL.add)
+        robv, robs = ROBV[t], ROBS[t]
+        nr = 48 if last else 24
 
-        def count_r(p, q, i, c):
-            col = c + 320 * (c // 192)
-            go(("pc", s_[:, col:col + q - p]), zq(Z2048, i), ("cmpc", s_[:, p:q]), c // 192)
-        scalar_path(st, limn, count_r)
-        new = "ys" if last else "sn%d" % (t + 1)
-        rec = "nrf" if last else new
-        for r in range(2):
-            lo, hi = 192 * r, 192 * r + 192
+        def fwd(q, lo, hi):
+            return (ms, s_[:, 16 + lo + q:16 + hi:16])
+
+        def rev(q, lo, hi):
+            return (ms, s_[:, 783 - lo - q:783 - hi:-16])
+        group([(("pm", s_[:, 48:72]), zq(ZO + t, q), fwd(q, 0, 384)) for q in range(16)])
+        v_copy(("ld", s_[:]), ("pm", s_[:, 48:72]))
+        ld_done = len(ops) - 2
+
+        def keys_n(o, k, lo, hi):
+            group([(o, bias(B_2K), ones(hi - lo)), (o, ("bk", s_[:, k, :]), back(ms, lo, hi))])
+        for lo, hi in robs:
+            keys_n(("pr", s_[:, lo:hi]), t, lo, hi)
+        group([(("px", s_[:, 0:nr]), zq(ZO + t, q), rev(q, 0, 16 * nr)) for q in range(16)], ld_done)
+        lr_done = len(ops) - 1
+        v_copy(("lr", s_[:, 0:nr]), ("px", s_[:, 0:nr]))
+        m = 0 if last else 24
+        if not last:
+            group([(("pn", s_[:, 0:24]), zq(ZK + t + 1, q), fwd(q, 0, 384)) for q in range(16)], lr_done)
+        for lo, hi in robv:
+            group([(("pn", s_[:, m:m + (hi - lo) // 16]), zq(ZK + t, q), rev(q, lo, hi)) for q in range(16)], lr_done)
+            m += (hi - lo) // 16
+        if not last:
+            keys_n(("pm", s_[:, 128:512]), t + 1, 0, 384)
+
+        def pick(out, c0, win, lst, lo, hi):
+            return act((out, s_[:, c0 + lo:c0 + hi]), win + ((lst, s_[:, lo // 16:hi // 16]),), AF.Copy)
+        lo, hi = robs[0]
+        v_copy(("g32", s_[:, lo:hi]), SW + (("ld", s_[:, lo // 16:hi // 16]),))
+        n_offsets("onr", "g32", ("pr", s_[:, lo:hi]), lo, hi)
+        for a, b in spans(robs[1:]):
+            line(pick("g32", 0, SW, "ld", a, b))
+            n_offsets("onr", "g32", ("pr", s_[:, a:b]), a, b)
+        if not last:
+            line(pick("lo%d" % t, 0, LW, "ld", 0, 192))
+            send("lo%d" % t, 0, limn, 384, True)
+        for a, b in spans(robs + robv):
+            line(pick(limn, 0, LW, "lr", a, b))
+        line(act(("vt", s_[:, 0:m]), ("pn", s_[:, 0:m]), AF.Identity, bias=2048.0))
+        v_ts(("give", s_[:]), SW + (("ld", s_[:]),), 4096.0, AL.min, -2048.0, AL.add)
+        v_tr(("t0", s_[:, 0:12]), ("give", s_[:]))
+        for a, b in spans(robv):
+            held.append(pick("g32", 0, SW, "ld", a, b))
+        if last:
+            held.append(pick("lo2", -576, LW, "lr", 576, 768))
+            send("lo2", 0, limn, 576, False)
+            pick(limn, 0, LW, "lr", 384, 576)
+        else:
+            pick(limn, 384, LW, "ld", 192, 384)
+        t_stage(([] if last else [(0, 12)]) + [(lo // 32, hi // 32) for lo, hi in robv], "vt")
+        m0 = 0 if last else 24
+        t_offsets(("offr", s_[:, :, 0:m - m0]), m0, m)
+        if not last:
+            for b in range(3):
+                cut(("osd%d" % t, s_[:, 64 * b:64 * b + 64]), ("pq", s_[:, :, 4 * b:4 * b + 4]))
+            send("osd%d" % t, 0, "oin%d" % t, 0, True)
+            t_offsets(("offd", s_[:, :, 12:24]), 12, 24)
+        send(ms, 16, ms, 784, True)
+        v_ts(("have", s_[:]), SW + (("lr", s_[:, 0:24]),), 4096.0, AL.min, -2048.0, AL.add)
+        group([(blocks(0, 384), bias(B_2K), ones(384)), (blocks(0, 384), ID, ("have", s_[:]))])
+        o = blocks(512, 896)
+        group([(o, bias(B_4K), ones(384)), (o, ID, ("have", s_[:])), (o, ID, ("give", s_[:]))])
+
+        def rob_first(lo, hi):
+            return [(bias(B_ROB), ones(hi - lo)), (bias(B_BIG), ones(hi - lo)), (("bigi", s_[:]), ("have", s_[:, lo:hi]))]
+        rec = "ys" if last else "rec"
+
+        def settle(pb, lo, hi):
             c = s_[:, lo:hi]
-            for i in range(NRS[t][r], 16):
-                v_tt(("cmpv", s_[:, i, lo:hi]), FIT + (("offd", s_[:, r, 12 * i:12 * i + 12]),), (limn, c), AL.is_gt)
-                go(("pc", s_[:, 512 * r:512 * r + 192]), zq(Z4096, i), ("cmpv", s_[:, i, lo:hi]), r)
-            v_tt(("val", c), ("pc", s_[:, 512 * r:512 * r + 192]), ("give", c), AL.max)
-            v_tt((rec, c), ("pc", s_[:, 1024 + lo:1024 + hi]), ("val", c), AL.min)
-            v_tt((new, s_[:, 767 - lo:767 - hi:-1]), ("pm", c), (rec, c), AL.subtract)
-            if r == 0:
-                send(new, 576, "yin" if last else "sin%d" % (t + 1), 0)
-            if last:
-                act(("ys", c), ("nrf", c), AF.Identity, bias=2048.0)
-                if r == 0:
-                    dma("S", ("ysr", c), ("ys", c), 2000.0)
-                    yp = ("p4", s_[:, 16:19, 0, :])
-                    group([(yp, zq(ZU, k), ("ms2", s_[:, 48 * k:48 * k + 48]) if k < 12 else ("mi2", s_[:, 48 * k - 576:48 * k - 528]))
-                           for k in range(16)])
-                    act(("yub", s_[:]), yp, AF.Identity, bias=2048.0)
-                    dma("S", ("yu", s_[:]), ("yub", s_[:]), 2000.0)
-            elif r == 0:
-                v_tr(("t0", s_[:, 0:6]), (new, s_[:, 0:192]))
-                v_tr(("t0", s_[:, 18:24]), (new, s_[:, 576:768]))
-                offsets([(0, 6), (18, 24)], 0, ("ve", s_[:]), "pe", [("offc", None, 0)], False)
-                leaving("offl%d" % (t + 1), "pe", 12)
-                send("offl%d" % (t + 1), 0, "offi%d" % (t + 1), 0)
-            else:
-                v_tr(("t0", s_[:, 6:18]), (new, s_[:, 192:576]))
-                offsets([(6, 18)], 16, ("vc", s_[:, 12:36]), "pr", [], False)
-                v_copy(("offv", s_[:]), ("pr", s_[:, :, 0:24]))
+            v_tt(("val", c), (pb, c), ("g32", c), AL.max)
+            v_tt((rec, c), blocks(lo, hi), ("val", c), AL.min)
+
+        def donors_left(lo, hi):
+            v_tt(("ys", s_[:, 767 - lo:767 - hi:-1]) if last else ("nd%d" % t, s_[:, lo:hi]), blocks(512 + lo, 512 + hi), (rec, s_[:, lo:hi]), AL.subtract)
+        m = 0
+        for k, (lo, hi) in enumerate(robs):
+            pb = ("pn", "pr")[k % 2]
+            scalar_run("onr", lo, hi, limn, (pb, s_[:, lo:hi]), rob_first(lo, hi))
+            settle(pb, lo, hi)
+            if k < len(robv):
+                lo, hi = robv[k]
+                vector_run("offr", m, "cr", 16 * m, (limn, s_[:, lo:hi]), ("px", s_[:, lo:hi]), rob_first(lo, hi))
+                settle("px", lo, hi)
+                m += (hi - lo) // 16
+            if last and k == 0:
+                donors_left(0, 192)
+                send("ys", 576, "yin", 0, False)
+                dma("S", ("ysr", s_[:, 0:192]), ("ys", s_[:, 0:192]), 2000.0)
+        if last:
+            flush()
+            donors_left(192, 384)
+            break
+        donors_left(0, 192)
+        send("nd%d" % t, 0, "sin%d" % t, 0, True)
+        donors_left(192, 384)
+
+        def donors():
+            for b in range(3):
+                v_copy(("offd", s_[:, :, 4 * b:4 * b + 4]), ("oin%d" % t, s_[:, 64 * b:64 * b + 64]))
+            vector_run("offd", 0, "cv", 0, (limn, s_[:, 384:768]), ("pn", s_[:, 0:384]), [(bias(B_CHK), ones(384))])
+            v_tt(("sw", s_[:, 576:768]), ("pn", s_[:, 192:384]), ("nd%d" % t, s_[:, 192:384]), AL.max)
+            v_tt(("sw", s_[:, 384:576]), ("pn", s_[:, 0:192]), ("sin%d" % t, s_[:]), AL.max)
+            mark(384, 768, ONV[0][0])
+            post(0, 384, lambda a, b: ("hol", s_[:, 400 + a:400 + b]), ONV[0][1])
+        checks(CHK, limn, "rec", lambda lo, hi: n_offsets("onc", "rec", ("pm", s_[:, 128 + lo:128 + hi]), lo, hi), donors, ONV)
+    yp = ("pm", s_[:, 0:48])
+    group([(yp, zq(ZK, k), back("ms2", 48 * k, 48 * k + 48) if k < 12 else ("ms2", s_[:, 1551 - 48 * k:1503 - 48 * k:-1])) for k in range(16)])
+    act(("yub", s_[:]), yp, AF.Identity, bias=2048.0)
+    dma("S", ("yu", s_[:]), ("yub", s_[:]), 2000.0)
+    dma("G", ("ylim", s_[:]), ("lim3", s_[:]), 2500.0)
     dma("S", ("ysr", s_[:, 192:576]), ("ys", s_[:, 192:576]), 2000.0)
     dma("A", ("ysr", s_[:, 576:768]), ("yin", s_[:]), 2000.0)
-    dma("G", ("ylim", s_[:]), ("lim3", s_[:]), 2500.0)
     return ops
 
 
 def lay_out(ops):
     n = len(ops)
     pre = [set(o["deps"]) | ({o["after"]} if o["after"] is not None else set()) for o in ops]
+    prev = {}
+    for k, o in enumerate(ops):
+        if o["q"] in "SG":
+            if o["q"] in prev:
+                pre[k].add(prev[o["q"]])
+            prev[o["q"]] = k
     users = [[] for _ in ops]
     for k, p in enumerate(pre):
         for d in p:
             users[d].append(k)
-    left = [len(p) for p in pre]
-    ready = [0.0] * n
-    queues = {}
-    for k, o in enumerate(ops):
-        queues.setdefault(o["q"], []).append(k)
-    head = {q: 0 for q in queues}
-    free = {q: 0.0 for q in queues}
-    level = [0.0] * n
-    nxt = {}
-    for k in range(n - 1, -1, -1):
-        o = ops[k]
-        m = max([level[u] + o["lat"] + HOP for u in users[k]] + [0.0])
-        if o["q"] not in "PR":
-            m = max(m, nxt.get(o["q"], 0.0))
-        level[k] = m + o["cost"]
-        nxt[o["q"]] = level[k]
-    loose = set(k for k in range(n) if ops[k]["q"] in "PR" and left[k] == 0)
-    order = []
-    while len(order) < n:
-        cand = list(loose)
-        for q in queues:
-            if q not in "PR" and head[q] < len(queues[q]) and left[queues[q][head[q]]] == 0:
-                cand.append(queues[q][head[q]])
-        k = min(cand, key=lambda c: (max(ready[c], free[ops[c]["q"]]), -level[c], c))
-        o = ops[k]
-        st = max(ready[k], free[o["q"]])
-        free[o["q"]] = st + o["cost"]
-        if o["q"] in "PR":
+
+    def delay(k, u):
+        if k not in ops[u]["deps"] and ops[u]["kind"] != "arr":
+            return 0.0
+        return ops[k]["lat"] + (0.0 if ops[k]["q"] == ops[u]["q"] == "P" else HOP)
+    ahead = [[(u, delay(k, u)) for u in users[k]] for k in range(n)]
+    behind = [[(d, delay(d, k)) for d in pre[k]] for k in range(n)]
+
+    def place(nxt, deg, key, first, slack):
+        left, ready, start, seq = list(deg), list(first), [0.0] * n, []
+        free = {q: 0.0 for q in "VAPGSR"}
+        loose = set(k for k in range(n) if left[k] == 0)
+        while loose:
+            k = min(loose, key=lambda c: (max(ready[c], free[ops[c]["q"]]), c))
+            q = ops[k]["q"]
+            t = max(ready[k], free[q]) + (slack if q in "VA" else 0.0)
+            k = min((c for c in loose if ops[c]["q"] == q and ready[c] <= t), key=lambda c: (key[c], c))
             loose.discard(k)
-        else:
-            head[o["q"]] += 1
-        order.append(k)
-        for u in users[k]:
-            hop = 0.0 if o["q"] == ops[u]["q"] == "P" else HOP
-            ready[u] = max(ready[u], st + o["cost"] + o["lat"] + hop)
-            left[u] -= 1
-            if left[u] == 0 and ops[u]["q"] in "PR":
-                loose.add(u)
-    return order
+            t, c = max(ready[k], free[q]), ops[k]["cost"]
+            free[q] = t + c
+            start[k] = t
+            seq.append(k)
+            for u, d in nxt[k]:
+                ready[u] = max(ready[u], t + c + d)
+                left[u] -= 1
+                if left[u] == 0:
+                    loose.add(u)
+        return start, seq
+    best = None
+    for slack in SLACKS:
+        key = [-float(k) for k in range(n)]
+        for _ in range(PASSES):
+            st, seq = place(behind, [len(u) for u in users], key, [o["lat"] for o in ops], slack)
+            st, seq = place(ahead, [len(p) for p in pre], [-st[k] - ops[k]["cost"] for k in range(n)], [0.0] * n, slack)
+            end = max(st[k] + ops[k]["cost"] + ops[k]["lat"] for k in range(n))
+            if best is None or end < best[0]:
+                best = (end, seq)
+            key = [-st[k] - ops[k]["cost"] for k in range(n)]
+    return best[1]
 
 
 def plan():

@@ -7,30 +7,52 @@ AF = ActivationFunctionType
 s_ = np.s_
 N = 8
 RO = 3
-VS = 288
-CHK0 = (((160, 288), (64, 160)), ((0, 64),))
-CHK = (((320, 384), (256, 320), (192, 256), (64, 192)), ((0, 64),))
-ROBV = (((0, 192),), ((0, 192),), ((0, 128), (192, 288)))
-ROBS = (((320, 384), (256, 320), (192, 256)),) * 2 + (((128, 192), (288, 384)),)
+VS = 320
+CHK0 = (((256, 320), (192, 256), (128, 192)), ((64, 128),), ((0, 64),))
+LIST0 = ((256, 320), (0, 256))
+CHK = (((192, 256), (320, 384), (256, 320), (128, 192), (64, 128)), ((0, 64),))
+LISTV = ((320, 384), (256, 320), (192, 256), (0, 192))
+LEAD = (2, 0)
+LO2 = 2
+TAIL = (0, 1, 8)
+LASTV = (0,)
+CASES = ((1.0, 1.0, 1.0), (1.0, 1.0, 1.0), (0.75, 1.0, 1.0), (1.25, 1.0, 1.0), (1.0, 1.1, 1.0), (1.0, 1.0, 1.5))
+HOTS, FEED = (0.0, 400.0, 1000.0, 3000.0), ("val", "rec", "ys", "pw", "onc", "osd0", "osd1")
+CALL, FLY = 1000.0, (1500.0, 1200.0)
+GO = ((0, 1), (2,))
+MID = None
+ALLH, ALLN = True, ((128, 192), (0, 128), (192, 384))
+ONG = "d"
+WIDE = 128
+DIRECT = {("si", 0): 16, ("rec", 0): 16}
+EARLY = ("pi", "ph", "cols", "pb", "zz", "bk", "meta0", "cb", "cb2")
+ONVD = (0, 0)
+SCAN0, SCAN = (0, 768), (0, 768)
+AHEAD = False
+HAVE = -1
+ROBV = (((192, 256), (0, 192)),) * 2 + ((),)
+ROBS = (((320, 384), (256, 320)),) * 2 + (((128, 192), (64, 128), (0, 64), (192, 256), (256, 320), (320, 384)),)
 ONV0 = ((0, 0), (1, 1), (1, 1), (1, 1))
-ONV = ((1, 1), (1, 1), (1, 1), (1, 1))
+ONV = ((1, 1), (0, 0), (1, 1), (1, 1))
 NV0 = (768 - VS) // 16
 LC = 9216
 B, H, F, I, U = "bfloat16", "float16", "float32", "int32", "uint16"
 SB = {
     "si": ([128, 768], I), "li": ([128, 768], I), "ui": ([8, 768], I), "fb": ([128, 4096], B),
-    "u16": ([8, 784], H), "flag": ([64, 768], B), "hi": ([64, 768], B), "one": ([128, 512], B), "cb": ([1, 640], B), "ck": ([1, 128], H),
+    "u16": ([8, 784], H), "flag": ([64, 768], B), "hi": ([64, 768], B), "one": ([128, 512], B), "cb": ([1, 512], B), "cb2": ([2, 128], B), "vi": ([128, 48], I), "ck": ([1, 128], H),
     "wid": ([128, 160], B), "w0": ([128, 160], B), "w1": ([128, 160], B), "nid": ([128, 128], B), "bigi": ([128, 128], B),
     "blk0": ([128, 128], B), "blk": ([128, 128], B), "up": ([128, 128], B), "dn": ([128, 128], B), "dia": ([128, 128], B),
     "d1": ([128, 128], B), "d2": ([128, 128], B), "bk": ([128, 3, 128], B),
-    "zz": ([128, 8, 144], B), "zc": ([128, 144], H), "z8": ([8, 144], B), "b8w": ([8, 128], B), "zr": ([1, 144], B), "ir": ([1, 2, 784], B),
+    "zz": ([128, 9, 144], B), "zc": ([128, 144], H), "z8": ([8, 144], B), "b8w": ([8, 128], B), "zr": ([1, 144], B), "ir": ([1, 2, 784], B),
     "r3": ([8, 64], B), "pu": ([8, 128], B), "ev": ([64, 144], B), "phi": ([64, 128], B), "pfl": ([64, 128], B),
     "n4k": ([64, 64], B),
-    "pi": ([128, 8], I), "pg": ([128, 8], I), "ph": ([128, 8], I), "pb": ([128, 8], I), "cols": ([128, 20], F), "b8": ([128, 8], F),
+    "pi": ([128, 8], I), "pg": ([128, 8], I), "ph": ([128, 8], I), "pb": ([128, 8], I), "cols": ([128, 32], F), "b8": ([128, 8], F),
     "ai1": ([128, 768], B), "ai2": ([128, 768], B), "meta0": ([128, 768], B),
     "sn0": ([128, 768 - VS], H), "t0": ([128, 16, 2, 16], H), "pq": ([128, 16, 48], I), "vt": ([128, 48], F), "pw": ([128, 384], I),
-    "off0": ([128, 16, NV0], U), "offr": ([128, 16, 16], U), "offd": ([128, 16, 24], U), "onr": ([128, 384], U), "onc": ([128, 384], U),
-    "cv": ([128, 16, 768 - VS], B), "cr": ([128, 16, 256], B), "fc": ([128, LC], B), "cc": ([128, LC], B),
+    "off0": ([128, 768 - VS], U), "offr": ([128, 384], U), "offd": ([128, 192], U), "offa": ([128, 192], U), "offb": ([128, 16, 12], U),
+    "onr": ([128, 384], U), "onc": ([128, 384], U),
+    "rep0": ([128, 2 * (768 - VS)], B), "repr": ([128, 1536], B), "repd": ([128, 384], B), "repa": ([128, 384], B),
+    "cv": ([128, 16 * (768 - VS)], B), "cr": ([128, 16 * 384], B), "fc": ([128, LC], B), "cc": ([128, LC], B),
     "sw": ([128, 768], F), "hol": ([128, 784], B), "th": ([128, 768], B), "cum": ([128, 768], H), "cm": ([128, 768], H),
     "ini": ([128, 8], F), "plc": ([128, 48], U), "ld": ([128, 24], U), "lr": ([128, 48], U),
     "give": ([128, 384], H), "have": ([128, 384], H), "g32": ([128, 384], F), "val": ([128, 384], F), "rec": ([128, 384], F),
@@ -44,15 +66,19 @@ SCRATCH = {_k: ("sbuf", _v[0], _v[1]) for _k, _v in SB.items()}
 SCRATCH.update({"pd": ("psum", [128, 1024], F), "pr": ("psum", [128, 512], F), "pn": ("psum", [128, 512], F), "px": ("psum", [128, 512], F),
                 "p4": ("psum", [128, 32, 2, 16], F), "pm": ("psum", [128, 512], F)})
 BANK0 = {"pd": 0, "pr": 2, "pn": 3, "px": 4, "p4": 5, "pm": 7}
-SEMAPHORES = ["qV", "qA", "qP", "qG"] + ["d%d" % _k for _k in range(70)]
+SEMAPHORES = ["qV", "qA", "qP", "qG"] + ["d%d" % _k for _k in range(90)]
 
-CY, GA, SCT, PECY, HOP, PASSES, SLACKS = 0.83, 1.56, 3.8, 0.42, 100.0, 3, (0.0, 120.0, 250.0)
+CY, GA, SCT, PECY, HOP, PASSES, SLACKS = 0.83, 1.56, 3.8, 0.5, 100.0, 3, (0.0, 120.0, 250.0)
 
 
 def _cells(ap):
     shape = SCRATCH[ap[0]][1]
     idx = ap[1] if isinstance(ap[1], tuple) else (ap[1],)
     return np.arange(int(np.prod(shape[1:]))).reshape(shape[1:])[idx[1:]].reshape(-1)
+
+
+def copies(lo, hi):
+    return 8 if hi - lo <= 32 else 4 if hi - lo <= WIDE else 2
 
 
 def spans(runs):
@@ -209,17 +235,21 @@ def build():
     def dma(q, out, a, lat):
         return add(q, lambda g, T: {"S": g.sync, "A": g.scalar, "G": g}[q].dma_start(A_(T, out), A_(T, a)), [a], [out], 60.0, kind="dma", lat=lat)
 
-    def send(src, c0, dst, d0, back):
-        at = [64 * (2 - b if back else b) for b in range(3)]
+    sent = [None]
+
+    def send(src, c0, dst, d0, back, only=None, after=None):
+        bs = only or (0, 1, 2)
+        at = [64 * (2 - b if back else b) for b in bs]
         srcs = [(src, s_[:, c0 + a:c0 + a + 64]) for a in at]
         dsts = [(dst, s_[:, d0 + a:d0 + a + 64]) for a in at]
-        me = add("G", (srcs, dsts), srcs, [], 700.0, kind="send", lat=4500.0)
-        ops[me]["arr"] = [add("R", b, [], [dsts[b]], 0.0, kind="arr", after=me) for b in range(3)]
+        sent[0] = me = add("G", (srcs, dsts, bs), srcs, [], CALL, kind="send", lat=FLY[0] + FLY[1] * len(bs), after=after)
+        ops[me]["arr"] = [add("R", (bs, k), [], [dsts[k]], 0.0, kind="arr", after=me) for k in range(len(bs))]
 
     ID = ("wid", s_[:, 16:144])
-    Z4096, Z1, ZK, ZO = 0, 1, 2, 5
-    B_CHK, B_ROB, B_2K, B_4K, B_BIG = range(5)
-    C_W1, C_ROW, C_TH, C_W0, C_FL, C_HI, C_T3, C_DG, C_PAIR, C_BK = range(10)
+    Z4096, Z1, ZY, ZD, ZR = 0, 1, 2, 3, 6
+    B_CHK, B_T, B_2K, B_4K = range(4)
+    C_W1, C_ROW, C_TH, C_W0, C_FL, C_HI, C_T3, C_DG, C_PAIR, C_E, C_K, C_KS, C_D, C_R = 0, 1, 2, 3, 4, 5, 6, 7, 8, 9, 17, 20, 23, 26
+    FINE = 16384.0
     FIT = ("fb", s_[:, 0:4096])
 
     def zq(k, q):
@@ -250,8 +280,11 @@ def build():
     v_set(("zz", s_[:, Z1, :]), 0.0)
     for z in ("zc", "zr", "ck", "r3", "pu"):
         v_set((z, s_[:]), 0.0)
-    for k, c in enumerate((-45056.0, -28672.0, 2048.0, 4096.0, 67108864.0)):
+    for k, c in enumerate((-45056.0, 2048.0 * FINE, 2048.0, 4096.0)):
         v_set(bias(k), c)
+    v_set(("cb2", s_[:]), 67108864.0)
+    v_set(("cb2", s_[0:1, :]), -28672.0)
+    v_set(("ck", s_[:, 12:128:16]), 2048.0)
     g_sel(("wid", s_[:]), ("one", s_[:, 0:160]), [[1, 160]], AL.is_equal, -16, -1)
     g_sel(("z8", s_[:]), ("one", s_[0:8, 0:144]), [[1, 144]], AL.is_equal, -15, -16)
     g_sel(("b8w", s_[:]), ("one", s_[0:8, 0:128]), [[1, 8], [0, 16]], AL.is_equal, 0, -1)
@@ -270,20 +303,28 @@ def build():
     v_ts(("pb", s_[:, 1:2]), ("pi", s_[:, 0:1]), 15, AL.bitwise_and)
     v_ts(("pb", s_[:, 2:3]), ("pi", s_[:, 0:1]), 7, AL.bitwise_and)
     v_ts(("pb", s_[:, 3:4]), ("pi", s_[:, 0:1]), 1, AL.arith_shift_right, 7, AL.bitwise_and)
-    v_copy(("cols", s_[:, C_W1:C_ROW + 1]), ("pb", s_[:, 0:2]))
-    v_ts(col(C_W0), ("pb", s_[:, 0:1]), 0.0, AL.is_equal)
+    v_copy(col(C_ROW), ("pb", s_[:, 1:2]))
+    v_ts(col(C_W1), ("pb", s_[:, 0:1]), FINE, AL.mult)
+    v_ts(col(C_W0), ("pb", s_[:, 0:1]), 0.0, AL.is_equal, FINE, AL.mult)
     v_ts(col(C_TH), ("pb", s_[:, 1:2]), -256.0, AL.mult, 128.0, AL.add)
     v_ts(col(C_FL), ("pb", s_[:, 2:3]), 256.0 * 997, AL.mult, -256.0 * 2047.5, AL.add)
     v_ts(col(C_HI), ("pb", s_[:, 2:3]), 997.0, AL.mult)
     v_ts(col(C_T3), ("pb", s_[:, 2:3]), 3.0, AL.is_lt)
     v_ts(col(C_DG), ("pb", s_[:, 1:2]), 0.0, AL.is_equal, -2.0, AL.add)
     v_copy(col(C_PAIR), ("pb", s_[:, 3:4]))
-    v_ts(("cols", s_[:, C_BK:C_BK + 8]), ("ph", s_[:]), col(C_PAIR), AL.is_equal)
+
+    def cols(k, n):
+        return ("cols", s_[:, k:k + n])
+    v_ts(cols(C_E, 8), ("ph", s_[:]), col(C_PAIR), AL.is_equal)
+    v_ts(cols(C_K, 3), cols(C_E, 3), col(C_E + 6), AL.add)
+    v_ts(cols(C_KS, 3), cols(C_E, 3), col(C_E + 6), AL.add, 1 / FINE, AL.mult)
+    v_tt(cols(C_D, 2), cols(C_E + 3, 2), cols(C_KS + 1, 2), AL.add)
+    v_tt(cols(C_R, 3), cols(C_E + 3, 3), cols(C_KS, 3), AL.add)
     v_ts(("zz", s_[:, Z1, 15:128:16]), ("pg", s_[:]), 0.0, AL.is_equal)
     act(("zz", s_[:, Z4096, :]), ("zz", s_[:, Z1, :]), AF.Copy, scale=4096.0)
     act(("b8", s_[:]), ("zz", s_[:, Z1, 15:128:16]), AF.Copy)
-    for k in range(6):
-        act(("zz", s_[:, ZK + k, :]), ("zz", s_[:, Z1, :]), AF.Copy, scale=col(C_BK + k))
+    for k, c in enumerate((C_K, C_D, C_D + 1, C_E + 5, C_R, C_R + 1, C_R + 2)):
+        act(("zz", s_[:, ZY + k, :]), ("zz", s_[:, Z1, :]), AF.Copy, scale=col(c))
     U16 = ("u16", s_[:, 16:784])
     v_ts(U16, ("ui", s_[:]), -2048.0, AL.add)
     act(("w0", s_[:]), ("wid", s_[:]), AF.Copy, scale=col(C_W0))
@@ -307,7 +348,7 @@ def build():
         nb = sum(hi - lo for lo, hi in runs)
         for k0 in range((nb + 15) // 16):
             a0, a1 = 16 * k0, min(nb, 16 * k0 + 16)
-            items = [(("p4", s_[:, a0:a1]), bias(B_2K), ones(32 * (a1 - a0)))]
+            items = [(("p4", s_[:, a0:a1]), bias(B_T), ones(32 * (a1 - a0)))]
             at = 0
             for lo, hi in runs:
                 x0, x1 = max(at, a0), min(at + hi - lo, a1)
@@ -325,16 +366,22 @@ def build():
     def cut(out, a):
         v_ts(out, a, 5, AL.arith_shift_right, 4095, AL.bitwise_and)
 
-    def t_offsets(out, m0, m1):
+    def narrow(out, a, ong):
+        if ong:
+            g_sel(out, a, [[0, n_of(out)]], AL.is_ge, 0, 0)
+        else:
+            v_copy(out, a)
+
+    def t_offsets(out, m0, m1, ong=False):
         a = ("pq", s_[:, :, m0:m1])
         cut(a, a)
-        v_copy(out, a)
+        narrow(out, a, ong)
 
-    def n_offsets(out, s, v, lo, hi):
+    def n_offsets(out, s, v, lo, hi, ong=False):
         c = s_[:, lo:hi]
         v_tt(("pw", c), (s, c), v, AL.mult)
         cut(("pw", c), ("pw", c))
-        v_copy((out, c), ("pw", c))
+        narrow((out, c), ("pw", c), ong)
 
     ring, unit, held, tail = [0], [0], [], [None]
 
@@ -342,11 +389,17 @@ def build():
         ops[k]["after"] = tail[0]
         tail[0] = k
 
+    def on_vector(at):
+        return [k for k in range(at, len(ops)) if ops[k]["q"] == "V"]
+
+    def weave(a, b):
+        return [k for pair in zip(a, b) for k in pair] + a[len(b):] + b[len(a):]
+
     def flush(most=99):
         for _ in range(min(most, len(held))):
             line(held.pop(0))
 
-    def scalar_run(off, lo, hi, lim, out, first, ahead=True):
+    def scalar_run(off, lo, hi, lim, out, first, ahead=True, onv=(), spare=False, direct=0, lp=None):
         n = hi - lo
         at = ring[0]
         ring[0] += 16 * n
@@ -359,38 +412,56 @@ def build():
         for k, (l, r) in enumerate(first):
             mm(out, l, r, k == 0, False)
         per = 8 if n <= 64 else 4
-        for i0 in range(0, 16, per):
-            base = 512 * (unit[0] % 2)
-            unit[0] += 1
+        if direct:
+            if lp is None:
+                lp = ("pm", s_[:, 0:n])
+                mm(lp, ID, (lim, s_[:, lo:hi]), True, True)
+            for i in range(16 - direct, 16):
+                v_tt(("cc", s_[:, at + n * i:at + n * i + n]), ("fc", s_[:, at + i:at + 16 * n:16]), lp, AL.is_gt)
+                mm(out, zq(Z4096, i), ("cc", s_[:, at + n * i:at + n * i + n]), False, direct == 16 and i == 15)
+        for i0 in range(0, 16 - direct, per):
+            pb, base = ("pm", 0) if spare and i0 == 0 else ("pd", 512 * (unit[0] % 2))
+            unit[0] += pb == "pd"
             for j in range(per):
-                o = ("pd", s_[:, base + n * j:base + n * j + n])
+                o = (pb, s_[:, base + n * j:base + n * j + n])
                 group([(o, ID, ("fc", s_[:, at + i0 + j:at + 16 * n:16])), (o, ("nid", s_[:]), (lim, s_[:, lo:hi]))])
-            held.append(step(("cc", s_[:, at + n * i0:at + n * (i0 + per)]), ("pd", s_[:, base:base + n * per]), -128.0))
+            o, a = ("cc", s_[:, at + n * i0:at + n * (i0 + per)]), (pb, s_[:, base:base + n * per])
+            if i0 // per in onv:
+                v_ts(o, a, 0.5, AL.is_gt)
+            else:
+                held.append(step(o, a, -128.0))
             for i in range(i0, i0 + per):
-                mm(out, zq(Z4096, i), ("cc", s_[:, at + n * i:at + n * i + n]), False, i == 15)
+                mm(out, zq(Z4096, i), ("cc", s_[:, at + n * i:at + n * i + n]), False, i == 15 - direct)
 
     chain = [None]
 
-    def vector_run(off, m0, cmp, c0, lim, out, first):
-        n = n_of(lim)
-        for k, (l, r) in enumerate(first):
-            mm(out, l, r, k == 0, False)
-        for i in range(16):
-            c = (cmp, s_[:, i, c0:c0 + n])
-            chain[0] = v_tt(c, FIT + ((off, s_[:, i, m0:m0 + n // 16]),), lim, AL.is_gt, chain[0])
-            mm(out, zq(Z4096, i), c, False, i == 15)
+    def vector_run(off, cmp, c0, lim, out, first):
+        n = n_of(out)
+        r, m = n_of(lim) // n, n // 16
+        for k, (l, x) in enumerate(first):
+            mm(out, l, x, k == 0, False)
+        for i0 in range(0, 16, r):
+            o = (off[0], s_[:, off[1] + m * i0:off[1] + m * (i0 + r)])
+            chain[0] = v_tt((cmp, s_[:, c0 + n * i0:c0 + n * (i0 + r)]), FIT + (o,), lim, AL.is_gt, chain[0])
+            for i in range(i0, i0 + r):
+                mm(out, zq(Z4096, i), (cmp, s_[:, c0 + n * i:c0 + n * i + n]), False, i == 15)
 
     nini = [0]
 
-    def post(r0, r1, src, onv):
-        pieces = [(a, b) for a, b in ((r0, min(r1, 384)), (max(r0, 384), r1)) if a < b]
-        for a, b in pieces:
-            o = blocks(a + 128 * (a >= 384), b + 128 * (a >= 384))
+    def banked(r0, r1):
+        cuts = [r0] + [c for c in (384, 704) if r0 < c < r1] + [r1]
+        return [(a, b, ("pn", s_[:, 0:b - a]) if a >= 704 else blocks(a + 128 * (a >= 384), b + 128 * (a >= 384)))
+                for a, b in zip(cuts, cuts[1:])]
+
+    def classes(r0, r1, src, onv):
+        for a, b, o in banked(r0, r1):
             mm(o, ("blk", s_[:]), src(a, b), True, True)
             if onv:
                 v_ts(("th", s_[:, a:b]), o, col(C_ROW), AL.is_ge)
             else:
                 step(("th", s_[:, a:b]), o, col(C_TH))
+
+    def ranks(r0, r1):
         c = s_[:, r0:r1]
         v_scan(("cum", c), ("th", c), ("ini", s_[:, nini[0] % 8:nini[0] % 8 + 1]) if r0 else 0.0)
         if r1 < 768:
@@ -399,8 +470,7 @@ def build():
         else:
             mm(("pn", s_[:, 500:501]), ("d1", s_[:]), ("cum", s_[:, 767:768]), True, True)
             v_ts(("zc", s_[:, 15:128:16]), ("b8", s_[:]), ("pn", s_[:, 500:501]), AL.mult)
-        for a, b in pieces:
-            o = blocks(a + 128 * (a >= 384), b + 128 * (a >= 384))
+        for a, b, o in banked(r0, r1):
             mm(o, ("d2", s_[:]), ("cum", s_[:, a:b]), True, True)
             v_tt(("cm", s_[:, a:b]), o, ("th", s_[:, a:b]), AL.mult)
 
@@ -417,45 +487,56 @@ def build():
     def hol_back(a, b):
         return back("hol", a, b)
 
-    def checks(plan_, lim, s, offsets, donors, onv):
+    def hol_on(a, b):
+        return ("hol", s_[:, 400 + a:400 + b])
+
+    def checks(plan_, lists, lim, s, offsets, donors, onv, scans):
         for k, runs in enumerate(plan_):
             pb = "pr" if (len(plan_) - k) % 2 else "px"
             for lo, hi in runs:
-                offsets(lo, hi)
-                scalar_run("onc", lo, hi, lim, (pb, s_[:, lo:hi]), [(bias(B_CHK), ones(hi - lo))], (lo, hi) != plan_[0][0])
+                for a, b in lists:
+                    if b == hi:
+                        offsets(a, b)
+                scalar_run("onc", lo, hi, lim, (pb, s_[:, lo:hi]), [(bias(B_CHK), ones(hi - lo))], AHEAD or (lo, hi) != plan_[0][0],
+                           (), False, DIRECT.get((s, lo), 0))
             if k == 0:
                 donors()
             lo, hi = min(r[0] for r in runs), max(r[1] for r in runs)
             holes(lo, hi, (pb, s_[:, lo:hi]), (s, s_[:, lo:hi]), onv[k + 1][0])
-            post(768 - hi, 768 - lo, hol_back, onv[k + 1][1])
+            classes(768 - hi, 768 - lo, hol_back, onv[k + 1][1])
+            for a, b in zip(scans, scans[1:]):
+                if 768 - hi < b <= 768 - lo or (k == 0 and b <= 768 - hi):
+                    ranks(a, b)
         flush()
 
     group([(("pn", s_[:, 0:NV0]), ("z8", s_[:, 15 - q:143 - q]), ("u16", s_[:, 16 + VS + q:784:16])) for q in range(16)])
-    act(("vt", s_[:, 0:NV0]), ("pn", s_[:, 0:NV0]), AF.Identity, bias=2048.0)
+    act(("vt", s_[:, 0:NV0]), ("pn", s_[:, 0:NV0]), AF.Identity, bias=2048.0 / FINE, scale=1 / FINE)
     o = ("pm", s_[:, 128:128 + VS])
     group([(o, bias(B_2K), ones(VS)), (o, ("b8w", s_[:]), ("u16", s_[:, 16:16 + VS]))])
     v_ts(("sn0", s_[:]), ("si", s_[:, VS:768]), -2048.0, AL.add)
     v_tr(("t0", s_[:, 0:NV0 // 2]), ("sn0", s_[:]))
     v_copy(("lim0", s_[:, 0:VS]), ("li", s_[:, 0:VS]))
-    v_copy(("lim0", s_[:, VS:768]), ("li", s_[:, VS:768]))
+    v_copy(("rep0", s_[:, 0:768 - VS]), ("li", s_[:, VS:768]))
+    v_copy(("rep0", s_[:, 768 - VS:2 * (768 - VS)]), ("rep0", s_[:, 0:768 - VS]))
+    dma("S", ("lim0", s_[:, VS:768]), ("rep0", s_[:, 0:768 - VS]), 2500.0)
     t_stage([(0, NV0 // 2)], "vt")
     t_offsets(("off0", s_[:]), 0, NV0)
     act(("bigi", s_[:]), ID, AF.Copy, scale=-32768.0)
     act(("dia", s_[:]), ID, AF.Copy, scale=col(C_DG))
     for t in range(RO):
-        act(("bk", s_[:, t, :]), ("blk", s_[:]), AF.Copy, scale=col(C_BK + t))
+        act(("bk", s_[:, t, :]), ("blk", s_[:]), AF.Copy, scale=col(C_K + t))
     o = ("px", s_[0:64, 0:128])
     group([(o, ("wid", s_[0:64, 16:80]), ("ev", s_[:, 16:144])), (o, ("nid", s_[0:64, 0:64]), ("ev", s_[:, 15:143]))])
     o = ("px", s_[0:64, 128:256])
     mm(o, ("n4k", s_[:]), ("ev", s_[:, 15:143]), True, True)
-    o = ("px", s_[:, 256:384])
-    group([(o, ID, (z, s_[:])) for z in ("up", "dn", "dia")])
-    o = ("px", s_[:, 384:512])
-    group([(o, ID, ID), (o, ("nid", s_[:]), ("up", s_[:]))])
     act(("phi", s_[:]), ("px", s_[0:64, 0:128]), AF.Copy, scale=col(C_T3, 64))
     act(("pfl", s_[:]), ("px", s_[0:64, 128:256]), AF.Copy, scale=col(C_T3, 64))
-    act(("d2", s_[:]), ("px", s_[:, 256:384]), AF.Copy)
-    act(("d1", s_[:]), ("px", s_[:, 384:512]), AF.Copy)
+    o = ("pr", s_[:, 256:384])
+    group([(o, ID, (z, s_[:])) for z in ("up", "dn", "dia")])
+    o = ("pr", s_[:, 384:512])
+    group([(o, ID, ID), (o, ("nid", s_[:]), ("up", s_[:]))])
+    act(("d2", s_[:]), ("pr", s_[:, 256:384]), AF.Copy)
+    act(("d1", s_[:]), ("pr", s_[:, 384:512]), AF.Copy)
 
     def digits(t):
         return [("zr", s_[:, 9 - 2 * t - k:137 - 2 * t - k]) for k in range(2)]
@@ -465,10 +546,10 @@ def build():
         act(("meta0", s_[:, lo:hi]), o, AF.Copy)
 
     def donors0():
-        vector_run("off0", 0, "cv", 0, ("lim0", s_[:, VS:768]), ("pn", s_[:, 0:768 - VS]), [(bias(B_CHK), ones(768 - VS))])
+        vector_run(("off0", 0), "cv", 0, ("rep0", s_[:]), ("pn", s_[:, 0:768 - VS]), [(bias(B_CHK), ones(768 - VS))])
         holes(VS, 768, ("pn", s_[:, 0:768 - VS]), ("si", s_[:, VS:768]), ONV0[0][0])
-        post(0, 768 - VS, hol_back, ONV0[0][1])
-    checks(CHK0, "lim0", "si", lambda lo, hi: n_offsets("onc", "si", ("pm", s_[:, 128 + lo:128 + hi]), lo, hi), donors0, ONV0)
+        classes(0, 768 - VS, hol_back, ONV0[0][1])
+    checks(CHK0, LIST0, "lim0", "si", lambda lo, hi: n_offsets("onc", "si", ("pm", s_[:, 128 + lo:128 + hi]), lo, hi), donors0, ONV0, SCAN0)
 
     SW = ("sw", s_[:, 0:768])
     for t in range(RO):
@@ -477,8 +558,8 @@ def build():
         LW = ("lim%d" % t, s_[:, 0:768])
         ring[0] = 0
         X = ("pm", s_[:, 0:48])
-        group([(X, zq(Z1, q), ("cm", s_[:, q:768:16])) for q in range(16)] +
-              [(X, ("zc", s_[:, 15 - q:143 - q]), ("th", s_[:, q:768:16])) for q in range(16)])
+        group([(X, ("zc", s_[:, 15 - q:143 - q]), ("th", s_[:, q:768:16])) for q in range(16)] +
+              [(X, zq(Z1, q), ("cm", s_[:, q:768:16])) for q in range(16)])
         WIN = (ms, s_[:, 16:784], ("plc", s_[:]))
         if t == 0:
             v_ts(("plc", s_[:]), X, -1.0, AL.mult, 767.0, AL.add)
@@ -502,66 +583,37 @@ def build():
 
         def rev(q, lo, hi):
             return (ms, s_[:, 783 - lo - q:783 - hi:-16])
-        group([(("pm", s_[:, 48:72]), zq(ZO + t, q), fwd(q, 0, 384)) for q in range(16)])
+        group([(("pm", s_[:, 48:72]), zq(ZD + t, q), fwd(q, 0, 384)) for q in range(16)])
+        ld_done = len(ops) - 1
         v_copy(("ld", s_[:]), ("pm", s_[:, 48:72]))
-        ld_done = len(ops) - 2
+
+        def keys_t(m, p, lo, hi):
+            a, c = (p, s_[:, lo:hi]), s_[:, m:m + hi - lo]
+            v_copy(("vi", c), a)
+            v_tt(("vt", c), a, ("vi", c), AL.subtract)
 
         def keys_n(o, k, lo, hi):
-            group([(o, bias(B_2K), ones(hi - lo)), (o, ("bk", s_[:, k, :]), back(ms, lo, hi))])
-        for lo, hi in robs:
-            keys_n(("pr", s_[:, lo:hi]), t, lo, hi)
-        group([(("px", s_[:, 0:nr]), zq(ZO + t, q), rev(q, 0, 16 * nr)) for q in range(16)], ld_done)
-        lr_done = len(ops) - 1
-        v_copy(("lr", s_[:, 0:nr]), ("px", s_[:, 0:nr]))
+            mm(o, ("bk", s_[:, k, :]), back(ms, lo, hi), True, True)
         m = 0 if last else 24
         if not last:
-            group([(("pn", s_[:, 0:24]), zq(ZK + t + 1, q), fwd(q, 0, 384)) for q in range(16)], lr_done)
-        for lo, hi in robv:
-            group([(("pn", s_[:, m:m + (hi - lo) // 16]), zq(ZK + t, q), rev(q, lo, hi)) for q in range(16)], lr_done)
+            keys_t(0, "pm", 48, 72)
+        for lo, hi in spans(robs):
+            keys_n(("pr", s_[:, lo:hi]), t, lo, hi)
+        group([(("px", s_[:, 0:nr]), zq(ZR + t, q), rev(q, 0, 16 * nr)) for q in range(16)], ld_done)
+        v_copy(("lr", s_[:, 0:nr]), ("px", s_[:, 0:nr]))
+        tcol = {}
+        for lo, hi in spans(robv):
+            keys_t(m, "px", lo // 16, hi // 16)
+            tcol.update({k: m + (k - lo) // 16 for k in range(lo, hi, 16)})
             m += (hi - lo) // 16
         if not last:
             keys_n(("pm", s_[:, 128:512]), t + 1, 0, 384)
 
         def pick(out, c0, win, lst, lo, hi):
             return act((out, s_[:, c0 + lo:c0 + hi]), win + ((lst, s_[:, lo // 16:hi // 16]),), AF.Copy)
-        lo, hi = robs[0]
-        v_copy(("g32", s_[:, lo:hi]), SW + (("ld", s_[:, lo // 16:hi // 16]),))
-        n_offsets("onr", "g32", ("pr", s_[:, lo:hi]), lo, hi)
-        for a, b in spans(robs[1:]):
-            line(pick("g32", 0, SW, "ld", a, b))
-            n_offsets("onr", "g32", ("pr", s_[:, a:b]), a, b)
-        if not last:
-            line(pick("lo%d" % t, 0, LW, "ld", 0, 192))
-            send("lo%d" % t, 0, limn, 384, True)
-        for a, b in spans(robs + robv):
-            line(pick(limn, 0, LW, "lr", a, b))
-        line(act(("vt", s_[:, 0:m]), ("pn", s_[:, 0:m]), AF.Identity, bias=2048.0))
-        v_ts(("give", s_[:]), SW + (("ld", s_[:]),), 4096.0, AL.min, -2048.0, AL.add)
-        v_tr(("t0", s_[:, 0:12]), ("give", s_[:]))
-        for a, b in spans(robv):
-            held.append(pick("g32", 0, SW, "ld", a, b))
-        if last:
-            held.append(pick("lo2", -576, LW, "lr", 576, 768))
-            send("lo2", 0, limn, 576, False)
-            pick(limn, 0, LW, "lr", 384, 576)
-        else:
-            pick(limn, 384, LW, "ld", 192, 384)
-        t_stage(([] if last else [(0, 12)]) + [(lo // 32, hi // 32) for lo, hi in robv], "vt")
-        m0 = 0 if last else 24
-        t_offsets(("offr", s_[:, :, 0:m - m0]), m0, m)
-        if not last:
-            for b in range(3):
-                cut(("osd%d" % t, s_[:, 64 * b:64 * b + 64]), ("pq", s_[:, :, 4 * b:4 * b + 4]))
-            send("osd%d" % t, 0, "oin%d" % t, 0, True)
-            t_offsets(("offd", s_[:, :, 12:24]), 12, 24)
-        send(ms, 16, ms, 784, True)
-        v_ts(("have", s_[:]), SW + (("lr", s_[:, 0:24]),), 4096.0, AL.min, -2048.0, AL.add)
-        group([(blocks(0, 384), bias(B_2K), ones(384)), (blocks(0, 384), ID, ("have", s_[:]))])
-        o = blocks(512, 896)
-        group([(o, bias(B_4K), ones(384)), (o, ID, ("have", s_[:])), (o, ID, ("give", s_[:]))])
 
         def rob_first(lo, hi):
-            return [(bias(B_ROB), ones(hi - lo)), (bias(B_BIG), ones(hi - lo)), (("bigi", s_[:]), ("have", s_[:, lo:hi]))]
+            return [(("cb2", s_[:]), ("one", s_[0:2, 0:hi - lo])), (("bigi", s_[:]), ("have", s_[:, lo:hi]))]
         rec = "ys" if last else "rec"
 
         def settle(pb, lo, hi):
@@ -571,40 +623,198 @@ def build():
 
         def donors_left(lo, hi):
             v_tt(("ys", s_[:, 767 - lo:767 - hi:-1]) if last else ("nd%d" % t, s_[:, lo:hi]), blocks(512 + lo, 512 + hi), (rec, s_[:, lo:hi]), AL.subtract)
-        m = 0
+
+        def serials(out, lst, lo, hi):
+            return v_ts((out, s_[:, lo:hi]), SW + ((lst, s_[:, lo // 16:hi // 16]),), 4096.0, AL.min, -2048.0, AL.add)
+
+        def sums(lo, hi):
+            group([(blocks(lo, hi), bias(B_2K), ones(hi - lo)), (blocks(lo, hi), ID, ("have", s_[:, lo:hi]))])
+            o = blocks(512 + lo, 512 + hi)
+            group([(o, bias(B_4K), ones(hi - lo)), (o, ID, ("have", s_[:, lo:hi])), (o, ID, ("give", s_[:, lo:hi]))])
+        if last and ALLH:
+            send(ms, 16, ms, 784, True)
+
+            def v_pick(out, c0, lo, hi):
+                return v_copy((out, s_[:, c0 + lo:c0 + hi]), LW + (("lr", s_[:, lo // 16:hi // 16]),))
+            at = len(ops)
+            for lo, hi in ALLN:
+                if lo == 0:
+                    line(pick("g32", 0, SW, "ld", lo, hi))
+                else:
+                    v_copy(("g32", s_[:, lo:hi]), SW + (("ld", s_[:, lo // 16:hi // 16]),))
+                n_offsets("onr", "g32", ("pr", s_[:, lo:hi]), lo, hi)
+            first = on_vector(at)[:8]
+            for a, b in zip(first, first[1:]):
+                ops[b]["after"] = a
+            for lo, hi in ((0, 192), (192, 384)):
+                v_pick(limn, 0, lo, hi)
+                mm(("pd", s_[:, lo + 320 * (lo > 0):hi + 320 * (lo > 0)]), ID, (limn, s_[:, lo:hi]), True, True)
+                ops[serials("have", "lr", lo, hi)]["after"] = first[3]
+                ops[serials("give", "ld", lo, hi)]["after"] = first[3]
+            sums(0, 192)
+            v_pick("lo2", -576, 576, 768)
+            send("lo2", 0, limn, 576, False)
+            gone = []
+            for k, (lo, hi) in enumerate(robs):
+                pb = ("pn", "px")[k % 2]
+                at = lo + 320 * (lo >= 192)
+                scalar_run("onr", lo, hi, limn, (pb, s_[:, lo:hi]), rob_first(lo, hi), direct=16, lp=("pd", s_[:, at:at + hi - lo]))
+                settle(pb, lo, hi)
+                donors_left(lo, hi)
+                gone.append((128 - lo) // 64)
+                for bs in GO:
+                    if gone[-1] in bs and all(x in gone for x in bs):
+                        send("ys", 576, "yin", 0, False, bs)
+                if k == 2:
+                    sums(192, 384)
+                    dma("S", ("ysr", s_[:, 0:192]), ("ys", s_[:, 0:192]), 2000.0)
+            line(pick(limn, 0, LW, "lr", 384, 576))
+            break
+        v_ts(("give", s_[:]), SW + (("ld", s_[:]),), 4096.0, AL.min, -2048.0, AL.add)
+        first, later, part = [len(ops) - 1], [], {}
+        v_tr(("t0", s_[:, 0:12]), ("give", s_[:]))
+        first.append(len(ops) - 1)
+        for k, (a, b) in enumerate(spans(robs)):
+            line(pick("g32", 0, SW, "ld", a, b))
+            n_offsets("onr", "g32", ("pr", s_[:, a:b]), a, b)
+            part["n%d" % k] = on_vector(len(ops) - 3)
+            if k == 0:
+                first[LEAD[last]:LEAD[last]] = range(len(ops) - 3, len(ops))
+        if not last:
+            line(pick("lo%d" % t, 0, LW, "ld", 0, 192))
+            send("lo%d" % t, 0, limn, 384, True)
+        for k, (a, b) in enumerate(spans(robs)):
+            (later.append if k else line)(pick(limn, 0, LW, "lr", a, b))
+        for k, (a, b) in enumerate(robv):
+            (held.append if k or last else line)(pick("repr", 3 * a, LW, "lr", a, b))
+            if k == 0:
+                held.append(pick("g32", 0, SW, "ld", a, b))
+            at = len(ops)
+            for w in [(b - a) * r for r in (1, 2, 4) if r < copies(a, b)]:
+                v_copy(("repr", s_[:, 4 * a + w:4 * a + 2 * w]), ("repr", s_[:, 4 * a:4 * a + w]))
+            part["p%d" % k] = on_vector(at)
+            dma("S", (limn, s_[:, a:b]), ("repr", s_[:, 4 * a:3 * a + b]), 2500.0)
+        for a, b in spans(robv[1:]):
+            later.append(pick("g32", 0, SW, "ld", a, b))
+        if last:
+            held.insert(LO2, pick("lo2", -576, LW, "lr", 576, 768))
+            send("lo2", 0, limn, 576, False)
+            later.append(pick(limn, 0, LW, "lr", 384, 576))
+        else:
+            later.append(pick("repd", -192, LW, "ld", 192, 384))
+            dma("S", ("repd", s_[:, 192:384]), ("repd", s_[:, 0:192]), 2500.0)
+            dma("S", (limn, s_[:, 576:768]), ("repd", s_[:, 0:192]), 2500.0)
+            for k in range(2):
+                dma("S", ("repa", s_[:, 192 * k:192 * k + 192]), (limn, s_[:, 384:576]), 2500.0)
+        t_stage(([] if last else [(0, 12)]) + [(lo // 32, hi // 32) for lo, hi in spans(robv)], "vt")
+        first += range(len(ops) - 16, len(ops))
+        for lo, hi in robv:
+            t_offsets(("offr", s_[:, lo:hi]), tcol[lo], tcol[lo] + (hi - lo) // 16)
+            part["t%d" % lo] = on_vector(len(ops) - 2)
+            if lo == robv[0][0]:
+                first += range(len(ops) - 2, len(ops))
+        for a, b in zip(first, first[1:]):
+            ops[b]["after"] = a
+        chain[0] = first[-1]
+        if not last:
+            for b in range(3):
+                cut(("osd%d" % t, s_[:, 64 * b:64 * b + 64]), ("pq", s_[:, :, 4 * b:4 * b + 4]))
+            part["o"] = on_vector(len(ops) - 3)
+            send("osd%d" % t, 0, "oin%d" % t, 0, True)
+            t_offsets(("offd", s_[:]), 12, 24, "d" in ONG)
+        send(ms, 16, ms, 784, True, None, None if last else sent[0])
+        ops[v_ts(("have", s_[:]), SW + (("lr", s_[:, 0:24]),), 4096.0, AL.min, -2048.0, AL.add)]["after"] = first[HAVE]
+        group([(blocks(0, 384), bias(B_2K), ones(384)), (blocks(0, 384), ID, ("have", s_[:]))])
+        o = blocks(512, 896)
+        group([(o, bias(B_4K), ones(384)), (o, ID, ("have", s_[:])), (o, ID, ("give", s_[:]))])
+
+        def rob_first(lo, hi):
+            return [(("cb2", s_[:]), ("one", s_[0:2, 0:hi - lo])), (("bigi", s_[:]), ("have", s_[:, lo:hi]))]
+        rec = "ys" if last else "rec"
+
+        def settle(pb, lo, hi):
+            c = s_[:, lo:hi]
+            v_tt(("val", c), (pb, c), ("g32", c), AL.max)
+            v_tt((rec, c), blocks(lo, hi), ("val", c), AL.min)
+
+        def donors_left(lo, hi):
+            v_tt(("ys", s_[:, 767 - lo:767 - hi:-1]) if last else ("nd%d" % t, s_[:, lo:hi]), blocks(512 + lo, 512 + hi), (rec, s_[:, lo:hi]), AL.subtract)
+
+        gone = []
+
+        def leave(lo, hi):
+            for b in range(3):
+                if last and lo <= 128 - 64 * b < hi:
+                    donors_left(128 - 64 * b, 192 - 64 * b)
+                    gone.append(b)
+                    for bs in GO:
+                        if b in bs and all(x in gone for x in bs):
+                            send("ys", 576, "yin", 0, False, bs)
         for k, (lo, hi) in enumerate(robs):
             pb = ("pn", "pr")[k % 2]
-            scalar_run("onr", lo, hi, limn, (pb, s_[:, lo:hi]), rob_first(lo, hi))
+            if k == 2 and later:
+                held.extend(later)
+                del later[:]
+                flush()
+            at = len(ops)
+            scalar_run("onr", lo, hi, limn, (pb, s_[:, lo:hi]), rob_first(lo, hi), direct=DIRECT.get((t, lo), 0))
+            part["d%d" % k] = on_vector(at)
+            if k == len(robs) - 1 and not last:
+                held[0:0] = later
+            at = len(ops)
             settle(pb, lo, hi)
-            if k < len(robv):
+            leave(lo, hi)
+            part["s%d" % k] = on_vector(at)
+            for k in range(k, len(robv) if k == len(robs) - 1 else min(k + 1, len(robv))):
                 lo, hi = robv[k]
-                vector_run("offr", m, "cr", 16 * m, (limn, s_[:, lo:hi]), ("px", s_[:, lo:hi]), rob_first(lo, hi))
+                at = len(ops)
+                vector_run(("offr", lo), "cr", 16 * lo, ("repr", s_[:, 4 * lo:4 * lo + copies(lo, hi) * (hi - lo)]), ("px", s_[:, lo:hi]), rob_first(lo, hi))
+                part["r%d" % k] = on_vector(at)
+                at = len(ops)
                 settle("px", lo, hi)
-                m += (hi - lo) // 16
-            if last and k == 0:
-                donors_left(0, 192)
-                send("ys", 576, "yin", 0, False)
+                leave(lo, hi)
+                part["v%d" % k] = on_vector(at)
+            if last and k == 1:
                 dma("S", ("ysr", s_[:, 0:192]), ("ys", s_[:, 0:192]), 2000.0)
         if last:
             flush()
             donors_left(192, 384)
+            r1 = part["r1"]
+            seq = part["r0"] + weave(part["n1"], part["v0"]) + r1[:TAIL[0]] + part["s0"] + r1[TAIL[0]:TAIL[1]] + part["s1"] + r1[TAIL[1]:]
+            if part["d1"]:
+                seq = part["r0"] + part["d1"][:TAIL[2]] + weave(part["v0"], part["s0"]) + part["d1"][TAIL[2]:] + weave(part["n1"], part["s1"]) + r1 + part["d2"]
+            for a, b in zip(seq, seq[1:]):
+                ops[b]["after"] = a
             break
         donors_left(0, 192)
         send("nd%d" % t, 0, "sin%d" % t, 0, True)
         donors_left(192, 384)
 
         def donors():
+            vector_run(("offd", 0), "cv", 0, ("repd", s_[:]), ("pn", s_[:, 192:384]), [(bias(B_CHK), ones(192))])
+            holes(576, 768, ("pn", s_[:, 192:384]), ("nd%d" % t, s_[:, 192:384]), ONVD[0])
+            classes(192, 384, hol_on, ONVD[1])
             for b in range(3):
-                v_copy(("offd", s_[:, :, 4 * b:4 * b + 4]), ("oin%d" % t, s_[:, 64 * b:64 * b + 64]))
-            vector_run("offd", 0, "cv", 0, (limn, s_[:, 384:768]), ("pn", s_[:, 0:384]), [(bias(B_CHK), ones(384))])
-            v_tt(("sw", s_[:, 576:768]), ("pn", s_[:, 192:384]), ("nd%d" % t, s_[:, 192:384]), AL.max)
-            v_tt(("sw", s_[:, 384:576]), ("pn", s_[:, 0:192]), ("sin%d" % t, s_[:]), AL.max)
-            mark(384, 768, ONV[0][0])
-            post(0, 384, lambda a, b: ("hol", s_[:, 400 + a:400 + b]), ONV[0][1])
-        checks(CHK, limn, "rec", lambda lo, hi: n_offsets("onc", "rec", ("pm", s_[:, 128 + lo:128 + hi]), lo, hi), donors, ONV)
+                narrow(("offb", s_[:, :, 4 * b:4 * b + 4]), ("oin%d" % t, s_[:, 64 * b:64 * b + 64]), "a" in ONG)
+            narrow(("offa", s_[:]), ("offb", s_[:]), "a" in ONG)
+            vector_run(("offa", 0), "cv", 3072, ("repa", s_[:]), ("pn", s_[:, 0:192]), [(bias(B_CHK), ones(192))])
+            holes(384, 576, ("pn", s_[:, 0:192]), ("sin%d" % t, s_[:]), ONV[0][0])
+            classes(0, 192, hol_on, ONV[0][1])
+
+        def lists(lo, hi):
+            at = len(ops)
+            n_offsets("onc", "rec", ("pm", s_[:, 128 + lo:128 + hi]), lo, hi, "c" in ONG and lo == 0)
+            part["c%d" % lo] = on_vector(at)
+        checks(CHK, LISTV, limn, "rec", lists, donors, ONV, SCAN)
+        if MID:
+            r1 = part["r1"]
+            seq = (part["r0"] + weave(part["p1"] + part["t0"] + part["o"], part["v0"] + part["c192"]) + r1[:MID[0]] + part["s0"] + part["c320"]
+                   + r1[MID[0]:MID[1]] + part["s1"] + part["c256"] + r1[MID[1]:])
+            for a, b in zip(seq, seq[1:]):
+                ops[b]["after"] = a
     yp = ("pm", s_[:, 0:48])
-    group([(yp, zq(ZK, k), back("ms2", 48 * k, 48 * k + 48) if k < 12 else ("ms2", s_[:, 1551 - 48 * k:1503 - 48 * k:-1])) for k in range(16)])
-    act(("yub", s_[:]), yp, AF.Identity, bias=2048.0)
+    group([(yp, zq(ZY, k), back("ms2", 48 * k, 48 * k + 48) if k < 12 else ("ms2", s_[:, 1551 - 48 * k:1503 - 48 * k:-1])) for k in range(16)])
+    act(("yub", s_[:]), yp, AF.Copy)
     dma("S", ("yu", s_[:]), ("yub", s_[:]), 2000.0)
     dma("G", ("ylim", s_[:]), ("lim3", s_[:]), 2500.0)
     dma("S", ("ysr", s_[:, 192:576]), ("ys", s_[:, 192:576]), 2000.0)
@@ -617,7 +827,7 @@ def lay_out(ops):
     pre = [set(o["deps"]) | ({o["after"]} if o["after"] is not None else set()) for o in ops]
     prev = {}
     for k, o in enumerate(ops):
-        if o["q"] in "SG":
+        if o["q"] == "S":
             if o["q"] in prev:
                 pre[k].add(prev[o["q"]])
             prev[o["q"]] = k
@@ -633,7 +843,7 @@ def lay_out(ops):
     ahead = [[(u, delay(k, u)) for u in users[k]] for k in range(n)]
     behind = [[(d, delay(d, k)) for d in pre[k]] for k in range(n)]
 
-    def place(nxt, deg, key, first, slack):
+    def place(nxt, deg, key, first, slack, hot):
         left, ready, start, seq = list(deg), list(first), [0.0] * n, []
         free = {q: 0.0 for q in "VAPGSR"}
         loose = set(k for k in range(n) if left[k] == 0)
@@ -641,7 +851,7 @@ def lay_out(ops):
             k = min(loose, key=lambda c: (max(ready[c], free[ops[c]["q"]]), c))
             q = ops[k]["q"]
             t = max(ready[k], free[q]) + (slack if q in "VA" else 0.0)
-            k = min((c for c in loose if ops[c]["q"] == q and ready[c] <= t), key=lambda c: (key[c], c))
+            k = min((c for c in loose if ops[c]["q"] == q and ready[c] <= t + 0.01 - (0.0 if ops[c]["nm"] in FEED else slack if q in "VA" else 0.0)), key=lambda c: (key[c] - (hot if ops[c]["nm"] in FEED else 1e6 if nxt is ahead and ops[c]["nm"] in EARLY else 0.0), c))
             loose.discard(k)
             t, c = max(ready[k], free[q]), ops[k]["cost"]
             free[q] = t + c
@@ -653,16 +863,24 @@ def lay_out(ops):
                 if left[u] == 0:
                     loose.add(u)
         return start, seq
+    def span(seq, ind, ten, far):
+        end, free = [0.0] * n, {q: 0.0 for q in "VAPGSR"}
+        for k in seq:
+            o = ops[k]
+            t = max([free[o["q"]]] + [end[d] + x * (far if o["kind"] == "arr" else 1.0) for d, x in behind[k]])
+            free[o["q"]] = end[k] = t + o["cost"] * (ind if o["ind"] else ten if o["q"] == "P" else 1.0)
+        return max(end[k] + ops[k]["lat"] for k in range(n))
     best = None
     for slack in SLACKS:
-        key = [-float(k) for k in range(n)]
-        for _ in range(PASSES):
-            st, seq = place(behind, [len(u) for u in users], key, [o["lat"] for o in ops], slack)
-            st, seq = place(ahead, [len(p) for p in pre], [-st[k] - ops[k]["cost"] for k in range(n)], [0.0] * n, slack)
-            end = max(st[k] + ops[k]["cost"] + ops[k]["lat"] for k in range(n))
-            if best is None or end < best[0]:
-                best = (end, seq)
-            key = [-st[k] - ops[k]["cost"] for k in range(n)]
+        for hot in HOTS:
+            key = [-float(k) for k in range(n)]
+            for p in range(PASSES):
+                st, seq = place(behind, [len(u) for u in users], key, [o["lat"] for o in ops], slack, 0.0)
+                st, seq = place(ahead, [len(p) for p in pre], [-st[k] - ops[k]["cost"] for k in range(n)], [0.0] * n, slack, hot)
+                end = sum(span(seq, *c) for c in CASES)
+                if best is None or end < best[0]:
+                    best = (end, seq)
+                key = [-st[k] - ops[k]["cost"] for k in range(n)]
     return best[1]
 
 
@@ -733,9 +951,8 @@ def rank_program(g, core, T, topo):
     ops, order = PLAN[0]
     cores = T.cores
 
-    def sets(r):
-        return engine_sets(topo, cores[r], [cores[(r + 1 + b) % N] for b in range(3)])
-    mine = sets(rank)
+    def sets(r, bs):
+        return engine_sets(topo, cores[r], [cores[(r + 1 + b) % N] for b in bs])
     Q = {"V": g.vector, "A": g.scalar, "P": g.tensor, "G": g, "S": g.sync}
 
     def full(o):
@@ -744,8 +961,9 @@ def rank_program(g, core, T, topo):
         if o["kind"] == "dma":
             return 16
         if o["kind"] == "send":
-            return sum(len(e) for e in mine)
-        return len(sets((rank - 1 - o["fn"]) % N)[o["fn"]])
+            return sum(len(e) for e in sets(rank, o["fn"][2]))
+        bs, j = o["fn"]
+        return len(sets((rank - 1 - bs[j]) % N, bs)[j])
     for k in order:
         o = ops[k]
         if o["kind"] == "arr":
@@ -753,13 +971,13 @@ def rank_program(g, core, T, topo):
         for d in o["waits"]:
             Q[o["q"]].wait_ge(T.sem[ops[d]["sem"]], full(ops[d]))
         if o["kind"] == "send":
-            srcs, dsts = o["fn"]
+            srcs, dsts, bs = o["fn"]
             trs = []
-            for b in range(3):
-                rid, pid, _se = topo.addr(cores[(rank + 1 + b) % N])
-                trs.append(RemoteDMATransfer(dst_ids=[DstId(rid=rid, pnc=pid)], dma_engine_mask=sum(1 << e for e in mine[b]),
-                                             remote_sem=T.sem[ops[o["arr"][b]]["sem"]],
-                                             src=T[srcs[b][0]][srcs[b][1]], dst=T[dsts[b][0]][dsts[b][1]]))
+            for j, e in enumerate(sets(rank, bs)):
+                rid, pid, _se = topo.addr(cores[(rank + 1 + bs[j]) % N])
+                trs.append(RemoteDMATransfer(dst_ids=[DstId(rid=rid, pnc=pid)], dma_engine_mask=sum(1 << x for x in e),
+                                             remote_sem=T.sem[ops[o["arr"][j]]["sem"]],
+                                             src=T[srcs[j][0]][srcs[j][1]], dst=T[dsts[j][0]][dsts[j][1]]))
             g.remote_dma_fused(trs, local_sem=T.sem[o["sem"]])
             continue
         ins = o["fn"](g, T)

@@ -12,27 +12,22 @@ CHK0 = (((256, 320), (192, 256), (128, 192)), ((64, 128),), ((0, 64),))
 LIST0 = ((256, 320), (0, 256))
 CHK = (((192, 256), (320, 384), (256, 320), (128, 192), (64, 128)), ((0, 64),))
 LISTV = ((320, 384), (256, 320), (192, 256), (0, 192))
-LEAD = (2, 0)
-LO2 = 2
-TAIL = (0, 1, 8)
-LASTV = (0,)
-CASES = ((1.0, 1.0, 1.0), (1.0, 1.0, 1.0), (0.75, 1.0, 1.0), (1.25, 1.0, 1.0), (1.0, 1.1, 1.0), (1.0, 1.0, 1.5))
-HOTS, FEED = (0.0, 400.0, 1000.0, 3000.0), ("val", "rec", "ys", "pw", "onc", "osd0", "osd1")
-CALL, FLY = 1000.0, (1500.0, 1200.0)
+ALLN = ((128, 192), (0, 128), (192, 384))
 GO = ((0, 1), (2,))
-MID = None
-ALLH, ALLN = True, ((128, 192), (0, 128), (192, 384))
-ONG = "d"
-WIDE = 128
-DIRECT = {("si", 0): 16, ("rec", 0): 16}
-EARLY = ("pi", "ph", "cols", "pb", "zz", "bk", "meta0", "cb", "cb2")
+REPD, REPA = 2, 4
+FLAG = (0,)
+FIRST, LATE = 8, -4
+SCAN0, SCAN = (448, 768), (192, 768)
 ONVD = (0, 0)
-SCAN0, SCAN = (0, 768), (0, 768)
-AHEAD = False
-HAVE = -1
+EARLY = ("pg", "one", "wid", "pi", "ph", "cols", "pb", "cb", "cb2", "r3")
+AHEAD_BY = {"Vf0": -500, "Vf2": 2000, "Vf3": 4000, "Vf4": -1000, "Vf5": -1000, "Vosd": -2000, "Vpq": -500, "Vcr": -1000, "Vcv": -2000,
+            "Vlim3": 500, "Vsw1": 500, "Vsw6": 500, "Vlo": -500, "Vvi": -500, "Vvt": -1000, "Vonr": 4000, "Vold": 4000, "Vlr": 1000,
+            "Voff": -2000, "Vrepr": 500, "Vg3": -500, "Afc": 1000, "Ppd": 500, "Ppm": 1000}
+WAIT_FOR = {"Ppm": 130, "Ppn": 130, "Ppx": 130, "Vt": 130, "Vsw1": 130, "Vsw6": 130, "Vys": 130, "Voff": 300}
+CALL, FLY = 1000.0, (1500.0, 1200.0)
 ROBV = (((192, 256), (0, 192)),) * 2 + ((),)
 ROBS = (((320, 384), (256, 320)),) * 2 + (((128, 192), (64, 128), (0, 64), (192, 256), (256, 320), (320, 384)),)
-ONV0 = ((0, 0), (1, 1), (1, 1), (1, 1))
+ONV0 = ((1, 1), (1, 1), (1, 1), (1, 1))
 ONV = ((1, 1), (0, 0), (1, 1), (1, 1))
 NV0 = (768 - VS) // 16
 LC = 9216
@@ -41,25 +36,25 @@ SB = {
     "si": ([128, 768], I), "li": ([128, 768], I), "ui": ([8, 768], I), "fb": ([128, 4096], B),
     "u16": ([8, 784], H), "flag": ([64, 768], B), "hi": ([64, 768], B), "one": ([128, 512], B), "cb": ([1, 512], B), "cb2": ([2, 128], B), "vi": ([128, 48], I), "ck": ([1, 128], H),
     "wid": ([128, 160], B), "w0": ([128, 160], B), "w1": ([128, 160], B), "nid": ([128, 128], B), "bigi": ([128, 128], B),
-    "blk0": ([128, 128], B), "blk": ([128, 128], B), "up": ([128, 128], B), "dn": ([128, 128], B), "dia": ([128, 128], B),
-    "d1": ([128, 128], B), "d2": ([128, 128], B), "bk": ([128, 3, 128], B),
-    "zz": ([128, 9, 144], B), "zc": ([128, 144], H), "z8": ([8, 144], B), "b8w": ([8, 128], B), "zr": ([1, 144], B), "ir": ([1, 2, 784], B),
+    "blk0": ([128, 128], B), "blk": ([128, 128], B), "up": ([128, 128], B),
+    "d1": ([128, 128], B), "bk": ([128, 3, 128], B),
+    "zz": ([128, 9, 144], B), "z8": ([8, 144], B), "b8w": ([8, 128], B), "zr": ([1, 144], B), "ir": ([1, 2, 784], B),
     "r3": ([8, 64], B), "pu": ([8, 128], B), "ev": ([64, 144], B), "phi": ([64, 128], B), "pfl": ([64, 128], B),
     "n4k": ([64, 64], B),
-    "pi": ([128, 8], I), "pg": ([128, 8], I), "ph": ([128, 8], I), "pb": ([128, 8], I), "cols": ([128, 32], F), "b8": ([128, 8], F),
+    "pi": ([128, 8], I), "pg": ([128, 8], I), "ph": ([128, 8], I), "pb": ([128, 8], I), "cols": ([128, 32], F),
     "ai1": ([128, 768], B), "ai2": ([128, 768], B), "meta0": ([128, 768], B),
     "sn0": ([128, 768 - VS], H), "t0": ([128, 16, 2, 16], H), "pq": ([128, 16, 48], I), "vt": ([128, 48], F), "pw": ([128, 384], I),
     "off0": ([128, 768 - VS], U), "offr": ([128, 384], U), "offd": ([128, 192], U), "offa": ([128, 192], U), "offb": ([128, 16, 12], U),
     "onr": ([128, 384], U), "onc": ([128, 384], U),
-    "rep0": ([128, 2 * (768 - VS)], B), "repr": ([128, 1536], B), "repd": ([128, 384], B), "repa": ([128, 384], B),
+    "rep0": ([128, 2 * (768 - VS)], B), "repr": ([128, 1536], B), "repd": ([128, 768], B), "repa": ([128, 768], B), "d1b": ([128, 128], B),
     "cv": ([128, 16 * (768 - VS)], B), "cr": ([128, 16 * 384], B), "fc": ([128, LC], B), "cc": ([128, LC], B),
-    "sw": ([128, 768], F), "hol": ([128, 784], B), "th": ([128, 768], B), "cum": ([128, 768], H), "cm": ([128, 768], H),
-    "ini": ([128, 8], F), "plc": ([128, 48], U), "ld": ([128, 24], U), "lr": ([128, 48], U),
+    "sw": ([128, 768], F), "hol": ([128, 784], B), "th": ([128, 768], B), "cum": ([128, 768], H), "cm": ([128, 960], H),
+    "ini": ([128, 8], F), "off2": ([128, 2], F), "old": ([128, 576], B), "plc": ([128, 48], U), "ld": ([128, 24], U), "lr": ([128, 48], U),
     "give": ([128, 384], H), "have": ([128, 384], H), "g32": ([128, 384], F), "val": ([128, 384], F), "rec": ([128, 384], F),
-    "ys": ([128, 768], F), "yin": ([128, 192], F), "yub": ([128, 48], F), "lim3": ([128, 768], B),
+    "ys": ([128, 768], F), "yin": ([128, 192], F), "yub": ([128, 48], F), "lim3": ([128, 768], F), "idf": ([128, 128], F),
 }
 for _t in range(RO):
-    SB.update({"lim%d" % _t: ([128, 768], B), "ms%d" % _t: ([128, 976], B), "lo%d" % _t: ([128, 192], B)})
+    SB.update({"lim%d" % _t: ([128, 768], B), "ms%d" % _t: ([128, 976], B), "lo%d" % _t: ([128, 192], B if _t < RO - 1 else F)})
     if _t < RO - 1:
         SB.update({"nd%d" % _t: ([128, 384], F), "sin%d" % _t: ([128, 192], F), "osd%d" % _t: ([128, 192], I), "oin%d" % _t: ([128, 192], I)})
 SCRATCH = {_k: ("sbuf", _v[0], _v[1]) for _k, _v in SB.items()}
@@ -68,7 +63,7 @@ SCRATCH.update({"pd": ("psum", [128, 1024], F), "pr": ("psum", [128, 512], F), "
 BANK0 = {"pd": 0, "pr": 2, "pn": 3, "px": 4, "p4": 5, "pm": 7}
 SEMAPHORES = ["qV", "qA", "qP", "qG"] + ["d%d" % _k for _k in range(90)]
 
-CY, GA, SCT, PECY, HOP, PASSES, SLACKS = 0.83, 1.56, 3.8, 0.5, 100.0, 3, (0.0, 120.0, 250.0)
+CY, GA, SCT, PECY, HOP, PASSES = 0.83, 1.56, 3.8, 0.5, 100.0, 2
 
 
 def _cells(ap):
@@ -78,7 +73,16 @@ def _cells(ap):
 
 
 def copies(lo, hi):
-    return 8 if hi - lo <= 32 else 4 if hi - lo <= WIDE else 2
+    return 4 if hi - lo <= 128 else 2
+
+
+def tag(ap):
+    nm = ap[0].rstrip("012")
+    if nm in ("val", "rec", "pw", "onc"):
+        return "f%d" % (_cells(ap).min() // 64)
+    if nm in ("sw", "hol", "th", "nd"):
+        return "%s%d" % (nm, (_cells(ap).min() - 16 * (nm == "hol")) // 64)
+    return nm
 
 
 def spans(runs):
@@ -151,7 +155,7 @@ def build():
                     lw[ap[0]][_cells(ap)] = me
         deps.discard(me)
         ops.append({"q": q, "fn": fn, "deps": deps, "cost": cost, "kind": kind, "after": after, "lat": lat, "ind": ind,
-                    "nm": (writes + reads)[0][0]})
+                    "nm": (writes + reads)[0][0], "tag": tag((writes + reads)[0])})
         return me
 
     def n_of(ap):
@@ -216,7 +220,7 @@ def build():
 
     def mm(out, l, r, start, stop, after=None):
         return add("P", lambda g, T: g.tensor.matmul(A_(T, out), A_(T, l), A_(T, r), start, stop), [l, r], [out],
-                   max(64, n_of(r)) * PECY, acc=(start, stop), after=after)
+                   max(64, n_of(r)) * PECY * (4 if SCRATCH[r[0]][2] == F else 1), acc=(start, stop), after=after)
 
     def group(items, after=None):
         for k, (o, l, r) in enumerate(items):
@@ -271,14 +275,16 @@ def build():
         return (buf, s_[:, 783 - lo:783 - hi:-1])
 
     dma("S", ("si", s_[:]), ("sr", s_[:]), 3000.0)
-    dma("A", ("ui", s_[:]), ("u", s_[:]), 2200.0)
-    dma("S", ("li", s_[:]), ("lim", s_[:]), 4000.0)
-    dma("S", ("fb", s_[:]), ("fit", s_[:]), 7500.0)
+    a = dma("A", ("ui", s_[:]), ("u", s_[:]), 2200.0)
+    b = dma("A", ("li", s_[:, VS:768]), ("lim", s_[:, VS:768]), 3700.0)
+    dma("S", ("fb", s_[:]), ("fit", s_[:]), 7100.0)
+    c = dma("A", ("li", s_[:, 0:VS]), ("lim", s_[:, 0:VS]), 7500.0)
+    ops[b]["after"], ops[c]["after"] = a, b
     v_set(("one", s_[:]), 1.0)
     g_iota(("pi", s_[:]), [[-16, 8]], 0, 1)
     g_iota(("ph", s_[:]), [[1, 8]], 0, 0)
     v_set(("zz", s_[:, Z1, :]), 0.0)
-    for z in ("zc", "zr", "ck", "r3", "pu"):
+    for z in ("zr", "ck", "r3", "pu"):
         v_set((z, s_[:]), 0.0)
     for k, c in enumerate((-45056.0, 2048.0 * FINE, 2048.0, 4096.0)):
         v_set(bias(k), c)
@@ -289,12 +295,14 @@ def build():
     g_sel(("z8", s_[:]), ("one", s_[0:8, 0:144]), [[1, 144]], AL.is_equal, -15, -16)
     g_sel(("b8w", s_[:]), ("one", s_[0:8, 0:128]), [[1, 8], [0, 16]], AL.is_equal, 0, -1)
     g_sel(("ev", s_[:]), ("one", s_[0:64, 0:144]), [[1, 144]], AL.is_equal, -16, -2)
-    g_iota(("ir", s_[:, 0, 16:784]), [[-32, 24], [0, 32]], 736, 0)
-    g_iota(("ir", s_[:, 1, 16:784]), [[0, 24], [-1, 32]], 31, 0)
     g_sel(("blk0", s_[:]), ("one", s_[:, 0:128]), [[-16, 8], [0, 16]], AL.is_ge, 0, 1)
     g_sel(("blk", s_[:]), ("blk0", s_[:]), [[16, 8], [0, 16]], AL.is_ge, 15, -1)
     g_sel(("up", s_[:]), ("blk", s_[:]), [[1, 128]], AL.is_equal, 1, -1)
-    g_sel(("dn", s_[:]), ("blk", s_[:]), [[1, 128]], AL.is_equal, -1, -1)
+    g_iota(("ir", s_[:, 0, 16:784]), [[-32, 24], [0, 32]], 736, 0)
+    g_iota(("ir", s_[:, 1, 16:784]), [[0, 24], [-1, 32]], 31, 0)
+    first = [k for k, o in enumerate(ops) if o["q"] == "G"]
+    for a, b in zip(first, first[1:]):
+        ops[b]["after"] = a
     v_set(("zr", s_[:, 15:144:16]), 1.0)
     v_set(("ck", s_[:, 3:128:16]), 997.0)
     v_set(("ck", s_[:, 5:128:16]), 1994.0)
@@ -310,7 +318,6 @@ def build():
     v_ts(col(C_FL), ("pb", s_[:, 2:3]), 256.0 * 997, AL.mult, -256.0 * 2047.5, AL.add)
     v_ts(col(C_HI), ("pb", s_[:, 2:3]), 997.0, AL.mult)
     v_ts(col(C_T3), ("pb", s_[:, 2:3]), 3.0, AL.is_lt)
-    v_ts(col(C_DG), ("pb", s_[:, 1:2]), 0.0, AL.is_equal, -2.0, AL.add)
     v_copy(col(C_PAIR), ("pb", s_[:, 3:4]))
 
     def cols(k, n):
@@ -322,16 +329,15 @@ def build():
     v_tt(cols(C_R, 3), cols(C_E + 3, 3), cols(C_KS, 3), AL.add)
     v_ts(("zz", s_[:, Z1, 15:128:16]), ("pg", s_[:]), 0.0, AL.is_equal)
     act(("zz", s_[:, Z4096, :]), ("zz", s_[:, Z1, :]), AF.Copy, scale=4096.0)
-    act(("b8", s_[:]), ("zz", s_[:, Z1, 15:128:16]), AF.Copy)
-    for k, c in enumerate((C_K, C_D, C_D + 1, C_E + 5, C_R, C_R + 1, C_R + 2)):
-        act(("zz", s_[:, ZY + k, :]), ("zz", s_[:, Z1, :]), AF.Copy, scale=col(c))
     U16 = ("u16", s_[:, 16:784])
-    v_ts(U16, ("ui", s_[:]), -2048.0, AL.add)
+    v_ts(("u16", s_[:, 16 + VS:784]), ("ui", s_[:, VS:768]), -2048.0, AL.add)
+    v_ts(("u16", s_[:, 16:16 + VS]), ("ui", s_[:, 0:VS]), -2048.0, AL.add)
     act(("w0", s_[:]), ("wid", s_[:]), AF.Copy, scale=col(C_W0))
     act(("w1", s_[:]), ("wid", s_[:]), AF.Copy, scale=col(C_W1))
     act(("nid", s_[:]), ID, AF.Copy, scale=-1.0)
+    act(("bigi", s_[:]), ID, AF.Copy, scale=-32768.0)
     for t in range(RO):
-        act(("r3", s_[:, t:64:8]), ("wid", s_[0:8, 16:24]), AF.Copy)
+        ops[step(("r3", s_[:, t:64:8]), ("wid", s_[0:8, 16:24]), -128.0)]["cost"] += 1300.0 * (t == 0)
         act(("pu", s_[:, 2 * t + 1:128:16]), ("wid", s_[0:8, 16:24]), AF.Copy)
     act(("n4k", s_[:]), ("wid", s_[0:64, 16:80]), AF.Copy, scale=-4096.0)
 
@@ -344,7 +350,7 @@ def build():
         group([(o, ("r3", s_[:]), back("u16", lo, hi)), (o, ("n4k", s_[:]), ("flag", s_[:, lo:hi]))])
     act(("hi", s_[:]), ("pd", s_[0:64, 0:768]), AF.Identity, bias=col(C_HI, 64))
 
-    def t_stage(runs, v):
+    def t_stage(runs, v, after=None):
         nb = sum(hi - lo for lo, hi in runs)
         for k0 in range((nb + 15) // 16):
             a0, a1 = 16 * k0, min(nb, 16 * k0 + 16)
@@ -359,7 +365,7 @@ def build():
                             items.append((("p4", s_[:, x0:x1, b, :]), ("w%d" % b, s_[:, c0:c0 + 128]),
                                           ("t0", s_[:, lo + x0 - at:lo + x1 - at, x, :])))
                 at += hi - lo
-            group(items)
+            group(items, after)
         for i in range(16):
             v_tt(("pq", s_[:, i, 0:2 * nb]), ("p4", s_[:, 0:nb, :, i]), (v, s_[:, 0:2 * nb]), AL.mult)
 
@@ -392,26 +398,21 @@ def build():
     def on_vector(at):
         return [k for k in range(at, len(ops)) if ops[k]["q"] == "V"]
 
-    def weave(a, b):
-        return [k for pair in zip(a, b) for k in pair] + a[len(b):] + b[len(a):]
-
-    def flush(most=99):
-        for _ in range(min(most, len(held))):
+    def flush():
+        while held:
             line(held.pop(0))
 
-    def scalar_run(off, lo, hi, lim, out, first, ahead=True, onv=(), spare=False, direct=0, lp=None):
+    def scalar_run(off, lo, hi, lim, out, first, ahead=True, direct=0, lp=None):
         n = hi - lo
         at = ring[0]
         ring[0] += 16 * n
         if not ahead:
             flush()
-        for a in range(lo, hi, 64):
-            b = min(hi, a + 64)
-            line(act(("fc", s_[:, at + 16 * (a - lo):at + 16 * (b - lo)]), FIT + ((off, s_[:, a:b]),), AF.Copy))
-            flush(2 if b < hi else 99)
+        line(act(("fc", s_[:, at:at + 16 * n]), FIT + ((off, s_[:, lo:hi]),), AF.Copy))
+        flush()
         for k, (l, r) in enumerate(first):
             mm(out, l, r, k == 0, False)
-        per = 8 if n <= 64 else 4
+        per = 8
         if direct:
             if lp is None:
                 lp = ("pm", s_[:, 0:n])
@@ -420,16 +421,13 @@ def build():
                 v_tt(("cc", s_[:, at + n * i:at + n * i + n]), ("fc", s_[:, at + i:at + 16 * n:16]), lp, AL.is_gt)
                 mm(out, zq(Z4096, i), ("cc", s_[:, at + n * i:at + n * i + n]), False, direct == 16 and i == 15)
         for i0 in range(0, 16 - direct, per):
-            pb, base = ("pm", 0) if spare and i0 == 0 else ("pd", 512 * (unit[0] % 2))
-            unit[0] += pb == "pd"
+            pb, base = "pd", 512 * (unit[0] % 2)
+            unit[0] += 1
             for j in range(per):
                 o = (pb, s_[:, base + n * j:base + n * j + n])
                 group([(o, ID, ("fc", s_[:, at + i0 + j:at + 16 * n:16])), (o, ("nid", s_[:]), (lim, s_[:, lo:hi]))])
             o, a = ("cc", s_[:, at + n * i0:at + n * (i0 + per)]), (pb, s_[:, base:base + n * per])
-            if i0 // per in onv:
-                v_ts(o, a, 0.5, AL.is_gt)
-            else:
-                held.append(step(o, a, -128.0))
+            held.append(step(o, a, -128.0))
             for i in range(i0, i0 + per):
                 mm(out, zq(Z4096, i), ("cc", s_[:, at + n * i:at + n * i + n]), False, i == 15 - direct)
 
@@ -461,18 +459,28 @@ def build():
             else:
                 step(("th", s_[:, a:b]), o, col(C_TH))
 
-    def ranks(r0, r1):
+    def ranks(r0, r1, on, more):
         c = s_[:, r0:r1]
-        v_scan(("cum", c), ("th", c), ("ini", s_[:, nini[0] % 8:nini[0] % 8 + 1]) if r0 else 0.0)
-        if r1 < 768:
+        v_scan(("cum", c), ("th", c), ("ini", s_[:, nini[0] % 8:nini[0] % 8 + 1]) if on else 0.0)
+        if more:
             nini[0] += 1
             v_copy(("ini", s_[:, nini[0] % 8:nini[0] % 8 + 1]), ("cum", s_[:, r1 - 1:r1]))
-        else:
-            mm(("pn", s_[:, 500:501]), ("d1", s_[:]), ("cum", s_[:, 767:768]), True, True)
-            v_ts(("zc", s_[:, 15:128:16]), ("b8", s_[:]), ("pn", s_[:, 500:501]), AL.mult)
         for a, b, o in banked(r0, r1):
-            mm(o, ("d2", s_[:]), ("cum", s_[:, a:b]), True, True)
-            v_tt(("cm", s_[:, a:b]), o, ("th", s_[:, a:b]), AL.mult)
+            group([(o, ("d1b", s_[:]), ("th", s_[:, a:b])), (o, ("d1", s_[:]), ("cum", s_[:, a:b]))])
+
+    def select(cutp):
+        e1, e2 = ("cum", s_[:, cutp - 1:cutp]), ("cum", s_[:, 767:768])
+        for k in range(2):
+            o = ("pn", s_[:, 500 + k:501 + k])
+            group([(o, ("up", s_[:]), e1), (o, ("up", s_[:]), e2)] + [(o, ("d1", s_[:]), e1)] * k)
+        v_ts(("off2", s_[:]), ("pn", s_[:, 500:502]), -2048.0, AL.add)
+        for r0, r1, k in ((0, cutp, 0), (cutp, 768, 1)):
+            for a, b, o in banked(r0, r1):
+                c = ("cm", s_[:, a + 768:b + 768] if b <= 192 else s_[:, a:b])
+                if 384 <= a < 704:
+                    act(c, o, AF.Relu, bias=("off2", s_[:, k:k + 1]))
+                else:
+                    v_ts(c, o, ("off2", s_[:, k:k + 1]), AL.add, 0.0, AL.max)
 
     def mark(lo, hi, onv):
         if onv:
@@ -481,8 +489,17 @@ def build():
             step(("hol", s_[:, 16 + lo:16 + hi]), ("sw", s_[:, lo:hi]), -256.0 * 4095.5)
 
     def holes(lo, hi, p, s, onv):
+        if lo in FLAG:
+            v_ts(("hol", s_[:, 16 + lo:16 + hi]), p, 4096.0, AL.is_ge)
         v_tt(("sw", s_[:, lo:hi]), p, s, AL.max)
-        mark(lo, hi, onv)
+        if lo not in FLAG:
+            mark(lo, hi, onv)
+
+    def start(lo, hi, s):
+        if lo not in FLAG:
+            return [(bias(B_CHK), ones(hi - lo))]
+        v_ts(("old", s_[:, lo:hi]), s, 4096.0, AL.is_ge, -2.0, AL.mult)
+        return [(bias(B_CHK), ones(hi - lo)), (("bigi", s_[:]), ("old", s_[:, lo:hi]))]
 
     def hol_back(a, b):
         return back("hol", a, b)
@@ -497,16 +514,20 @@ def build():
                 for a, b in lists:
                     if b == hi:
                         offsets(a, b)
-                scalar_run("onc", lo, hi, lim, (pb, s_[:, lo:hi]), [(bias(B_CHK), ones(hi - lo))], AHEAD or (lo, hi) != plan_[0][0],
-                           (), False, DIRECT.get((s, lo), 0))
+                scalar_run("onc", lo, hi, lim, (pb, s_[:, lo:hi]), start(lo, hi, (s, s_[:, lo:hi])), (lo, hi) != plan_[0][0],
+                           16 if lo == 0 else 0)
             if k == 0:
-                donors()
+                donors[0]()
             lo, hi = min(r[0] for r in runs), max(r[1] for r in runs)
             holes(lo, hi, (pb, s_[:, lo:hi]), (s, s_[:, lo:hi]), onv[k + 1][0])
             classes(768 - hi, 768 - lo, hol_back, onv[k + 1][1])
             for a, b in zip(scans, scans[1:]):
-                if 768 - hi < b <= 768 - lo or (k == 0 and b <= 768 - hi):
-                    ranks(a, b)
+                if 768 - hi < b <= 768 - lo:
+                    ranks(a, b, a > scans[0], b < 768)
+            if k == 0:
+                donors[1]()
+                ranks(0, scans[0], False, False)
+        select(scans[0])
         flush()
 
     group([(("pn", s_[:, 0:NV0]), ("z8", s_[:, 15 - q:143 - q]), ("u16", s_[:, 16 + VS + q:784:16])) for q in range(16)])
@@ -515,41 +536,45 @@ def build():
     group([(o, bias(B_2K), ones(VS)), (o, ("b8w", s_[:]), ("u16", s_[:, 16:16 + VS]))])
     v_ts(("sn0", s_[:]), ("si", s_[:, VS:768]), -2048.0, AL.add)
     v_tr(("t0", s_[:, 0:NV0 // 2]), ("sn0", s_[:]))
-    v_copy(("lim0", s_[:, 0:VS]), ("li", s_[:, 0:VS]))
+    narrow(("lim0", s_[:, 0:VS]), ("li", s_[:, 0:VS]), True)
     v_copy(("rep0", s_[:, 0:768 - VS]), ("li", s_[:, VS:768]))
     v_copy(("rep0", s_[:, 768 - VS:2 * (768 - VS)]), ("rep0", s_[:, 0:768 - VS]))
     dma("S", ("lim0", s_[:, VS:768]), ("rep0", s_[:, 0:768 - VS]), 2500.0)
     t_stage([(0, NV0 // 2)], "vt")
     t_offsets(("off0", s_[:]), 0, NV0)
-    act(("bigi", s_[:]), ID, AF.Copy, scale=-32768.0)
-    act(("dia", s_[:]), ID, AF.Copy, scale=col(C_DG))
-    for t in range(RO):
-        act(("bk", s_[:, t, :]), ("blk", s_[:]), AF.Copy, scale=col(C_K + t))
     o = ("px", s_[0:64, 0:128])
     group([(o, ("wid", s_[0:64, 16:80]), ("ev", s_[:, 16:144])), (o, ("nid", s_[0:64, 0:64]), ("ev", s_[:, 15:143]))])
     o = ("px", s_[0:64, 128:256])
     mm(o, ("n4k", s_[:]), ("ev", s_[:, 15:143]), True, True)
     act(("phi", s_[:]), ("px", s_[0:64, 0:128]), AF.Copy, scale=col(C_T3, 64))
     act(("pfl", s_[:]), ("px", s_[0:64, 128:256]), AF.Copy, scale=col(C_T3, 64))
-    o = ("pr", s_[:, 256:384])
-    group([(o, ID, (z, s_[:])) for z in ("up", "dn", "dia")])
     o = ("pr", s_[:, 384:512])
     group([(o, ID, ID), (o, ("nid", s_[:]), ("up", s_[:]))])
-    act(("d2", s_[:]), ("pr", s_[:, 256:384]), AF.Copy)
     act(("d1", s_[:]), ("pr", s_[:, 384:512]), AF.Copy)
+    act(("d1b", s_[:]), ("pr", s_[:, 384:512]), AF.Copy, scale=2048.0)
 
     def digits(t):
         return [("zr", s_[:, 9 - 2 * t - k:137 - 2 * t - k]) for k in range(2)]
-    for (lo, hi), o in zip(HALVES, (blocks(512, 1024), ("px", s_[:, 0:256]))):
+    for lo, hi in HALVES:
+        o = blocks(lo, hi)
         group([(o, ("pu", s_[:]), back("u16", lo, hi)), (o, ("pfl", s_[:]), ("flag", s_[:, lo:hi])), (o, ("phi", s_[:]), ("hi", s_[:, lo:hi])),
                (o, ("ck", s_[:]), ones(hi - lo))] + [(o, z, ("ir", s_[:, k, 16 + lo:16 + hi])) for k, z in enumerate(digits(0))])
-        act(("meta0", s_[:, lo:hi]), o, AF.Copy)
+    act(("meta0", s_[:]), blocks(0, 768), AF.Copy)
 
     def donors0():
         vector_run(("off0", 0), "cv", 0, ("rep0", s_[:]), ("pn", s_[:, 0:768 - VS]), [(bias(B_CHK), ones(768 - VS))])
+
+    def donors1():
         holes(VS, 768, ("pn", s_[:, 0:768 - VS]), ("si", s_[:, VS:768]), ONV0[0][0])
         classes(0, 768 - VS, hol_back, ONV0[0][1])
-    checks(CHK0, LIST0, "lim0", "si", lambda lo, hi: n_offsets("onc", "si", ("pm", s_[:, 128 + lo:128 + hi]), lo, hi), donors0, ONV0, SCAN0)
+    checks(CHK0, LIST0, "lim0", "si", lambda lo, hi: n_offsets("onc", "si", ("pm", s_[:, 128 + lo:128 + hi]), lo, hi, lo == 0), (donors0, donors1), ONV0, SCAN0)
+    for k, c in ((ZD, C_D), (ZR, C_R)):
+        line(act(("zz", s_[:, k, :]), ("zz", s_[:, Z1, :]), AF.Copy, scale=col(c)))
+    for t in range(RO):
+        line(act(("bk", s_[:, t, :]), ("blk", s_[:]), AF.Copy, scale=col(C_K + t)))
+    for k, c in ((ZD + 1, C_D + 1), (ZD + 2, C_E + 5), (ZR + 1, C_R + 1), (ZR + 2, C_R + 2), (ZY, C_K)):
+        line(act(("zz", s_[:, k, :]), ("zz", s_[:, Z1, :]), AF.Copy, scale=col(c)))
+    line(act(("idf", s_[:]), ID, AF.Copy))
 
     SW = ("sw", s_[:, 0:768])
     for t in range(RO):
@@ -558,11 +583,10 @@ def build():
         LW = ("lim%d" % t, s_[:, 0:768])
         ring[0] = 0
         X = ("pm", s_[:, 0:48])
-        group([(X, ("zc", s_[:, 15 - q:143 - q]), ("th", s_[:, q:768:16])) for q in range(16)] +
-              [(X, zq(Z1, q), ("cm", s_[:, q:768:16])) for q in range(16)])
+        group([(X, zq(Z1, q), ("cm", s_[:, 192 + q:960:16] if t else s_[:, q:768:16])) for q in range(16)])
+        v_ts(("plc", s_[:]), X, -1.0, AL.add)
         WIN = (ms, s_[:, 16:784], ("plc", s_[:]))
         if t == 0:
-            v_ts(("plc", s_[:]), X, -1.0, AL.mult, 767.0, AL.add)
             v_copy(WIN, ("meta0", s_[:]))
             for o, src in ((blocks(0, 192), s_[207:15:-1]), (blocks(512, 896), s_[400:784]), (blocks(192, 384), s_[399:207:-1])):
                 group([(o, z, ("ir", s_[:, k, src])) for k, z in enumerate(digits(1))])
@@ -572,8 +596,6 @@ def build():
             dma("S", ("ai2", s_[2:128, :]), ("ai1", s_[0:126, :]), 2500.0)
             dma("S", ("ai2", s_[0:2, :]), ("ai1", s_[0:2, :]), 2500.0)
         else:
-            v_ts(("plc", s_[:, 0:36]), ("pm", s_[:, 12:48]), -1.0, AL.mult, 767.0, AL.add)
-            v_ts(("plc", s_[:, 36:48]), ("pm", s_[:, 0:12]), -1.0, AL.mult, 767.0, AL.add)
             v_tt(WIN, ("ms%d" % (t - 1), s_[:, 208:976]), ("ai%d" % t, s_[:]), AL.add)
         robv, robs = ROBV[t], ROBS[t]
         nr = 48 if last else 24
@@ -630,30 +652,32 @@ def build():
         def sums(lo, hi):
             group([(blocks(lo, hi), bias(B_2K), ones(hi - lo)), (blocks(lo, hi), ID, ("have", s_[:, lo:hi]))])
             o = blocks(512 + lo, 512 + hi)
-            group([(o, bias(B_4K), ones(hi - lo)), (o, ID, ("have", s_[:, lo:hi])), (o, ID, ("give", s_[:, lo:hi]))])
-        if last and ALLH:
+            group([(o, bias(B_2K), ones(hi - lo)), (o, ID, ("have", s_[:, lo:hi])), (o, ("idf", s_[:]), ("g32", s_[:, lo:hi]))])
+        if last:
             send(ms, 16, ms, 784, True)
 
             def v_pick(out, c0, lo, hi):
                 return v_copy((out, s_[:, c0 + lo:c0 + hi]), LW + (("lr", s_[:, lo // 16:hi // 16]),))
             at = len(ops)
             for lo, hi in ALLN:
-                if lo == 0:
-                    line(pick("g32", 0, SW, "ld", lo, hi))
-                else:
-                    v_copy(("g32", s_[:, lo:hi]), SW + (("ld", s_[:, lo // 16:hi // 16]),))
+                v_ts(("g32", s_[:, lo:hi]), SW + (("ld", s_[:, lo // 16:hi // 16]),), 4096.0, AL.min)
                 n_offsets("onr", "g32", ("pr", s_[:, lo:hi]), lo, hi)
-            first = on_vector(at)[:8]
+            first = on_vector(at)[:FIRST]
             for a, b in zip(first, first[1:]):
                 ops[b]["after"] = a
+            begin = at
             for lo, hi in ((0, 192), (192, 384)):
-                v_pick(limn, 0, lo, hi)
-                mm(("pd", s_[:, lo + 320 * (lo > 0):hi + 320 * (lo > 0)]), ID, (limn, s_[:, lo:hi]), True, True)
+                second = v_pick(limn, 0, lo, hi) - 1
+                mm(("pd", s_[:, lo + 320 * (lo > 0):hi + 320 * (lo > 0)]), ("idf", s_[:]), (limn, s_[:, lo:hi]), True, True)
                 ops[serials("have", "lr", lo, hi)]["after"] = first[3]
-                ops[serials("give", "ld", lo, hi)]["after"] = first[3]
+            for k in on_vector(at)[4:]:
+                if ops[k]["ind"] and ops[k]["after"] is None:
+                    ops[k]["after"] = first[3]
             sums(0, 192)
-            v_pick("lo2", -576, 576, 768)
+            ops[v_pick("lo2", -576, 576, 768)]["after"] = first[3]
             send("lo2", 0, limn, 576, False)
+            v_pick(limn, 0, 384, 576)
+            dma("S", ("ylim", s_[:, 0:384]), (limn, s_[:, 0:384]), 2200.0)
             gone = []
             for k, (lo, hi) in enumerate(robs):
                 pb = ("pn", "px")[k % 2]
@@ -666,159 +690,93 @@ def build():
                     if gone[-1] in bs and all(x in gone for x in bs):
                         send("ys", 576, "yin", 0, False, bs)
                 if k == 2:
+                    for x in on_vector(begin):
+                        if ops[x]["ind"] and ops[x]["tag"] in ("lim3", "have") and x > second:
+                            ops[x]["after"] = on_vector(begin)[LATE]
                     sums(192, 384)
                     dma("S", ("ysr", s_[:, 0:192]), ("ys", s_[:, 0:192]), 2000.0)
-            line(pick(limn, 0, LW, "lr", 384, 576))
             break
-        v_ts(("give", s_[:]), SW + (("ld", s_[:]),), 4096.0, AL.min, -2048.0, AL.add)
-        first, later, part = [len(ops) - 1], [], {}
-        v_tr(("t0", s_[:, 0:12]), ("give", s_[:]))
-        first.append(len(ops) - 1)
-        for k, (a, b) in enumerate(spans(robs)):
-            line(pick("g32", 0, SW, "ld", a, b))
-            n_offsets("onr", "g32", ("pr", s_[:, a:b]), a, b)
-            part["n%d" % k] = on_vector(len(ops) - 3)
-            if k == 0:
-                first[LEAD[last]:LEAD[last]] = range(len(ops) - 3, len(ops))
-        if not last:
-            line(pick("lo%d" % t, 0, LW, "ld", 0, 192))
-            send("lo%d" % t, 0, limn, 384, True)
-        for k, (a, b) in enumerate(spans(robs)):
-            (later.append if k else line)(pick(limn, 0, LW, "lr", a, b))
+        first, later = [serials("give", "ld", 0, 384)], []
+        first.append(v_tr(("t0", s_[:, 0:12]), ("give", s_[:])))
+        (a, b), = spans(robs)
+        line(pick("g32", 0, SW, "ld", a, b))
+        n_offsets("onr", "g32", ("pr", s_[:, a:b]), a, b)
+        first += range(len(ops) - 3, len(ops))
+        line(pick("lo%d" % t, 0, LW, "ld", 0, 192))
+        send("lo%d" % t, 0, limn, 384, True)
+        line(pick(limn, 0, LW, "lr", a, b))
         for k, (a, b) in enumerate(robv):
-            (held.append if k or last else line)(pick("repr", 3 * a, LW, "lr", a, b))
+            (held.append if k else line)(pick("repr", 3 * a, LW, "lr", a, b))
             if k == 0:
                 held.append(pick("g32", 0, SW, "ld", a, b))
-            at = len(ops)
-            for w in [(b - a) * r for r in (1, 2, 4) if r < copies(a, b)]:
+            for w in [(b - a) * r for r in (1, 2) if r < copies(a, b)]:
                 v_copy(("repr", s_[:, 4 * a + w:4 * a + 2 * w]), ("repr", s_[:, 4 * a:4 * a + w]))
-            part["p%d" % k] = on_vector(at)
             dma("S", (limn, s_[:, a:b]), ("repr", s_[:, 4 * a:3 * a + b]), 2500.0)
         for a, b in spans(robv[1:]):
             later.append(pick("g32", 0, SW, "ld", a, b))
-        if last:
-            held.insert(LO2, pick("lo2", -576, LW, "lr", 576, 768))
-            send("lo2", 0, limn, 576, False)
-            later.append(pick(limn, 0, LW, "lr", 384, 576))
-        else:
-            later.append(pick("repd", -192, LW, "ld", 192, 384))
-            dma("S", ("repd", s_[:, 192:384]), ("repd", s_[:, 0:192]), 2500.0)
-            dma("S", (limn, s_[:, 576:768]), ("repd", s_[:, 0:192]), 2500.0)
-            for k in range(2):
-                dma("S", ("repa", s_[:, 192 * k:192 * k + 192]), (limn, s_[:, 384:576]), 2500.0)
-        t_stage(([] if last else [(0, 12)]) + [(lo // 32, hi // 32) for lo, hi in spans(robv)], "vt")
+        later.append(pick("repd", -192, LW, "ld", 192, 384))
+        for k in range(1, REPD):
+            dma("S", ("repd", s_[:, 192 * k:192 * k + 192]), ("repd", s_[:, 0:192]), 2500.0)
+        dma("S", (limn, s_[:, 576:768]), ("repd", s_[:, 0:192]), 2500.0)
+        for k in range(REPA):
+            dma("S", ("repa", s_[:, 192 * k:192 * k + 192]), (limn, s_[:, 384:576]), 2500.0)
+        t_stage([(0, 12)] + [(lo // 32, hi // 32) for lo, hi in spans(robv)], "vt", ld_done)
         first += range(len(ops) - 16, len(ops))
         for lo, hi in robv:
             t_offsets(("offr", s_[:, lo:hi]), tcol[lo], tcol[lo] + (hi - lo) // 16)
-            part["t%d" % lo] = on_vector(len(ops) - 2)
             if lo == robv[0][0]:
                 first += range(len(ops) - 2, len(ops))
         for a, b in zip(first, first[1:]):
             ops[b]["after"] = a
         chain[0] = first[-1]
-        if not last:
-            for b in range(3):
-                cut(("osd%d" % t, s_[:, 64 * b:64 * b + 64]), ("pq", s_[:, :, 4 * b:4 * b + 4]))
-            part["o"] = on_vector(len(ops) - 3)
-            send("osd%d" % t, 0, "oin%d" % t, 0, True)
-            t_offsets(("offd", s_[:]), 12, 24, "d" in ONG)
-        send(ms, 16, ms, 784, True, None, None if last else sent[0])
-        ops[v_ts(("have", s_[:]), SW + (("lr", s_[:, 0:24]),), 4096.0, AL.min, -2048.0, AL.add)]["after"] = first[HAVE]
+        for b in range(3):
+            cut(("osd%d" % t, s_[:, 64 * b:64 * b + 64]), ("pq", s_[:, :, 4 * b:4 * b + 4]))
+        send("osd%d" % t, 0, "oin%d" % t, 0, True)
+        t_offsets(("offd", s_[:]), 12, 24, True)
+        send(ms, 16, ms, 784, True, None, sent[0])
+        ops[serials("have", "lr", 0, 384)]["after"] = first[-1]
         group([(blocks(0, 384), bias(B_2K), ones(384)), (blocks(0, 384), ID, ("have", s_[:]))])
         o = blocks(512, 896)
         group([(o, bias(B_4K), ones(384)), (o, ID, ("have", s_[:])), (o, ID, ("give", s_[:]))])
-
-        def rob_first(lo, hi):
-            return [(("cb2", s_[:]), ("one", s_[0:2, 0:hi - lo])), (("bigi", s_[:]), ("have", s_[:, lo:hi]))]
-        rec = "ys" if last else "rec"
-
-        def settle(pb, lo, hi):
-            c = s_[:, lo:hi]
-            v_tt(("val", c), (pb, c), ("g32", c), AL.max)
-            v_tt((rec, c), blocks(lo, hi), ("val", c), AL.min)
-
-        def donors_left(lo, hi):
-            v_tt(("ys", s_[:, 767 - lo:767 - hi:-1]) if last else ("nd%d" % t, s_[:, lo:hi]), blocks(512 + lo, 512 + hi), (rec, s_[:, lo:hi]), AL.subtract)
-
-        gone = []
-
-        def leave(lo, hi):
-            for b in range(3):
-                if last and lo <= 128 - 64 * b < hi:
-                    donors_left(128 - 64 * b, 192 - 64 * b)
-                    gone.append(b)
-                    for bs in GO:
-                        if b in bs and all(x in gone for x in bs):
-                            send("ys", 576, "yin", 0, False, bs)
         for k, (lo, hi) in enumerate(robs):
             pb = ("pn", "pr")[k % 2]
-            if k == 2 and later:
-                held.extend(later)
-                del later[:]
-                flush()
-            at = len(ops)
-            scalar_run("onr", lo, hi, limn, (pb, s_[:, lo:hi]), rob_first(lo, hi), direct=DIRECT.get((t, lo), 0))
-            part["d%d" % k] = on_vector(at)
-            if k == len(robs) - 1 and not last:
+            scalar_run("onr", lo, hi, limn, (pb, s_[:, lo:hi]), rob_first(lo, hi))
+            if k == len(robs) - 1:
                 held[0:0] = later
-            at = len(ops)
             settle(pb, lo, hi)
-            leave(lo, hi)
-            part["s%d" % k] = on_vector(at)
-            for k in range(k, len(robv) if k == len(robs) - 1 else min(k + 1, len(robv))):
-                lo, hi = robv[k]
-                at = len(ops)
-                vector_run(("offr", lo), "cr", 16 * lo, ("repr", s_[:, 4 * lo:4 * lo + copies(lo, hi) * (hi - lo)]), ("px", s_[:, lo:hi]), rob_first(lo, hi))
-                part["r%d" % k] = on_vector(at)
-                at = len(ops)
-                settle("px", lo, hi)
-                leave(lo, hi)
-                part["v%d" % k] = on_vector(at)
-            if last and k == 1:
-                dma("S", ("ysr", s_[:, 0:192]), ("ys", s_[:, 0:192]), 2000.0)
-        if last:
-            flush()
-            donors_left(192, 384)
-            r1 = part["r1"]
-            seq = part["r0"] + weave(part["n1"], part["v0"]) + r1[:TAIL[0]] + part["s0"] + r1[TAIL[0]:TAIL[1]] + part["s1"] + r1[TAIL[1]:]
-            if part["d1"]:
-                seq = part["r0"] + part["d1"][:TAIL[2]] + weave(part["v0"], part["s0"]) + part["d1"][TAIL[2]:] + weave(part["n1"], part["s1"]) + r1 + part["d2"]
-            for a, b in zip(seq, seq[1:]):
-                ops[b]["after"] = a
-            break
+            lo, hi = robv[k]
+            vector_run(("offr", lo), "cr", 16 * lo, ("repr", s_[:, 4 * lo:4 * lo + copies(lo, hi) * (hi - lo)]), ("px", s_[:, lo:hi]), rob_first(lo, hi))
+            settle("px", lo, hi)
         donors_left(0, 192)
         send("nd%d" % t, 0, "sin%d" % t, 0, True)
         donors_left(192, 384)
 
         def donors():
-            vector_run(("offd", 0), "cv", 0, ("repd", s_[:]), ("pn", s_[:, 192:384]), [(bias(B_CHK), ones(192))])
+            vector_run(("offd", 0), "cv", 0, ("repd", s_[:, 0:192 * REPD]), ("pn", s_[:, 192:384]), [(bias(B_CHK), ones(192))])
             holes(576, 768, ("pn", s_[:, 192:384]), ("nd%d" % t, s_[:, 192:384]), ONVD[0])
             classes(192, 384, hol_on, ONVD[1])
             for b in range(3):
-                narrow(("offb", s_[:, :, 4 * b:4 * b + 4]), ("oin%d" % t, s_[:, 64 * b:64 * b + 64]), "a" in ONG)
-            narrow(("offa", s_[:]), ("offb", s_[:]), "a" in ONG)
-            vector_run(("offa", 0), "cv", 3072, ("repa", s_[:]), ("pn", s_[:, 0:192]), [(bias(B_CHK), ones(192))])
+                narrow(("offb", s_[:, :, 4 * b:4 * b + 4]), ("oin%d" % t, s_[:, 64 * b:64 * b + 64]), True)
+            narrow(("offa", s_[:]), ("offb", s_[:]), True)
+            vector_run(("offa", 0), "cv", 3072, ("repa", s_[:, 0:192 * REPA]), ("pn", s_[:, 0:192]), start(384, 576, ("sin%d" % t, s_[:])))
+
+        def arrived():
             holes(384, 576, ("pn", s_[:, 0:192]), ("sin%d" % t, s_[:]), ONV[0][0])
             classes(0, 192, hol_on, ONV[0][1])
 
         def lists(lo, hi):
-            at = len(ops)
-            n_offsets("onc", "rec", ("pm", s_[:, 128 + lo:128 + hi]), lo, hi, "c" in ONG and lo == 0)
-            part["c%d" % lo] = on_vector(at)
-        checks(CHK, LISTV, limn, "rec", lists, donors, ONV, SCAN)
-        if MID:
-            r1 = part["r1"]
-            seq = (part["r0"] + weave(part["p1"] + part["t0"] + part["o"], part["v0"] + part["c192"]) + r1[:MID[0]] + part["s0"] + part["c320"]
-                   + r1[MID[0]:MID[1]] + part["s1"] + part["c256"] + r1[MID[1]:])
-            for a, b in zip(seq, seq[1:]):
-                ops[b]["after"] = a
+            n_offsets("onc", "rec", ("pm", s_[:, 128 + lo:128 + hi]), lo, hi, lo == 0)
+        checks(CHK, LISTV, limn, "rec", lists, (donors, arrived), ONV, SCAN)
     yp = ("pm", s_[:, 0:48])
     group([(yp, zq(ZY, k), back("ms2", 48 * k, 48 * k + 48) if k < 12 else ("ms2", s_[:, 1551 - 48 * k:1503 - 48 * k:-1])) for k in range(16)])
     act(("yub", s_[:]), yp, AF.Copy)
-    dma("S", ("yu", s_[:]), ("yub", s_[:]), 2000.0)
-    dma("G", ("ylim", s_[:]), ("lim3", s_[:]), 2500.0)
-    dma("S", ("ysr", s_[:, 192:576]), ("ys", s_[:, 192:576]), 2000.0)
-    dma("A", ("ysr", s_[:, 576:768]), ("yin", s_[:]), 2000.0)
+    dma("S", ("ylim", s_[:, 384:768]), ("lim3", s_[:, 384:768]), 2200.0)
+    dma("S", ("ysr", s_[:, 576:704]), ("yin", s_[:, 0:128]), 1800.0)
+    dma("A", ("yu", s_[:]), ("yub", s_[:]), 1800.0)
+    dma("A", ("ysr", s_[:, 192:320]), ("ys", s_[:, 192:320]), 1800.0)
+    dma("S", ("ysr", s_[:, 704:768]), ("yin", s_[:, 128:192]), 1800.0)
+    dma("A", ("ysr", s_[:, 448:576]), ("ys", s_[:, 448:576]), 1800.0)
+    dma("A", ("ysr", s_[:, 320:448]), ("ys", s_[:, 320:448]), 1800.0)
     return ops
 
 
@@ -843,15 +801,15 @@ def lay_out(ops):
     ahead = [[(u, delay(k, u)) for u in users[k]] for k in range(n)]
     behind = [[(d, delay(d, k)) for d in pre[k]] for k in range(n)]
 
-    def place(nxt, deg, key, first, slack, hot):
+    def place(nxt, deg, key, first, slack):
         left, ready, start, seq = list(deg), list(first), [0.0] * n, []
         free = {q: 0.0 for q in "VAPGSR"}
         loose = set(k for k in range(n) if left[k] == 0)
         while loose:
             k = min(loose, key=lambda c: (max(ready[c], free[ops[c]["q"]]), c))
             q = ops[k]["q"]
-            t = max(ready[k], free[q]) + (slack if q in "VA" else 0.0)
-            k = min((c for c in loose if ops[c]["q"] == q and ready[c] <= t + 0.01 - (0.0 if ops[c]["nm"] in FEED else slack if q in "VA" else 0.0)), key=lambda c: (key[c] - (hot if ops[c]["nm"] in FEED else 1e6 if nxt is ahead and ops[c]["nm"] in EARLY else 0.0), c))
+            t = max(ready[k], free[q]) + 0.01
+            k = min((c for c in loose if ops[c]["q"] == q and ready[c] <= t + slack[c]), key=lambda c: (key[c], c))
             loose.discard(k)
             t, c = max(ready[k], free[q]), ops[k]["cost"]
             free[q] = t + c
@@ -863,25 +821,14 @@ def lay_out(ops):
                 if left[u] == 0:
                     loose.add(u)
         return start, seq
-    def span(seq, ind, ten, far):
-        end, free = [0.0] * n, {q: 0.0 for q in "VAPGSR"}
-        for k in seq:
-            o = ops[k]
-            t = max([free[o["q"]]] + [end[d] + x * (far if o["kind"] == "arr" else 1.0) for d, x in behind[k]])
-            free[o["q"]] = end[k] = t + o["cost"] * (ind if o["ind"] else ten if o["q"] == "P" else 1.0)
-        return max(end[k] + ops[k]["lat"] for k in range(n))
-    best = None
-    for slack in SLACKS:
-        for hot in HOTS:
-            key = [-float(k) for k in range(n)]
-            for p in range(PASSES):
-                st, seq = place(behind, [len(u) for u in users], key, [o["lat"] for o in ops], slack, 0.0)
-                st, seq = place(ahead, [len(p) for p in pre], [-st[k] - ops[k]["cost"] for k in range(n)], [0.0] * n, slack, hot)
-                end = sum(span(seq, *c) for c in CASES)
-                if best is None or end < best[0]:
-                    best = (end, seq)
-                key = [-st[k] - ops[k]["cost"] for k in range(n)]
-    return best[1]
+    key = [-float(k) for k in range(n)]
+    for p in range(PASSES):
+        st, seq = place(behind, [len(u) for u in users], key, [o["lat"] for o in ops], [0.0] * n)
+        late = [-st[k] - o["cost"] - (1e6 if o["nm"] in EARLY else 0.0) for k, o in enumerate(ops)]
+        st, seq = place(ahead, [len(p) for p in pre], late, [0.0] * n, [0.0] * n)
+        key = [-st[k] - ops[k]["cost"] for k in range(n)]
+    return place(ahead, [len(p) for p in pre], [late[k] - AHEAD_BY.get(o["q"] + o["tag"], 0.0) for k, o in enumerate(ops)], [0.0] * n,
+                 [WAIT_FOR.get(o["q"] + o["tag"], 0.0) for o in ops])[1]
 
 
 def plan():

import numpy as np
from concourse.bass import DstId, RemoteDMATransfer
from concourse.mybir import dt, AluOpType, AxisListType, ActivationFunctionType

AL = AluOpType
AF = ActivationFunctionType
s_ = np.s_
N = 8
RO = 3
VS = 320
CHK0 = (((256, 320), (192, 256), (128, 192)), ((64, 128),), ((0, 64),))
LIST0 = ((256, 320), (0, 256))
CHK = (((192, 256), (320, 384), (256, 320), (128, 192), (64, 128)), ((0, 64),))
LISTV = ((320, 384), (256, 320), (192, 256), (0, 192))
ALLN = ((128, 192), (0, 128), (192, 384))
GO = ((0, 1), (2,))
REPD, REPA = 2, 4
FLAG = (0,)
FIRST, LATE = 8, -4
SCAN0, SCAN = (448, 768), (192, 768)
ONVD = (0, 0)
EARLY = ("pg", "one", "wid", "pi", "ph", "cols", "pb", "cb", "cb2", "r3")
AHEAD_BY = {"Vf0": -500, "Vf2": 2000, "Vf3": 4000, "Vf4": -1000, "Vf5": -1000, "Vosd": -2000, "Vpq": -500, "Vcr": -1000, "Vcv": -2000,
            "Vlim3": 500, "Vsw1": 500, "Vsw6": 500, "Vlo": -500, "Vvi": -500, "Vvt": -1000, "Vonr": 4000, "Vold": 4000, "Vlr": 1000,
            "Voff": -2000, "Vrepr": 500, "Vg3": -500, "Afc": 1000, "Ppd": 500, "Ppm": 1000}
WAIT_FOR = {"Ppm": 130, "Ppn": 130, "Ppx": 130, "Vt": 130, "Vsw1": 130, "Vsw6": 130, "Vys": 130, "Voff": 300}
CALL, FLY = 1000.0, (1500.0, 1200.0)
ROBV = (((192, 256), (0, 192)),) * 2 + ((),)
ROBS = (((320, 384), (256, 320)),) * 2 + (((128, 192), (64, 128), (0, 64), (192, 256), (256, 320), (320, 384)),)
ONV0 = ((1, 1), (1, 1), (1, 1), (1, 1))
ONV = ((1, 1), (0, 0), (1, 1), (1, 1))
NV0 = (768 - VS) // 16
LC = 9216
B, H, F, I, U = "bfloat16", "float16", "float32", "int32", "uint16"
SB = {
    "si": ([128, 768], I), "li": ([128, 768], I), "ui": ([8, 768], I), "fb": ([128, 4096], B),
    "u16": ([8, 784], H), "flag": ([64, 768], B), "hi": ([64, 768], B), "one": ([128, 512], B), "cb": ([1, 512], B), "cb2": ([2, 128], B), "vi": ([128, 48], I), "ck": ([1, 128], H),
    "wid": ([128, 160], B), "w0": ([128, 160], B), "w1": ([128, 160], B), "nid": ([128, 128], B), "bigi": ([128, 128], B),
    "blk0": ([128, 128], B), "blk": ([128, 128], B), "up": ([128, 128], B),
    "d1": ([128, 128], B), "bk": ([128, 3, 128], B),
    "zz": ([128, 9, 144], B), "z8": ([8, 144], B), "b8w": ([8, 128], B), "zr": ([1, 144], B), "ir": ([1, 2, 784], B),
    "r3": ([8, 64], B), "pu": ([8, 128], B), "ev": ([64, 144], B), "phi": ([64, 128], B), "pfl": ([64, 128], B),
    "n4k": ([64, 64], B),
    "pi": ([128, 8], I), "pg": ([128, 8], I), "ph": ([128, 8], I), "pb": ([128, 8], I), "cols": ([128, 32], F),
    "ai1": ([128, 768], B), "ai2": ([128, 768], B), "meta0": ([128, 768], B),
    "sn0": ([128, 768 - VS], H), "t0": ([128, 16, 2, 16], H), "pq": ([128, 16, 48], I), "vt": ([128, 48], F), "pw": ([128, 384], I),
    "off0": ([128, 768 - VS], U), "offr": ([128, 384], U), "offd": ([128, 192], U), "offa": ([128, 192], U), "offb": ([128, 16, 12], U),
    "onr": ([128, 384], U), "onc": ([128, 384], U),
    "rep0": ([128, 2 * (768 - VS)], B), "repr": ([128, 1536], B), "repd": ([128, 768], B), "repa": ([128, 768], B), "d1b": ([128, 128], B),
    "cv": ([128, 16 * (768 - VS)], B), "cr": ([128, 16 * 384], B), "fc": ([128, LC], B), "cc": ([128, LC], B),
    "sw": ([128, 768], F), "hol": ([128, 784], B), "th": ([128, 768], B), "cum": ([128, 768], H), "cm": ([128, 960], H),
    "ini": ([128, 8], F), "off2": ([128, 2], F), "old": ([128, 576], B), "plc": ([128, 48], U), "ld": ([128, 24], U), "lr": ([128, 48], U),
    "give": ([128, 384], H), "have": ([128, 384], H), "g32": ([128, 384], F), "val": ([128, 384], F), "rec": ([128, 384], F),
    "ys": ([128, 768], F), "yin": ([128, 192], F), "yub": ([128, 48], F), "lim3": ([128, 768], F), "idf": ([128, 128], F),
}
for _t in range(RO):
    SB.update({"lim%d" % _t: ([128, 768], B), "ms%d" % _t: ([128, 976], B), "lo%d" % _t: ([128, 192], B if _t < RO - 1 else F)})
    if _t < RO - 1:
        SB.update({"nd%d" % _t: ([128, 384], F), "sin%d" % _t: ([128, 192], F), "osd%d" % _t: ([128, 192], I), "oin%d" % _t: ([128, 192], I)})
SCRATCH = {_k: ("sbuf", _v[0], _v[1]) for _k, _v in SB.items()}
SCRATCH.update({"pd": ("psum", [128, 1024], F), "pr": ("psum", [128, 512], F), "pn": ("psum", [128, 512], F), "px": ("psum", [128, 512], F),
                "p4": ("psum", [128, 32, 2, 16], F), "pm": ("psum", [128, 512], F)})
BANK0 = {"pd": 0, "pr": 2, "pn": 3, "px": 4, "p4": 5, "pm": 7}
SEMAPHORES = ["qV", "qA", "qP", "qG"] + ["d%d" % _k for _k in range(90)]

CY, GA, SCT, PECY, HOP, PASSES = 0.83, 1.56, 3.8, 0.5, 100.0, 2


def _cells(ap):
    shape = SCRATCH[ap[0]][1]
    idx = ap[1] if isinstance(ap[1], tuple) else (ap[1],)
    return np.arange(int(np.prod(shape[1:]))).reshape(shape[1:])[idx[1:]].reshape(-1)


def copies(lo, hi):
    return 4 if hi - lo <= 128 else 2


def tag(ap):
    nm = ap[0].rstrip("012")
    if nm in ("val", "rec", "pw", "onc"):
        return "f%d" % (_cells(ap).min() // 64)
    if nm in ("sw", "hol", "th", "nd"):
        return "%s%d" % (nm, (_cells(ap).min() - 16 * (nm == "hol")) // 64)
    return nm


def spans(runs):
    out = []
    for lo, hi in sorted(runs):
        if out and out[-1][1] == lo:
            out[-1] = (out[-1][0], hi)
        else:
            out.append((lo, hi))
    return out


def build():
    ops = []
    lw, rd, bank, grp = {}, {}, {}, {}

    def add(q, fn, reads, writes, cost, kind="c", acc=None, after=None, lat=0.0, ind=False):
        me = len(ops)
        deps = set()
        banks = set()
        for ap, wr in [(a, False) for a in reads] + [(a, True) for a in writes]:
            nm = ap[0]
            if nm not in SCRATCH:
                continue
            cells = _cells(ap)
            size = int(np.prod(SCRATCH[nm][1][1:]))
            if nm not in lw:
                lw[nm] = np.full(size, -1)
                rd[nm] = []
            if nm in BANK0:
                banks.update(int(b) + BANK0[nm] for b in np.unique(cells // 512))
            if acc is not None and wr and not acc[0]:
                continue
            deps.update(int(w) for w in np.unique(lw[nm][cells]) if w >= 0)
            m = np.zeros(size, bool)
            m[cells] = True
            if wr:
                keep = []
                for o, om in rd[nm]:
                    if (om & m).any():
                        deps.add(o)
                        om = om & ~m
                    if om.any():
                        keep.append((o, om))
                rd[nm] = keep
                lw[nm][cells] = me
            else:
                rd[nm].append((me, m))
        for b in banks:
            e = bank.setdefault(b, [q, [], []])
            if e[0] != q:
                bank[b] = e = [q, [], e[1]]
            deps.update(e[2])
            e[1].append(me)
        if acc is not None:
            b = min(banks)
            if acc[0]:
                if b in grp:
                    deps.add(grp[b][-1])
                grp[b] = [me]
                grp[(b, "c")] = [writes[0]]
            else:
                deps.add(grp[b][0])
                if acc[1]:
                    deps.update(grp[b])
                grp[b].append(me)
                grp[(b, "c")].append(writes[0])
            if acc[1]:
                for ap in grp[(b, "c")]:
                    lw[ap[0]][_cells(ap)] = me
        deps.discard(me)
        ops.append({"q": q, "fn": fn, "deps": deps, "cost": cost, "kind": kind, "after": after, "lat": lat, "ind": ind,
                    "nm": (writes + reads)[0][0], "tag": tag((writes + reads)[0])})
        return me

    def n_of(ap):
        return len(_cells(ap))

    def A_(T, ap):
        if not isinstance(ap, tuple):
            return ap
        if len(ap) == 3:
            return T[ap[0]][ap[1]].indirect(T[ap[2][0]][ap[2][1]])
        return T[ap[0]][ap[1]]

    def parts(ap):
        return [ap[:2], ap[2]] if len(ap) == 3 else [ap]

    def vec(call, out, ins, mul=None, extra=(), after=None):
        reads = [p for a in ins for p in parts(a)] + [e for e in extra if isinstance(e, tuple)] + parts(out)[1:]
        if len(out) == 3:
            c = 50 + SCT * CY * n_of(ins[0])
        elif len(ins[0]) == 3:
            c = 50 + GA * CY * n_of(out)
        else:
            if mul is None:
                mul = 0.5 if all(SCRATCH[a[0]][2] in (B, H, U) for a in [out] + ins) else 1
            c = max(64, mul * n_of(out)) * CY
        return add("V", call, reads, [out[:2]], c, after=after, ind=len(out) == 3 or len(ins[0]) == 3)

    def v_copy(out, a):
        return vec(lambda g, T: g.vector.tensor_copy(A_(T, out), A_(T, a)), out, [a])

    def v_tt(out, a, b, op, after=None):
        return vec(lambda g, T: g.vector.tensor_tensor(A_(T, out), A_(T, a), A_(T, b), op), out, [a, b],
                   1 if a[0] in BANK0 or b[0] in BANK0 else 2, after=after)

    def v_ts(out, a, s1, op0, s2=None, op1=None):
        def call(g, T):
            if op1 is None:
                return g.vector.tensor_scalar(A_(T, out), A_(T, a), A_(T, s1), None, op0)
            return g.vector.tensor_scalar(A_(T, out), A_(T, a), A_(T, s1), A_(T, s2), op0, op1)
        return vec(call, out, [a], None, (s1, s2))

    def v_set(out, c):
        return add("V", lambda g, T: g.vector.memset(A_(T, out), c), [], [out], max(64, n_of(out) / 2) * CY)

    def v_tr(out, a):
        return vec(lambda g, T: g.vector.transpose(A_(T, out), A_(T, a)), out, [a])

    def v_scan(out, a, ini):
        return vec(lambda g, T: g.vector.tensor_tensor_scan(A_(T, out), A_(T, a), A_(T, a), A_(T, ini), AL.add, AL.max), out, [a], None, (ini,))

    def act(out, a, func, bias=0.0, scale=1.0):
        c = 65 + GA * CY * n_of(out) if len(a) == 3 else max(64, n_of(out)) * CY + 30

        def call(g, T):
            if func == AF.Copy:
                return g.scalar.activation(A_(T, out), A_(T, a), func, scale=A_(T, scale))
            return g.scalar.activation(A_(T, out), A_(T, a), func, bias=A_(T, bias), scale=A_(T, scale))
        return add("A", call, parts(a) + [x for x in (bias, scale) if isinstance(x, tuple)], [out], c, ind=len(a) == 3)

    def step(out, a, bias):
        return act(out, a, AF.Sigmoid, bias, 256.0)

    def mm(out, l, r, start, stop, after=None):
        return add("P", lambda g, T: g.tensor.matmul(A_(T, out), A_(T, l), A_(T, r), start, stop), [l, r], [out],
                   max(64, n_of(r)) * PECY * (4 if SCRATCH[r[0]][2] == F else 1), acc=(start, stop), after=after)

    def group(items, after=None):
        for k, (o, l, r) in enumerate(items):
            mm(o, l, r, k == 0, k == len(items) - 1, after)

    def g_iota(out, pat, base, cm):
        def call(g, T):
            if SCRATCH[out[0]][2] != I:
                return g.iota(A_(T, out), pat, base, cm, allow_small_or_imprecise_dtypes=True)
            return g.iota(A_(T, out), pat, base, cm)
        return add("G", call, [], [out], 130 + 2 * CY * n_of(out))

    def g_sel(out, a, pat, cmp, base, cm):
        return add("G", lambda g, T: g.affine_select(A_(T, out), A_(T, a), pat, cmp, 0.0, base, cm), [a], [out], 170 + 2 * CY * n_of(out))

    def dma(q, out, a, lat):
        return add(q, lambda g, T: {"S": g.sync, "A": g.scalar, "G": g}[q].dma_start(A_(T, out), A_(T, a)), [a], [out], 60.0, kind="dma", lat=lat)

    sent = [None]

    def send(src, c0, dst, d0, back, only=None, after=None):
        bs = only or (0, 1, 2)
        at = [64 * (2 - b if back else b) for b in bs]
        srcs = [(src, s_[:, c0 + a:c0 + a + 64]) for a in at]
        dsts = [(dst, s_[:, d0 + a:d0 + a + 64]) for a in at]
        sent[0] = me = add("G", (srcs, dsts, bs), srcs, [], CALL, kind="send", lat=FLY[0] + FLY[1] * len(bs), after=after)
        ops[me]["arr"] = [add("R", (bs, k), [], [dsts[k]], 0.0, kind="arr", after=me) for k in range(len(bs))]

    ID = ("wid", s_[:, 16:144])
    Z4096, Z1, ZY, ZD, ZR = 0, 1, 2, 3, 6
    B_CHK, B_T, B_2K, B_4K = range(4)
    C_W1, C_ROW, C_TH, C_W0, C_FL, C_HI, C_T3, C_DG, C_PAIR, C_E, C_K, C_KS, C_D, C_R = 0, 1, 2, 3, 4, 5, 6, 7, 8, 9, 17, 20, 23, 26
    FINE = 16384.0
    FIT = ("fb", s_[:, 0:4096])

    def zq(k, q):
        return ("zz", s_[:, k, 15 - q:143 - q])

    def bias(k):
        return ("cb", s_[0:1, 128 * k:128 * k + 128])

    def ones(n):
        return ("one", s_[0:1, 0:n])

    def col(k, p=128):
        return ("cols", s_[0:p, k:k + 1])

    def blocks(lo, hi):
        return ("p4", s_[:, lo // 32:hi // 32])

    def back(buf, lo, hi):
        return (buf, s_[:, 783 - lo:783 - hi:-1])

    dma("S", ("si", s_[:]), ("sr", s_[:]), 3000.0)
    a = dma("A", ("ui", s_[:]), ("u", s_[:]), 2200.0)
    b = dma("A", ("li", s_[:, VS:768]), ("lim", s_[:, VS:768]), 3700.0)
    dma("S", ("fb", s_[:]), ("fit", s_[:]), 7100.0)
    c = dma("A", ("li", s_[:, 0:VS]), ("lim", s_[:, 0:VS]), 7500.0)
    ops[b]["after"], ops[c]["after"] = a, b
    v_set(("one", s_[:]), 1.0)
    g_iota(("pi", s_[:]), [[-16, 8]], 0, 1)
    g_iota(("ph", s_[:]), [[1, 8]], 0, 0)
    v_set(("zz", s_[:, Z1, :]), 0.0)
    for z in ("zr", "ck", "r3", "pu"):
        v_set((z, s_[:]), 0.0)
    for k, c in enumerate((-45056.0, 2048.0 * FINE, 2048.0, 4096.0)):
        v_set(bias(k), c)
    v_set(("cb2", s_[:]), 67108864.0)
    v_set(("cb2", s_[0:1, :]), -28672.0)
    v_set(("ck", s_[:, 12:128:16]), 2048.0)
    g_sel(("wid", s_[:]), ("one", s_[:, 0:160]), [[1, 160]], AL.is_equal, -16, -1)
    g_sel(("z8", s_[:]), ("one", s_[0:8, 0:144]), [[1, 144]], AL.is_equal, -15, -16)
    g_sel(("b8w", s_[:]), ("one", s_[0:8, 0:128]), [[1, 8], [0, 16]], AL.is_equal, 0, -1)
    g_sel(("ev", s_[:]), ("one", s_[0:64, 0:144]), [[1, 144]], AL.is_equal, -16, -2)
    g_sel(("blk0", s_[:]), ("one", s_[:, 0:128]), [[-16, 8], [0, 16]], AL.is_ge, 0, 1)
    g_sel(("blk", s_[:]), ("blk0", s_[:]), [[16, 8], [0, 16]], AL.is_ge, 15, -1)
    g_sel(("up", s_[:]), ("blk", s_[:]), [[1, 128]], AL.is_equal, 1, -1)
    g_iota(("ir", s_[:, 0, 16:784]), [[-32, 24], [0, 32]], 736, 0)
    g_iota(("ir", s_[:, 1, 16:784]), [[0, 24], [-1, 32]], 31, 0)
    first = [k for k, o in enumerate(ops) if o["q"] == "G"]
    for a, b in zip(first, first[1:]):
        ops[b]["after"] = a
    v_set(("zr", s_[:, 15:144:16]), 1.0)
    v_set(("ck", s_[:, 3:128:16]), 997.0)
    v_set(("ck", s_[:, 5:128:16]), 1994.0)
    v_ts(("pg", s_[:]), ("pi", s_[:]), 4, AL.arith_shift_right)
    v_ts(("pb", s_[:, 0:1]), ("pi", s_[:, 0:1]), 4, AL.arith_shift_right, 1, AL.bitwise_and)
    v_ts(("pb", s_[:, 1:2]), ("pi", s_[:, 0:1]), 15, AL.bitwise_and)
    v_ts(("pb", s_[:, 2:3]), ("pi", s_[:, 0:1]), 7, AL.bitwise_and)
    v_ts(("pb", s_[:, 3:4]), ("pi", s_[:, 0:1]), 1, AL.arith_shift_right, 7, AL.bitwise_and)
    v_copy(col(C_ROW), ("pb", s_[:, 1:2]))
    v_ts(col(C_W1), ("pb", s_[:, 0:1]), FINE, AL.mult)
    v_ts(col(C_W0), ("pb", s_[:, 0:1]), 0.0, AL.is_equal, FINE, AL.mult)
    v_ts(col(C_TH), ("pb", s_[:, 1:2]), -256.0, AL.mult, 128.0, AL.add)
    v_ts(col(C_FL), ("pb", s_[:, 2:3]), 256.0 * 997, AL.mult, -256.0 * 2047.5, AL.add)
    v_ts(col(C_HI), ("pb", s_[:, 2:3]), 997.0, AL.mult)
    v_ts(col(C_T3), ("pb", s_[:, 2:3]), 3.0, AL.is_lt)
    v_copy(col(C_PAIR), ("pb", s_[:, 3:4]))

    def cols(k, n):
        return ("cols", s_[:, k:k + n])
    v_ts(cols(C_E, 8), ("ph", s_[:]), col(C_PAIR), AL.is_equal)
    v_ts(cols(C_K, 3), cols(C_E, 3), col(C_E + 6), AL.add)
    v_ts(cols(C_KS, 3), cols(C_E, 3), col(C_E + 6), AL.add, 1 / FINE, AL.mult)
    v_tt(cols(C_D, 2), cols(C_E + 3, 2), cols(C_KS + 1, 2), AL.add)
    v_tt(cols(C_R, 3), cols(C_E + 3, 3), cols(C_KS, 3), AL.add)
    v_ts(("zz", s_[:, Z1, 15:128:16]), ("pg", s_[:]), 0.0, AL.is_equal)
    act(("zz", s_[:, Z4096, :]), ("zz", s_[:, Z1, :]), AF.Copy, scale=4096.0)
    U16 = ("u16", s_[:, 16:784])
    v_ts(("u16", s_[:, 16 + VS:784]), ("ui", s_[:, VS:768]), -2048.0, AL.add)
    v_ts(("u16", s_[:, 16:16 + VS]), ("ui", s_[:, 0:VS]), -2048.0, AL.add)
    act(("w0", s_[:]), ("wid", s_[:]), AF.Copy, scale=col(C_W0))
    act(("w1", s_[:]), ("wid", s_[:]), AF.Copy, scale=col(C_W1))
    act(("nid", s_[:]), ID, AF.Copy, scale=-1.0)
    act(("bigi", s_[:]), ID, AF.Copy, scale=-32768.0)
    for t in range(RO):
        ops[step(("r3", s_[:, t:64:8]), ("wid", s_[0:8, 16:24]), -128.0)]["cost"] += 1300.0 * (t == 0)
        act(("pu", s_[:, 2 * t + 1:128:16]), ("wid", s_[0:8, 16:24]), AF.Copy)
    act(("n4k", s_[:]), ("wid", s_[0:64, 16:80]), AF.Copy, scale=-4096.0)

    HALVES = ((0, 512), (512, 768))
    for lo, hi in HALVES:
        mm(("pd", s_[0:64, lo:hi]), ("r3", s_[:]), back("u16", lo, hi), True, True)
    step(("flag", s_[:]), ("pd", s_[0:64, 0:768]), col(C_FL, 64))
    for lo, hi in HALVES:
        o = ("pd", s_[0:64, lo:hi])
        group([(o, ("r3", s_[:]), back("u16", lo, hi)), (o, ("n4k", s_[:]), ("flag", s_[:, lo:hi]))])
    act(("hi", s_[:]), ("pd", s_[0:64, 0:768]), AF.Identity, bias=col(C_HI, 64))

    def t_stage(runs, v, after=None):
        nb = sum(hi - lo for lo, hi in runs)
        for k0 in range((nb + 15) // 16):
            a0, a1 = 16 * k0, min(nb, 16 * k0 + 16)
            items = [(("p4", s_[:, a0:a1]), bias(B_T), ones(32 * (a1 - a0)))]
            at = 0
            for lo, hi in runs:
                x0, x1 = max(at, a0), min(at + hi - lo, a1)
                for b in range(2):
                    for x in range(2):
                        c0 = 16 + 16 * (b - x)
                        if x1 > x0:
                            items.append((("p4", s_[:, x0:x1, b, :]), ("w%d" % b, s_[:, c0:c0 + 128]),
                                          ("t0", s_[:, lo + x0 - at:lo + x1 - at, x, :])))
                at += hi - lo
            group(items, after)
        for i in range(16):
            v_tt(("pq", s_[:, i, 0:2 * nb]), ("p4", s_[:, 0:nb, :, i]), (v, s_[:, 0:2 * nb]), AL.mult)

    def cut(out, a):
        v_ts(out, a, 5, AL.arith_shift_right, 4095, AL.bitwise_and)

    def narrow(out, a, ong):
        if ong:
            g_sel(out, a, [[0, n_of(out)]], AL.is_ge, 0, 0)
        else:
            v_copy(out, a)

    def t_offsets(out, m0, m1, ong=False):
        a = ("pq", s_[:, :, m0:m1])
        cut(a, a)
        narrow(out, a, ong)

    def n_offsets(out, s, v, lo, hi, ong=False):
        c = s_[:, lo:hi]
        v_tt(("pw", c), (s, c), v, AL.mult)
        cut(("pw", c), ("pw", c))
        narrow((out, c), ("pw", c), ong)

    ring, unit, held, tail = [0], [0], [], [None]

    def line(k):
        ops[k]["after"] = tail[0]
        tail[0] = k

    def on_vector(at):
        return [k for k in range(at, len(ops)) if ops[k]["q"] == "V"]

    def flush():
        while held:
            line(held.pop(0))

    def scalar_run(off, lo, hi, lim, out, first, ahead=True, direct=0, lp=None):
        n = hi - lo
        at = ring[0]
        ring[0] += 16 * n
        if not ahead:
            flush()
        line(act(("fc", s_[:, at:at + 16 * n]), FIT + ((off, s_[:, lo:hi]),), AF.Copy))
        flush()
        for k, (l, r) in enumerate(first):
            mm(out, l, r, k == 0, False)
        per = 8
        if direct:
            if lp is None:
                lp = ("pm", s_[:, 0:n])
                mm(lp, ID, (lim, s_[:, lo:hi]), True, True)
            for i in range(16 - direct, 16):
                v_tt(("cc", s_[:, at + n * i:at + n * i + n]), ("fc", s_[:, at + i:at + 16 * n:16]), lp, AL.is_gt)
                mm(out, zq(Z4096, i), ("cc", s_[:, at + n * i:at + n * i + n]), False, direct == 16 and i == 15)
        for i0 in range(0, 16 - direct, per):
            pb, base = "pd", 512 * (unit[0] % 2)
            unit[0] += 1
            for j in range(per):
                o = (pb, s_[:, base + n * j:base + n * j + n])
                group([(o, ID, ("fc", s_[:, at + i0 + j:at + 16 * n:16])), (o, ("nid", s_[:]), (lim, s_[:, lo:hi]))])
            o, a = ("cc", s_[:, at + n * i0:at + n * (i0 + per)]), (pb, s_[:, base:base + n * per])
            held.append(step(o, a, -128.0))
            for i in range(i0, i0 + per):
                mm(out, zq(Z4096, i), ("cc", s_[:, at + n * i:at + n * i + n]), False, i == 15 - direct)

    chain = [None]

    def vector_run(off, cmp, c0, lim, out, first):
        n = n_of(out)
        r, m = n_of(lim) // n, n // 16
        for k, (l, x) in enumerate(first):
            mm(out, l, x, k == 0, False)
        for i0 in range(0, 16, r):
            o = (off[0], s_[:, off[1] + m * i0:off[1] + m * (i0 + r)])
            chain[0] = v_tt((cmp, s_[:, c0 + n * i0:c0 + n * (i0 + r)]), FIT + (o,), lim, AL.is_gt, chain[0])
            for i in range(i0, i0 + r):
                mm(out, zq(Z4096, i), (cmp, s_[:, c0 + n * i:c0 + n * i + n]), False, i == 15)

    nini = [0]

    def banked(r0, r1):
        cuts = [r0] + [c for c in (384, 704) if r0 < c < r1] + [r1]
        return [(a, b, ("pn", s_[:, 0:b - a]) if a >= 704 else blocks(a + 128 * (a >= 384), b + 128 * (a >= 384)))
                for a, b in zip(cuts, cuts[1:])]

    def classes(r0, r1, src, onv):
        for a, b, o in banked(r0, r1):
            mm(o, ("blk", s_[:]), src(a, b), True, True)
            if onv:
                v_ts(("th", s_[:, a:b]), o, col(C_ROW), AL.is_ge)
            else:
                step(("th", s_[:, a:b]), o, col(C_TH))

    def ranks(r0, r1, on, more):
        c = s_[:, r0:r1]
        v_scan(("cum", c), ("th", c), ("ini", s_[:, nini[0] % 8:nini[0] % 8 + 1]) if on else 0.0)
        if more:
            nini[0] += 1
            v_copy(("ini", s_[:, nini[0] % 8:nini[0] % 8 + 1]), ("cum", s_[:, r1 - 1:r1]))
        for a, b, o in banked(r0, r1):
            group([(o, ("d1b", s_[:]), ("th", s_[:, a:b])), (o, ("d1", s_[:]), ("cum", s_[:, a:b]))])

    def select(cutp):
        e1, e2 = ("cum", s_[:, cutp - 1:cutp]), ("cum", s_[:, 767:768])
        for k in range(2):
            o = ("pn", s_[:, 500 + k:501 + k])
            group([(o, ("up", s_[:]), e1), (o, ("up", s_[:]), e2)] + [(o, ("d1", s_[:]), e1)] * k)
        v_ts(("off2", s_[:]), ("pn", s_[:, 500:502]), -2048.0, AL.add)
        for r0, r1, k in ((0, cutp, 0), (cutp, 768, 1)):
            for a, b, o in banked(r0, r1):
                c = ("cm", s_[:, a + 768:b + 768] if b <= 192 else s_[:, a:b])
                if 384 <= a < 704:
                    act(c, o, AF.Relu, bias=("off2", s_[:, k:k + 1]))
                else:
                    v_ts(c, o, ("off2", s_[:, k:k + 1]), AL.add, 0.0, AL.max)

    def mark(lo, hi, onv):
        if onv:
            v_ts(("hol", s_[:, 16 + lo:16 + hi]), ("sw", s_[:, lo:hi]), 4096.0, AL.is_ge)
        else:
            step(("hol", s_[:, 16 + lo:16 + hi]), ("sw", s_[:, lo:hi]), -256.0 * 4095.5)

    def holes(lo, hi, p, s, onv):
        if lo in FLAG:
            v_ts(("hol", s_[:, 16 + lo:16 + hi]), p, 4096.0, AL.is_ge)
        v_tt(("sw", s_[:, lo:hi]), p, s, AL.max)
        if lo not in FLAG:
            mark(lo, hi, onv)

    def start(lo, hi, s):
        if lo not in FLAG:
            return [(bias(B_CHK), ones(hi - lo))]
        v_ts(("old", s_[:, lo:hi]), s, 4096.0, AL.is_ge, -2.0, AL.mult)
        return [(bias(B_CHK), ones(hi - lo)), (("bigi", s_[:]), ("old", s_[:, lo:hi]))]

    def hol_back(a, b):
        return back("hol", a, b)

    def hol_on(a, b):
        return ("hol", s_[:, 400 + a:400 + b])

    def checks(plan_, lists, lim, s, offsets, donors, onv, scans):
        for k, runs in enumerate(plan_):
            pb = "pr" if (len(plan_) - k) % 2 else "px"
            for lo, hi in runs:
                for a, b in lists:
                    if b == hi:
                        offsets(a, b)
                scalar_run("onc", lo, hi, lim, (pb, s_[:, lo:hi]), start(lo, hi, (s, s_[:, lo:hi])), (lo, hi) != plan_[0][0],
                           16 if lo == 0 else 0)
            if k == 0:
                donors[0]()
            lo, hi = min(r[0] for r in runs), max(r[1] for r in runs)
            holes(lo, hi, (pb, s_[:, lo:hi]), (s, s_[:, lo:hi]), onv[k + 1][0])
            classes(768 - hi, 768 - lo, hol_back, onv[k + 1][1])
            for a, b in zip(scans, scans[1:]):
                if 768 - hi < b <= 768 - lo:
                    ranks(a, b, a > scans[0], b < 768)
            if k == 0:
                donors[1]()
                ranks(0, scans[0], False, False)
        select(scans[0])
        flush()

    group([(("pn", s_[:, 0:NV0]), ("z8", s_[:, 15 - q:143 - q]), ("u16", s_[:, 16 + VS + q:784:16])) for q in range(16)])
    act(("vt", s_[:, 0:NV0]), ("pn", s_[:, 0:NV0]), AF.Identity, bias=2048.0 / FINE, scale=1 / FINE)
    o = ("pm", s_[:, 128:128 + VS])
    group([(o, bias(B_2K), ones(VS)), (o, ("b8w", s_[:]), ("u16", s_[:, 16:16 + VS]))])
    v_ts(("sn0", s_[:]), ("si", s_[:, VS:768]), -2048.0, AL.add)
    v_tr(("t0", s_[:, 0:NV0 // 2]), ("sn0", s_[:]))
    narrow(("lim0", s_[:, 0:VS]), ("li", s_[:, 0:VS]), True)
    v_copy(("rep0", s_[:, 0:768 - VS]), ("li", s_[:, VS:768]))
    v_copy(("rep0", s_[:, 768 - VS:2 * (768 - VS)]), ("rep0", s_[:, 0:768 - VS]))
    dma("S", ("lim0", s_[:, VS:768]), ("rep0", s_[:, 0:768 - VS]), 2500.0)
    t_stage([(0, NV0 // 2)], "vt")
    t_offsets(("off0", s_[:]), 0, NV0)
    o = ("px", s_[0:64, 0:128])
    group([(o, ("wid", s_[0:64, 16:80]), ("ev", s_[:, 16:144])), (o, ("nid", s_[0:64, 0:64]), ("ev", s_[:, 15:143]))])
    o = ("px", s_[0:64, 128:256])
    mm(o, ("n4k", s_[:]), ("ev", s_[:, 15:143]), True, True)
    act(("phi", s_[:]), ("px", s_[0:64, 0:128]), AF.Copy, scale=col(C_T3, 64))
    act(("pfl", s_[:]), ("px", s_[0:64, 128:256]), AF.Copy, scale=col(C_T3, 64))
    o = ("pr", s_[:, 384:512])
    group([(o, ID, ID), (o, ("nid", s_[:]), ("up", s_[:]))])
    act(("d1", s_[:]), ("pr", s_[:, 384:512]), AF.Copy)
    act(("d1b", s_[:]), ("pr", s_[:, 384:512]), AF.Copy, scale=2048.0)

    def digits(t):
        return [("zr", s_[:, 9 - 2 * t - k:137 - 2 * t - k]) for k in range(2)]
    for lo, hi in HALVES:
        o = blocks(lo, hi)
        group([(o, ("pu", s_[:]), back("u16", lo, hi)), (o, ("pfl", s_[:]), ("flag", s_[:, lo:hi])), (o, ("phi", s_[:]), ("hi", s_[:, lo:hi])),
               (o, ("ck", s_[:]), ones(hi - lo))] + [(o, z, ("ir", s_[:, k, 16 + lo:16 + hi])) for k, z in enumerate(digits(0))])
    act(("meta0", s_[:]), blocks(0, 768), AF.Copy)

    def donors0():
        vector_run(("off0", 0), "cv", 0, ("rep0", s_[:]), ("pn", s_[:, 0:768 - VS]), [(bias(B_CHK), ones(768 - VS))])

    def donors1():
        holes(VS, 768, ("pn", s_[:, 0:768 - VS]), ("si", s_[:, VS:768]), ONV0[0][0])
        classes(0, 768 - VS, hol_back, ONV0[0][1])
    checks(CHK0, LIST0, "lim0", "si", lambda lo, hi: n_offsets("onc", "si", ("pm", s_[:, 128 + lo:128 + hi]), lo, hi, lo == 0), (donors0, donors1), ONV0, SCAN0)
    for k, c in ((ZD, C_D), (ZR, C_R)):
        line(act(("zz", s_[:, k, :]), ("zz", s_[:, Z1, :]), AF.Copy, scale=col(c)))
    for t in range(RO):
        line(act(("bk", s_[:, t, :]), ("blk", s_[:]), AF.Copy, scale=col(C_K + t)))
    for k, c in ((ZD + 1, C_D + 1), (ZD + 2, C_E + 5), (ZR + 1, C_R + 1), (ZR + 2, C_R + 2), (ZY, C_K)):
        line(act(("zz", s_[:, k, :]), ("zz", s_[:, Z1, :]), AF.Copy, scale=col(c)))
    line(act(("idf", s_[:]), ID, AF.Copy))

    SW = ("sw", s_[:, 0:768])
    for t in range(RO):
        last = t == RO - 1
        ms, limn = "ms%d" % t, "lim%d" % (t + 1)
        LW = ("lim%d" % t, s_[:, 0:768])
        ring[0] = 0
        X = ("pm", s_[:, 0:48])
        group([(X, zq(Z1, q), ("cm", s_[:, 192 + q:960:16] if t else s_[:, q:768:16])) for q in range(16)])
        v_ts(("plc", s_[:]), X, -1.0, AL.add)
        WIN = (ms, s_[:, 16:784], ("plc", s_[:]))
        if t == 0:
            v_copy(WIN, ("meta0", s_[:]))
            for o, src in ((blocks(0, 192), s_[207:15:-1]), (blocks(512, 896), s_[400:784]), (blocks(192, 384), s_[399:207:-1])):
                group([(o, z, ("ir", s_[:, k, src])) for k, z in enumerate(digits(1))])
            act(("ai1", s_[:, 0:192]), blocks(0, 192), AF.Copy)
            act(("ai1", s_[:, 576:768]), blocks(192, 384), AF.Copy)
            act(("ai1", s_[:, 192:576]), blocks(512, 896), AF.Copy)
            dma("S", ("ai2", s_[2:128, :]), ("ai1", s_[0:126, :]), 2500.0)
            dma("S", ("ai2", s_[0:2, :]), ("ai1", s_[0:2, :]), 2500.0)
        else:
            v_tt(WIN, ("ms%d" % (t - 1), s_[:, 208:976]), ("ai%d" % t, s_[:]), AL.add)
        robv, robs = ROBV[t], ROBS[t]
        nr = 48 if last else 24

        def fwd(q, lo, hi):
            return (ms, s_[:, 16 + lo + q:16 + hi:16])

        def rev(q, lo, hi):
            return (ms, s_[:, 783 - lo - q:783 - hi:-16])
        group([(("pm", s_[:, 48:72]), zq(ZD + t, q), fwd(q, 0, 384)) for q in range(16)])
        ld_done = len(ops) - 1
        v_copy(("ld", s_[:]), ("pm", s_[:, 48:72]))

        def keys_t(m, p, lo, hi):
            a, c = (p, s_[:, lo:hi]), s_[:, m:m + hi - lo]
            v_copy(("vi", c), a)
            v_tt(("vt", c), a, ("vi", c), AL.subtract)

        def keys_n(o, k, lo, hi):
            mm(o, ("bk", s_[:, k, :]), back(ms, lo, hi), True, True)
        m = 0 if last else 24
        if not last:
            keys_t(0, "pm", 48, 72)
        for lo, hi in spans(robs):
            keys_n(("pr", s_[:, lo:hi]), t, lo, hi)
        group([(("px", s_[:, 0:nr]), zq(ZR + t, q), rev(q, 0, 16 * nr)) for q in range(16)], ld_done)
        v_copy(("lr", s_[:, 0:nr]), ("px", s_[:, 0:nr]))
        tcol = {}
        for lo, hi in spans(robv):
            keys_t(m, "px", lo // 16, hi // 16)
            tcol.update({k: m + (k - lo) // 16 for k in range(lo, hi, 16)})
            m += (hi - lo) // 16
        if not last:
            keys_n(("pm", s_[:, 128:512]), t + 1, 0, 384)

        def pick(out, c0, win, lst, lo, hi):
            return act((out, s_[:, c0 + lo:c0 + hi]), win + ((lst, s_[:, lo // 16:hi // 16]),), AF.Copy)

        def rob_first(lo, hi):
            return [(("cb2", s_[:]), ("one", s_[0:2, 0:hi - lo])), (("bigi", s_[:]), ("have", s_[:, lo:hi]))]
        rec = "ys" if last else "rec"

        def settle(pb, lo, hi):
            c = s_[:, lo:hi]
            v_tt(("val", c), (pb, c), ("g32", c), AL.max)
            v_tt((rec, c), blocks(lo, hi), ("val", c), AL.min)

        def donors_left(lo, hi):
            v_tt(("ys", s_[:, 767 - lo:767 - hi:-1]) if last else ("nd%d" % t, s_[:, lo:hi]), blocks(512 + lo, 512 + hi), (rec, s_[:, lo:hi]), AL.subtract)

        def serials(out, lst, lo, hi):
            return v_ts((out, s_[:, lo:hi]), SW + ((lst, s_[:, lo // 16:hi // 16]),), 4096.0, AL.min, -2048.0, AL.add)

        def sums(lo, hi):
            group([(blocks(lo, hi), bias(B_2K), ones(hi - lo)), (blocks(lo, hi), ID, ("have", s_[:, lo:hi]))])
            o = blocks(512 + lo, 512 + hi)
            group([(o, bias(B_2K), ones(hi - lo)), (o, ID, ("have", s_[:, lo:hi])), (o, ("idf", s_[:]), ("g32", s_[:, lo:hi]))])
        if last:
            send(ms, 16, ms, 784, True)

            def v_pick(out, c0, lo, hi):
                return v_copy((out, s_[:, c0 + lo:c0 + hi]), LW + (("lr", s_[:, lo // 16:hi // 16]),))
            at = len(ops)
            for lo, hi in ALLN:
                v_ts(("g32", s_[:, lo:hi]), SW + (("ld", s_[:, lo // 16:hi // 16]),), 4096.0, AL.min)
                n_offsets("onr", "g32", ("pr", s_[:, lo:hi]), lo, hi)
            first = on_vector(at)[:FIRST]
            for a, b in zip(first, first[1:]):
                ops[b]["after"] = a
            begin = at
            for lo, hi in ((0, 192), (192, 384)):
                second = v_pick(limn, 0, lo, hi) - 1
                mm(("pd", s_[:, lo + 320 * (lo > 0):hi + 320 * (lo > 0)]), ("idf", s_[:]), (limn, s_[:, lo:hi]), True, True)
                ops[serials("have", "lr", lo, hi)]["after"] = first[3]
            for k in on_vector(at)[4:]:
                if ops[k]["ind"] and ops[k]["after"] is None:
                    ops[k]["after"] = first[3]
            sums(0, 192)
            ops[v_pick("lo2", -576, 576, 768)]["after"] = first[3]
            send("lo2", 0, limn, 576, False)
            v_pick(limn, 0, 384, 576)
            dma("S", ("ylim", s_[:, 0:384]), (limn, s_[:, 0:384]), 2200.0)
            gone = []
            for k, (lo, hi) in enumerate(robs):
                pb = ("pn", "px")[k % 2]
                at = lo + 320 * (lo >= 192)
                scalar_run("onr", lo, hi, limn, (pb, s_[:, lo:hi]), rob_first(lo, hi), direct=16, lp=("pd", s_[:, at:at + hi - lo]))
                settle(pb, lo, hi)
                donors_left(lo, hi)
                gone.append((128 - lo) // 64)
                for bs in GO:
                    if gone[-1] in bs and all(x in gone for x in bs):
                        send("ys", 576, "yin", 0, False, bs)
                if k == 2:
                    for x in on_vector(begin):
                        if ops[x]["ind"] and ops[x]["tag"] in ("lim3", "have") and x > second:
                            ops[x]["after"] = on_vector(begin)[LATE]
                    sums(192, 384)
                    dma("S", ("ysr", s_[:, 0:192]), ("ys", s_[:, 0:192]), 2000.0)
            break
        first, later = [serials("give", "ld", 0, 384)], []
        first.append(v_tr(("t0", s_[:, 0:12]), ("give", s_[:])))
        (a, b), = spans(robs)
        line(pick("g32", 0, SW, "ld", a, b))
        n_offsets("onr", "g32", ("pr", s_[:, a:b]), a, b)
        first += range(len(ops) - 3, len(ops))
        line(pick("lo%d" % t, 0, LW, "ld", 0, 192))
        send("lo%d" % t, 0, limn, 384, True)
        line(pick(limn, 0, LW, "lr", a, b))
        for k, (a, b) in enumerate(robv):
            (held.append if k else line)(pick("repr", 3 * a, LW, "lr", a, b))
            if k == 0:
                held.append(pick("g32", 0, SW, "ld", a, b))
            for w in [(b - a) * r for r in (1, 2) if r < copies(a, b)]:
                v_copy(("repr", s_[:, 4 * a + w:4 * a + 2 * w]), ("repr", s_[:, 4 * a:4 * a + w]))
            dma("S", (limn, s_[:, a:b]), ("repr", s_[:, 4 * a:3 * a + b]), 2500.0)
        for a, b in spans(robv[1:]):
            later.append(pick("g32", 0, SW, "ld", a, b))
        later.append(pick("repd", -192, LW, "ld", 192, 384))
        for k in range(1, REPD):
            dma("S", ("repd", s_[:, 192 * k:192 * k + 192]), ("repd", s_[:, 0:192]), 2500.0)
        dma("S", (limn, s_[:, 576:768]), ("repd", s_[:, 0:192]), 2500.0)
        for k in range(REPA):
            dma("S", ("repa", s_[:, 192 * k:192 * k + 192]), (limn, s_[:, 384:576]), 2500.0)
        t_stage([(0, 12)] + [(lo // 32, hi // 32) for lo, hi in spans(robv)], "vt", ld_done)
        first += range(len(ops) - 16, len(ops))
        for lo, hi in robv:
            t_offsets(("offr", s_[:, lo:hi]), tcol[lo], tcol[lo] + (hi - lo) // 16)
            if lo == robv[0][0]:
                first += range(len(ops) - 2, len(ops))
        for a, b in zip(first, first[1:]):
            ops[b]["after"] = a
        chain[0] = first[-1]
        for b in range(3):
            cut(("osd%d" % t, s_[:, 64 * b:64 * b + 64]), ("pq", s_[:, :, 4 * b:4 * b + 4]))
        send("osd%d" % t, 0, "oin%d" % t, 0, True)
        t_offsets(("offd", s_[:]), 12, 24, True)
        send(ms, 16, ms, 784, True, None, sent[0])
        ops[serials("have", "lr", 0, 384)]["after"] = first[-1]
        group([(blocks(0, 384), bias(B_2K), ones(384)), (blocks(0, 384), ID, ("have", s_[:]))])
        o = blocks(512, 896)
        group([(o, bias(B_4K), ones(384)), (o, ID, ("have", s_[:])), (o, ID, ("give", s_[:]))])
        for k, (lo, hi) in enumerate(robs):
            pb = ("pn", "pr")[k % 2]
            scalar_run("onr", lo, hi, limn, (pb, s_[:, lo:hi]), rob_first(lo, hi))
            if k == len(robs) - 1:
                held[0:0] = later
            settle(pb, lo, hi)
            lo, hi = robv[k]
            vector_run(("offr", lo), "cr", 16 * lo, ("repr", s_[:, 4 * lo:4 * lo + copies(lo, hi) * (hi - lo)]), ("px", s_[:, lo:hi]), rob_first(lo, hi))
            settle("px", lo, hi)
        donors_left(0, 192)
        send("nd%d" % t, 0, "sin%d" % t, 0, True)
        donors_left(192, 384)

        def donors():
            vector_run(("offd", 0), "cv", 0, ("repd", s_[:, 0:192 * REPD]), ("pn", s_[:, 192:384]), [(bias(B_CHK), ones(192))])
            holes(576, 768, ("pn", s_[:, 192:384]), ("nd%d" % t, s_[:, 192:384]), ONVD[0])
            classes(192, 384, hol_on, ONVD[1])
            for b in range(3):
                narrow(("offb", s_[:, :, 4 * b:4 * b + 4]), ("oin%d" % t, s_[:, 64 * b:64 * b + 64]), True)
            narrow(("offa", s_[:]), ("offb", s_[:]), True)
            vector_run(("offa", 0), "cv", 3072, ("repa", s_[:, 0:192 * REPA]), ("pn", s_[:, 0:192]), start(384, 576, ("sin%d" % t, s_[:])))

        def arrived():
            holes(384, 576, ("pn", s_[:, 0:192]), ("sin%d" % t, s_[:]), ONV[0][0])
            classes(0, 192, hol_on, ONV[0][1])

        def lists(lo, hi):
            n_offsets("onc", "rec", ("pm", s_[:, 128 + lo:128 + hi]), lo, hi, lo == 0)
        checks(CHK, LISTV, limn, "rec", lists, (donors, arrived), ONV, SCAN)
    yp = ("pm", s_[:, 0:48])
    group([(yp, zq(ZY, k), back("ms2", 48 * k, 48 * k + 48) if k < 12 else ("ms2", s_[:, 1551 - 48 * k:1503 - 48 * k:-1])) for k in range(16)])
    act(("yub", s_[:]), yp, AF.Copy)
    dma("S", ("ylim", s_[:, 384:768]), ("lim3", s_[:, 384:768]), 2200.0)
    dma("S", ("ysr", s_[:, 576:704]), ("yin", s_[:, 0:128]), 1800.0)
    dma("A", ("yu", s_[:]), ("yub", s_[:]), 1800.0)
    dma("A", ("ysr", s_[:, 192:320]), ("ys", s_[:, 192:320]), 1800.0)
    dma("S", ("ysr", s_[:, 704:768]), ("yin", s_[:, 128:192]), 1800.0)
    dma("A", ("ysr", s_[:, 448:576]), ("ys", s_[:, 448:576]), 1800.0)
    dma("A", ("ysr", s_[:, 320:448]), ("ys", s_[:, 320:448]), 1800.0)
    return ops


def lay_out(ops):
    n = len(ops)
    pre = [set(o["deps"]) | ({o["after"]} if o["after"] is not None else set()) for o in ops]
    prev = {}
    for k, o in enumerate(ops):
        if o["q"] == "S":
            if o["q"] in prev:
                pre[k].add(prev[o["q"]])
            prev[o["q"]] = k
    users = [[] for _ in ops]
    for k, p in enumerate(pre):
        for d in p:
            users[d].append(k)

    def delay(k, u):
        if k not in ops[u]["deps"] and ops[u]["kind"] != "arr":
            return 0.0
        return ops[k]["lat"] + (0.0 if ops[k]["q"] == ops[u]["q"] == "P" else HOP)
    ahead = [[(u, delay(k, u)) for u in users[k]] for k in range(n)]
    behind = [[(d, delay(d, k)) for d in pre[k]] for k in range(n)]

    def place(nxt, deg, key, first, slack):
        left, ready, start, seq = list(deg), list(first), [0.0] * n, []
        free = {q: 0.0 for q in "VAPGSR"}
        loose = set(k for k in range(n) if left[k] == 0)
        while loose:
            k = min(loose, key=lambda c: (max(ready[c], free[ops[c]["q"]]), c))
            q = ops[k]["q"]
            t = max(ready[k], free[q]) + 0.01
            k = min((c for c in loose if ops[c]["q"] == q and ready[c] <= t + slack[c]), key=lambda c: (key[c], c))
            loose.discard(k)
            t, c = max(ready[k], free[q]), ops[k]["cost"]
            free[q] = t + c
            start[k] = t
            seq.append(k)
            for u, d in nxt[k]:
                ready[u] = max(ready[u], t + c + d)
                left[u] -= 1
                if left[u] == 0:
                    loose.add(u)
        return start, seq
    key = [-float(k) for k in range(n)]
    for p in range(PASSES):
        st, seq = place(behind, [len(u) for u in users], key, [o["lat"] for o in ops], [0.0] * n)
        late = [-st[k] - o["cost"] - (1e6 if o["nm"] in EARLY else 0.0) for k, o in enumerate(ops)]
        st, seq = place(ahead, [len(p) for p in pre], late, [0.0] * n, [0.0] * n)
        key = [-st[k] - ops[k]["cost"] for k in range(n)]
    return place(ahead, [len(p) for p in pre], [late[k] - AHEAD_BY.get(o["q"] + o["tag"], 0.0) for k, o in enumerate(ops)], [0.0] * n,
                 [WAIT_FOR.get(o["q"] + o["tag"], 0.0) for o in ops])[1]


def plan():
    ops = build()
    order = lay_out(ops)
    pos = {k: j for j, k in enumerate(order)}
    known = {}
    for k in order:
        o = ops[k]
        o["waits"] = []
        if o["kind"] == "arr":
            o["clock"] = {}
            continue
        kn = known.setdefault(o["q"], {})
        for d in sorted(o["deps"], key=lambda x: -pos[x]):
            e = ops[d]
            key = e["q"] if e["kind"] == "c" else d
            if o["q"] == e["q"] == "P" or kn.get(key, -1) >= pos[d]:
                continue
            o["waits"].append(d)
            e["sig"] = True
            kn[key] = pos[d]
            for a, b in e["clock"].items():
                if kn.get(a, -1) < b:
                    kn[a] = b
        o["clock"] = dict(kn)
    cnt, nd = {}, 0
    for k in order:
        o = ops[k]
        if o["kind"] == "c":
            if o.get("sig"):
                cnt[o["q"]] = cnt.get(o["q"], 0) + 1
                o["sem"], o["n"] = "q" + o["q"], cnt[o["q"]]
        else:
            o["sem"] = "d%d" % nd
            nd += 1
    return ops, order


PLAN = []


def engine_sets(topo, src, dsts):
    can = [topo.engines(src, d) for d in dsts]
    pool = [e for e in can[0] if all(e in c for c in can)]
    out = [None] * len(dsts)
    for k, c in enumerate(can):
        own = [e for e in c if e not in pool and not any(o and e in o for o in out)]
        if own:
            out[k] = own
    rest = [k for k in range(len(dsts)) if out[k] is None]
    for j, k in enumerate(rest):
        left = len(rest) - j
        n = 1
        while (left + 1) * n <= len(pool):
            n *= 2
        out[k], pool = pool[:n], pool[n:]
    return out


def rank_program(g, core, T, topo):
    rank = T.rank_of(core)
    if rank is None:
        return
    if not PLAN:
        PLAN.append(plan())
    ops, order = PLAN[0]
    cores = T.cores

    def sets(r, bs):
        return engine_sets(topo, cores[r], [cores[(r + 1 + b) % N] for b in bs])
    Q = {"V": g.vector, "A": g.scalar, "P": g.tensor, "G": g, "S": g.sync}

    def full(o):
        if o["kind"] == "c":
            return o["n"]
        if o["kind"] == "dma":
            return 16
        if o["kind"] == "send":
            return sum(len(e) for e in sets(rank, o["fn"][2]))
        bs, j = o["fn"]
        return len(sets((rank - 1 - bs[j]) % N, bs)[j])
    for k in order:
        o = ops[k]
        if o["kind"] == "arr":
            continue
        for d in o["waits"]:
            Q[o["q"]].wait_ge(T.sem[ops[d]["sem"]], full(ops[d]))
        if o["kind"] == "send":
            srcs, dsts, bs = o["fn"]
            trs = []
            for j, e in enumerate(sets(rank, bs)):
                rid, pid, _se = topo.addr(cores[(rank + 1 + bs[j]) % N])
                trs.append(RemoteDMATransfer(dst_ids=[DstId(rid=rid, pnc=pid)], dma_engine_mask=sum(1 << x for x in e),
                                             remote_sem=T.sem[ops[o["arr"][j]]["sem"]],
                                             src=T[srcs[j][0]][srcs[j][1]], dst=T[dsts[j][0]][dsts[j][1]]))
            g.remote_dma_fused(trs, local_sem=T.sem[o["sem"]])
            continue
        ins = o["fn"](g, T)
        if o["kind"] == "dma":
            ins.then_inc(T.sem[o["sem"]], 16)
        elif o.get("sig"):
            ins.then_inc(T.sem[o["sem"]], 1)
    for k in order:
        o = ops[k]
        if o["kind"] != "c" and not o.get("sig"):
            g.wait_ge(T.sem[o["sem"]], full(o))
